import numpy as np, ml_dtypes
CORES = [9,25,41,57]
N = 4
BF = ml_dtypes.bfloat16
def f(rng, *shape):
    return (rng.standard_normal(shape, dtype=np.float32) * np.exp2(rng.integers(-2, 3, shape[:-1] + (1,)))).astype(BF)
def wide(rng, *shape):
    v = f(rng, *shape).astype(np.float32); k = shape[:-2] + (1, shape[-1])
    return (v * np.exp2(rng.integers(-6, 7, k)) * (rng.random(k) > 0.0625)).astype(BF)
def gentries(a):
    return np.ascontiguousarray(a.reshape(8, 16, -1).transpose(0, 2, 1)).reshape(8, -1)
def gtable(e):
    e = np.asarray(e); return np.ascontiguousarray(e.reshape(8, -1, 16).transpose(0, 2, 1)).reshape(128, -1).astype(np.int32)
L, M, S0, R = 2048, 4096, 12, 4
S = 16
def tame(v):
    u = np.minimum(np.maximum(v.astype(np.float32), np.float32(-960)), np.float32(960))
    return np.where(np.abs(u) < np.float32(2.0 ** -16), np.float32(0), u).astype(BF)
def speech(rng):
    q = 2.0 ** (-0.4 * rng.permutation(24)); ks = rng.integers(2, 7, 24); ks[np.argmax(q)] = 5
    W = [rng.permutation(S0)[:k] for k in ks]; w = np.zeros((N, 8, L), np.int64)
    for r in range(N):
        acc = np.add.accumulate(q * 2.0 ** rng.integers(-1, 2, 24))
        for g in range(8):
            i = np.minimum(np.searchsorted(acc, rng.random(L // 2) * acc[-1], side="right"), 23)
            v = np.concatenate([W[j] for j in i])[:L]; w[r, g] = np.where(rng.random(L) < 0.1, rng.integers(0, S0, L), v)
    return w
def lengths(rng):
    le = rng.integers(L // 2, L + 1, (N, 8)); le[rng.integers(0, N), rng.integers(0, 8)] = L
    return le
def plant(rng, w, le):
    r = rng.integers(0, len(w)); w[r, np.argmax(le[r]), :S0] = rng.permutation(S0)
def make(rng, w, le):
    st = np.zeros((N, 8, M), np.int32); ps = np.zeros((N, 8, L), np.int64)
    for r in range(N):
        for g in range(8):
            v = rng.permutation(np.concatenate((np.arange(S0), rng.integers(0, S0, M - S0)))); o = np.argsort(v, kind="stable")
            c = np.bincount(v, minlength=S0); first = np.add.accumulate(c) - c
            st[r, g] = v; ps[r, g] = o[first[w[r, g]] + rng.integers(0, c[w[r, g]])]
    return {"ve": tame(f(rng, N, 128, M)), "st": st, "pos": np.stack([gtable(p) for p in ps]), "le": le.reshape(N, 8, 1).astype(np.int32)}
def setup_inputs(rng):
    w, le = speech(rng), lengths(rng); plant(rng, w, le); return make(rng, w, le)
def setup_inputs_ends(rng):
    w, le = speech(rng), lengths(rng)
    for r in range(N): le[r, rng.permutation(8)[:4]] = np.array([0, 1, 2, L])
    ab = rng.permutation(S0)[:2]; v = w.reshape(N, 8, L // 2, 2); v[rng.random((N, 8, L // 2)) < 0.4] = ab; w = v.reshape(N, 8, L); w[:, :, :2] = ab
    for r in range(N):
        for g in range(8):
            if le[r, g] >= 2: w[r, g, le[r, g] - 2:le[r, g]] = ab
    plant(rng, w, le); d = make(rng, w, le)
    d["pos"][:, 8::16, 2] = 0; d["pos"][:, 9::16, 2] = M - 1; return d
def setup_inputs_ties(rng):
    w, le = speech(rng)[:N // 2], lengths(rng)[:N // 2]; plant(rng, w, le)
    return make(rng, np.concatenate((w, w ^ 1)), np.concatenate((le, le)))
def setup_inputs_few(rng):
    w = speech(rng); le = rng.integers(0, 2, (N, 8)); r, q = rng.permutation(N)[:2]; g = rng.integers(0, 8); le[q] = 0; le[q, (g + 3) % 8] = 1; le[r, g] = S0 + 2
    p = 1 + rng.permutation(S0 - 1); w[r, g, :S0 + 2] = np.concatenate((p[:1], [0], p[1:], [0], p[:1])); return make(rng, w, le)
def setup_inputs_loop(rng):
    W = [rng.permutation(S0)[:k] for k in range(2, 8)]; le = lengths(rng); w = np.zeros((N, 8, L), np.int64)
    for r in range(N):
        for g, i in enumerate(rng.permutation(np.array([0, 1, 2, 2, 3, 4, 5, 5]))): w[r, g] = W[i][(np.arange(L) + rng.integers(0, 8)) % len(W[i])]
    plant(rng, w, le); return make(rng, w, le)
def setup_inputs_spread(rng):
    w = np.stack([np.stack([np.repeat(rng.integers(0, S0, L), rng.integers(1, 40, L))[:L] for g in range(8)]) for r in range(N)])
    le = np.maximum(np.floor(L * rng.random((N, 8)) ** 4).astype(np.int64), 1); le[np.arange(N), rng.integers(0, 8, N)] = L
    plant(rng, w, le); d = make(rng, w, le); d["ve"] = tame(wide(rng, N, 128, M)); return d
def rounds(st, pos, le):
    s, pl = [], []
    for r in range(N):
        P = gentries(pos[r]).astype(np.int64)
        for g in range(8):
            p = P[g, :int(le[r, g, 0])]; pl.append(p); s.append(st[r, g][p].astype(np.int64))
    mg = np.zeros((R, 3), np.float32)
    for t in range(R):
        h = np.zeros(S * S, np.int64)
        for v in s: h += np.bincount((v[:-1] * S + v[1:])[v[:-1] != v[1:]], minlength=S * S)
        k = int(np.argmax(h)); a = k // S; b = k - S * a; mg[t] = a, b, h[k]
        for i in range(len(s)):
            v = s[i]; hit = np.zeros(v.size, bool); hit[:-1] = (v[:-1] == a) & (v[1:] == b)
            keep = np.ones(v.size, bool); keep[1:] = ~hit[:-1]
            s[i] = np.where(hit, S0 + t, v)[keep]; pl[i] = pl[i][keep]
    return s, pl, mg
def check_inputs(d):
    try:
        bad = []
        if not np.isfinite(d["ve"].astype(np.float32)).all(): bad.append("ve is finite")
        if d["st"].min() < 0 or d["st"].max() >= S0: bad.append("st is 0 to S0 - 1")
        if d["pos"].min() < 0 or d["pos"].max() >= M: bad.append("pos is 0 to M - 1")
        if d["le"].min() < 0 or d["le"].max() > L: bad.append("le is 0 to L")
        if not bad and rounds(d["st"], d["pos"], d["le"])[2][:, 2].min() < 1: bad.append("a pair is left in every round")
        return bad
    except Exception:
        return ["shapes"]
def reference(ve, st, pos, le):
    s, pl, mg = rounds(st, pos, le)
    y = np.zeros((N, 128, L), BF); fs = np.full((N, 8, L), -1, np.float32); fl = np.zeros((N, 8, 1), np.float32)
    for r in range(N):
        for g in range(8):
            v, p = s[8 * r + g], pl[8 * r + g]; fl[r, g, 0] = v.size; fs[r, g, :v.size] = v
            y[r, 16 * g:16 * g + 16, :v.size] = ve[r, 16 * g:16 * g + 16][:, p]
    return {"y": y, "fs": fs, "fl": fl, "mg": np.tile(mg, (N, 1, 1))}

@@ -1,0 +1,484 @@
+from concourse.bass import DstId, RemoteDMATransfer
+from concourse.mybir import AluOpType as ALU, AxisListType as AX, ActivationFunctionType as AF
+
+N, L, M, S0, R = 4, 2048, 4096, 12, 4
+H = 16
+W = 128 + 2 * H
+END = 15.0
+M16, M256, M4096 = 1.5 * 2.0 ** 27, 1.5 * 2.0 ** 31, 1.5 * 2.0 ** 35
+PADV = L + 1.0
+D0 = -1920.0
+BIG = 30000.0
+F, B, I, U, HF = "float32", "bfloat16", "int32", "uint16", "float16"
+GCUT = [(0, 32, "V"), (64, 96, "S"), (32, 56, "V"), (96, 120, "S"), (56, 64, "V"), (120, 128, "S")]
+YCUT = [(0, 24, "S"), (92, 116, "V"), (60, 92, "S"), (116, 128, "V"), (24, 60, "S")]
+BANKS = ("pa", "pb", "pc", "pd", "pe", "pg", "ph", "p3")
+SCRATCH = {"lei": ("sbuf", [8, 4], I), "lef": ("sbuf", [8, 4], F), "blkt": ("sbuf", [8, 128], F)}
+for _dt, _shape, _names in [
+        (I, [256], "sti"), (B, [256], "stb ci fi hd"), (B, [1024], "win"), (I, [128], "posi zi zu"), (B, [M + 16], "vew"),
+        (B, [L + 16], "y0"), (B, [L], "yo xs"), (U, [128], "offlo offp offy"), (U, [8], "offs"), (I, [8], "pi"),
+        (B, [128], "w0 w1 ww prow grow rv idb da db d16 sa tri ntri one none hb fsb"), (B, [8, 128], "lw lf"),
+        (F, [128], "wc idf g0 g1 dk nj j16 e2 gw vw emx fso"), (B, [144], "sb"), (F, [W], "jf"), (F, [8], "pf blk b16 kk th acc"),
+        (F, [32], "cc tr"), (B, [4, 128], "rep"), (B, [240], "iw"), (B, [8], "wb"), (B, [16], "i16"), (B, [W], "em0 s ns nx"),
+        (HF, [128], "idh sel lhl lhr zt xc"), (B, [5, 128], "ab"), (B, [4, W], "cd"), (B, [2, 18, 64], "ob"), (B, [2, 2, H], "hh"),
+        (B, [2, S0, 8], "eb"), (B, [96], "c8r bias"), (F, [96], "rst"), (F, [16], "so bt bf ml mr"), (HF, [96], "x0"),
+        (HF, [32], "x1 x2 x3"), (HF, [N, 96], "l0"), (HF, [N, 32], "l1 l2 l3"), (F, [48], "base low rm"), (F, [12], "mgb"),
+        (B, [8, 8, 16], "lt0 lt1 lt2"), (B, [136], "al"), (F, [132], "zero dq e1 gl zl zw"), (HF, [16, 128], "rp"),
+        (HF, [8, 2], "bp bn"), (B, [132], "qb c120"), (F, [8, 16], "hi"), (F, [136], "mm"), (B, [8, 132], "sg"), (F, [4], "flb")]:
+    for _n in _names.split(): SCRATCH[_n] = ("sbuf", [128] + _shape, _dt)
+for _b in BANKS: SCRATCH[_b] = ("psum", [128, 32, 16] if _b == "p3" else [128, 512], F)
+DMAS = ["pos", "st", "le", "ve", "mg", "fl", "fs", "y0", "y1", "y2", "y3", "y4"]
+SEMAPHORES = ["V", "S", "P", "G", "sent"] + ["d" + d for d in DMAS] + ["a%d_%d" % (t, r) for t in range(R) for r in range(N)]
+
+
+def emit(g, T, ops, tail):
+    q = {"V": g.vector, "S": g.scalar, "P": g.tensor, "G": g, "Y": g.sync}
+    writer, readers, deps = {}, {}, []
+    for n, (e, fn, rd, wr, sem) in enumerate(ops):
+        d = set()
+        for k in rd:
+            if k in writer: d.add(writer[k])
+            if k in BANKS: d.update(m for m in readers.get(k, []) if ops[m][0] != e)
+        for k in wr:
+            if k in writer and not (e == "P" and ops[writer[k]][0] == "P"): d.add(writer[k])
+            d.update(m for m in readers.get(k, []) if ops[m][0] != e or ops[m][4])
+        for k in rd: readers.setdefault(k, []).append(n)
+        for k in wr:
+            writer[k] = n
+            readers[k] = []
+        d.discard(n)
+        deps.append(d)
+    needed = set(m for d in deps for m in d)
+    count, token, seen = {}, {}, {}
+    for n, (e, fn, rd, wr, sem) in enumerate(ops):
+        want = {}
+        for m in deps[n]:
+            if m in token: want[token[m][0]] = max(want.get(token[m][0], 0), token[m][1])
+        for name, v in want.items():
+            if seen.get((e, name), 0) < v:
+                q[e].wait_ge(T.sem[name], v)
+                seen[(e, name)] = v
+        ins = fn(q[e])
+        if sem == "-": continue
+        if sem:
+            ins.then_inc(T.sem[sem], 16)
+            token[n] = (sem, 16)
+            count[sem] = 16
+        elif n in needed:
+            count[e] = count.get(e, 0) + 1
+            ins.then_inc(T.sem[e], 1)
+            token[n] = (e, count[e])
+    for name, v in list(count.items()) + tail:
+        if max([w for (e, k), w in seen.items() if k == name] + [0]) < v: g.wait_ge(T.sem[name], v)
+
+
+def rank_program(g, core, T, topo):
+    rank = T.rank_of(core)
+    if rank is None:
+        return
+    ops = []
+
+    def nm(x):
+        return [] if isinstance(x, (int, float)) or x is None else [x[1]]
+
+    def ap(x):
+        return x if isinstance(x, (int, float)) or x is None else x[0]
+
+    def A(name, key=None):
+        return (T[name][:], key or name)
+
+    def C(name, a, b=None, st=1, key=None):
+        return (T[name][:, a:(a + 1 if b is None else b):st], key or name)
+
+    def op(e, fn, rd, wr, sem=None):
+        ops.append((e, fn, rd, wr, sem))
+
+    def ts(o, i, s1, o0, s2=None, o1=None, x=()):
+        if o1 is None: op("V", lambda q: q.tensor_scalar(o[0], i[0], ap(s1), None, o0), nm(i) + nm(s1) + list(x), nm(o))
+        else: op("V", lambda q: q.tensor_scalar(o[0], i[0], ap(s1), ap(s2), o0, o1), nm(i) + nm(s1) + nm(s2) + list(x), nm(o))
+
+    def tt(o, a, b, o0, x=()):
+        op("V", lambda q: q.tensor_tensor(o[0], a[0], b[0], o0), nm(a) + nm(b) + list(x), nm(o))
+
+    def cp(o, i, x=()):
+        op("V", lambda q: q.tensor_copy(o[0], i[0]), nm(i) + list(x), nm(o))
+
+    def ms(o, v):
+        op("V", lambda q: q.memset(o[0], v), [], nm(o))
+
+    def scan(o, a, b, init, o0, o1, x=()):
+        op("V", lambda q: q.tensor_tensor_scan(o[0], a[0], b[0], init, o0, o1), nm(a) + nm(b) + list(x), nm(o))
+
+    def act(o, i, func=AF.Copy, bias=0.0, scale=1.0, x=(), acc=None):
+        kw = {} if acc is None else {"accum_out": acc[0]}
+        op("S", lambda q: q.activation(o[0], i[0], func, bias=ap(bias), scale=ap(scale), **kw),
+           nm(i) + nm(bias) + nm(scale) + list(x), nm(o) + nm(acc))
+
+    def mm(o, l, r, start, stop, x=()):
+        op("P", lambda q: q.matmul(o[0], l[0], r[0], start, stop), nm(l) + nm(r) + list(x), nm(o))
+
+    def iota(o, pat, base=0):
+        op("G", lambda q: q.iota(o[0], pat, base, 0, allow_small_or_imprecise_dtypes=True), [], nm(o))
+
+    def dma(e, o, i, rd, wr, sem):
+        op(e, lambda q: q.dma_start(o, i), rd, wr, "d" + sem)
+
+    def keys(name, n):
+        return ["%s%d" % (name, k) for k in range(n)]
+
+    peers = [(rank + k) % N for k in range(1, N)]
+    emask = topo.mask(core, T.cores[peers[0]])
+    for r in peers: emask &= topo.mask(core, T.cores[r])
+    neng = bin(emask).count("1")
+
+    def send(t):
+        tr = RemoteDMATransfer(dst_ids=[DstId(rid=topo.addr(T.cores[r])[0], pnc=topo.addr(T.cores[r])[1]) for r in peers],
+                               dma_engine_mask=emask, remote_sem=T.sem["a%d_%d" % (t, rank)], srcs=[T["x%d" % t][:]],
+                               dsts=[T["l%d" % t][:, rank, :] for r in peers])
+        op("G", lambda q: q.remote_dma_fused([tr], local_sem=T.sem.sent), ["x%d" % t, "x%dr" % t, "x%dl" % t], [], "-")
+
+    def arrived(t, r):
+        op("P", lambda q: q.wait_ge(T.sem["a%d_%d" % (t, r)], neng), [], [], "-")
+
+    add, sub, mul, mx, mn = ALU.add, ALU.subtract, ALU.mult, ALU.max, ALU.min
+    eq, ge, gt, lt, ne = ALU.is_equal, ALU.is_ge, ALU.is_gt, ALU.is_lt, ALU.not_equal
+    cc = lambda k: C("cc", k, key="cc%d" % k)
+    PG, PI, PSL, PC8, PP_ = C("pf", 0), C("pf", 1), C("pf", 2), C("pf", 3), C("pf", 4)
+    own = slice(H, H + 128)
+    J128, J16, SO = C("jf", 0, 128), C("jf", 0, 16), C("s", H, H + 128)
+
+    dma("S", T.sti[:], T.st[:], [], ["sti"], "st")
+    dma("Y", T.posi[:], T.pos[:], [], ["posi"], "pos")
+    dma("Y", T.lei[:, 0:1], T.le[:], [], ["lei"], "le")
+    dma("Y", T.vew[:, 0:M], T.ve[:], ["posi", "sti"], ["vew"], "ve")
+
+    op("G", lambda q: q.iota(T.pi[:, 4:5], [[0, 1]], 0, 1), [], ["pi4"])
+    iota(A("rv"), [[16, 8], [0, 4], [4, 4]])
+    iota(A("jf"), [[1, W]])
+    iota(A("grow"), [[1, 8], [0, 16]])
+    iota(A("prow"), [[0, 8], [1, 16]])
+    iota(A("c8r"), [[0, 12], [1, 8]])
+    iota(A("j16"), [[16, 128]])
+    iota(A("qb"), [[16, 132]])
+    iota(A("nj"), [[-32, 128]])
+    iota(A("zero"), [[0, 132]])
+    ms(A("iw"), 0.0)
+    ms(A("sb"), 0.0)
+    for k, (o, v) in enumerate([(ALU.arith_shift_right, 4), (ALU.bitwise_and, 15), (ALU.arith_shift_right, 3), (ALU.bitwise_and, 7)]):
+        ts(C("pi", k, key="pi%d" % k), C("pi", 4, key="pi4"), v, o)
+    cp(C("pf", 0, 5), C("pi", 0, 5, key="pi0"), x=keys("pi", 5))
+    ts(cc(1), PI, 1.0, eq, 31.0, mul)
+    ts(cc(2), PI, 2.0, eq, 1023.0, mul)
+    ts(cc(3), PI, 3.0, eq, 32767.0, mul)
+    for u in range(4):
+        ts((T.rep[:, u, :], "rep%d" % u), A("rv"), float(u), add, PP_, eq)
+    ts(cc(4), PI, 4.0, lt, cc(1), add)
+    ts(A("blk"), C("jf", 0, 8), PG, eq)
+    ts(A("i16"), J16, PI, eq)
+    ts(C("iw", 112, 128), J16, PI, eq)
+    ts(cc(5), cc(4), cc(2), add, cc(3), add)
+    ts(cc(6), PI, 128.0, mul, float(-H), add)
+    ts(A("idb"), J128, PP_, eq)
+    ts(A("wb"), A("blk"), cc(5), mul)
+    ts(cc(27), PI, 0.0, eq, END, mul)
+    ts(A("blkt"), (T.grow[0:8, :], "grow"), (T.pf[0:8, 4:5], "pf"), eq)
+
+    cp(A("stb"), A("sti"))
+    rb = ["pa", "pb", "pc", "pg"]
+    for u in range(4): mm(C(rb[u], 0, 256), (T.rep[:, u, :], "rep%d" % u), A("stb"), True, True)
+    for u in range(4): act(C("win", 256 * u, 256 * u + 256, key="win%d" % u), C(rb[u], 0, 256))
+    ts(A("zi"), A("posi"), 1024, ALU.bitwise_and)
+    ts(A("w1"), A("posi"), 2048.0, lt, 2.0 ** -10, mx)
+    ts(A("w0"), A("zi"), 1.0, lt, 2.0 ** -5, mx)
+    ts(A("zu"), A("posi"), 1023, ALU.bitwise_and)
+    tt(A("ww"), A("w0"), A("w1"), mul)
+    cp((T.lef[:, 0:1], "lef"), (T.lei[:, 0:1], "lei"))
+    for gg in range(8): ts((T.lw[:, gg, :], "lw%d" % gg), A("ww"), C("blk", gg), mul)
+    cp(A("offlo"), A("zu"))
+    for u in range(8):
+        mm(C("pd", 0, 128), C("iw", 112 - 16 * u, 240 - 16 * u), (T.lw[:, :, u:128:8], "lw0"), u == 0, u == 7, x=keys("lw", 8))
+    mm(C("pe", 0), A("blkt"), (T.lef[:, 0:1], "lef"), True, True)
+    for k, (a, b, e) in enumerate(GCUT):
+        o = C("xs", 16 * a, 16 * b, key="xs%d" % k)
+        i = (T.win[:, 0:1024].indirect(T.offlo[:, a:b]), "offlo")
+        if e == "V": cp(o, i, x=keys("win", 4))
+        else: act(o, i, x=keys("win", 4))
+        for i in range(a // 8, b // 8):
+            mm(C("ph", i, 128, 16), C("xs", 128 * i, 128 * i + 128, key="xs%d" % k), A("wb"), True, True)
+        if k == 1: act(A("wc"), C("pd", 0, 128))
+    ts(cc(7), C("pe", 0), cc(6), sub)
+    ts(cc(23), C("pe", 0), 1.0, mul)
+    tt(A("zi"), C("ph", 0, 128), A("wc"), mul)
+    ts(A("zu"), A("zi"), 31, ALU.bitwise_and)
+    cp(C("sb", 8, 136), A("zu"))
+    mm(C("pa", H, H + 128), C("sb", 8, 136), A("idb"), True, True)
+    mm(C("pa", 0, H), C("sb", 7, 135), C("idb", 128 - H, 128), True, True)
+    mm(C("pa", H + 128, W), C("sb", 9, 137), C("idb", 0, H), True, True)
+    ts(A("em0"), A("jf"), cc(7), ge, END, mul)
+    ts(A("bias"), A("c8r"), PC8, ne, -BIG, mul)
+    ts(C("em0", 0, H), C("em0", 0, H), cc(27), mx)
+    mm((T.pd[0:96, 0:96], "pd"), (T.idb[0:96, 0:96], "idb"), (T.bias[0:96, :], "bias"), True, False)
+    tt(A("s"), C("pa", 0, W), A("em0"), mx)
+
+    def onehots(n, ns_):
+        for k in range(ns_): act((T.ab[:, k, :], "ab%d" % k), SO, AF.Abs, float(k + 1 - n))
+        for k in range(ns_): act((T.ob[:, :, n - 1 - k, :], "ob%d" % (n - 1 - k)), (T.ab[:, k, :], "ab%d" % k), AF.Relu, 1.0, -1.0)
+        return lambda lo, up: [ts((T.ob[:, :, p, :], "ob%d" % p), SO, float(p), eq) for p in range(lo, min(up, n - ns_))]
+
+    onehots(S0, 2)(0, S0)
+    for h in range(2): cp((T.eb[:, h, :, 0:7], "eb%d" % h), (T.ob[:, h, 0:S0, 8:64:8], "ob0"), x=keys("ob", S0))
+    cp((T.eb[:, 0, :, 7], "eb2"), (T.ob[:, 1, 0:S0, 0], "ob0"))
+    ts((T.eb[:, 1, :, 7], "eb3"), C("jf", 0, S0), C("s", H + 128), eq)
+    for n, (h, k) in enumerate([(h, k) for h in range(2) for k in range(7)] + [(0, 7), (1, 7)]):
+        r = (T.ob[:, h, 0:S0, k + 1:64:8], "ob0") if k < 7 else (T.eb[:, h], "eb0")
+        mm((T.pd[0:96, 0:96], "pd"), (T.ob[:, h, 0:S0, k:64:8], "ob0"), r, False, n == 15, x=keys("ob", S0) + (keys("eb", 4) if k == 7 else []))
+
+    def codes(last):
+        act(C("pb", 0, W), A("s"), AF.Identity, -119.0, 16.0)
+        ts(A("ns"), A("s"), -1.0, mul, -200.0, add)
+        yield
+        scan((T.nx[:, W - 2::-1], "nx"), (T.ns[:, W - 1:0:-1], "ns"), (T.s[:, W - 1:0:-1], "s"), END, mn, mx)
+        scan(C("pc", 1, W), C("ns", 0, W - 1), C("pb", 0, W - 1), 16 * END - 119, mn, mx)
+        tt((T.cd[:, 0, :], "cd0"), C("pb", 0, W), A("nx"), add)
+        tt((T.cd[:, 1, 1:W], "cd1"), C("pc", 1, W), C("s", 1, W), add)
+        yield
+        if last: return
+        scan((T.cd[:, 3, W - 2::-1], "cd3"), (T.ns[:, W - 1:0:-1], "ns"), (T.cd[:, 0, W - 1:0:-1], "cd0"), 136.0, mn, mx)
+        scan((T.cd[:, 2, 1:W], "cd2"), C("ns", 0, W - 1), (T.cd[:, 1, 0:W - 1], "cd1"), 136.0, mn, mx)
+
+    ts(A("rst"), A("c8r"), 0.0, eq, -2 * BIG, mul)
+    ts((T.x0[96:128, :], "x0r"), (T.jf[96:128, 0:96], "jf"), 0.0, mul)
+    ts(cc(0), cc(23), PI, sub)
+    ts(A("g0"), A("j16"), cc(0), ge, float(M), mul)
+    ms(C("vew", M, M + 16, key="vewp"), 0.0)
+    tt(A("g1"), A("g0"), A("posi"), mx)
+    ms(C("nx", W - 1), END)
+    ms((T.cd[:, 1:3, 0:1], "cd1"), 136.0)
+    ms((T.cd[:, 3, W - 1:W], "cd3"), 136.0)
+    cp(A("offp"), A("g1"))
+    cg = codes(False)
+    next(cg)
+    act(C("y0", 0, L), (T.vew[:, 0:M + 16].indirect(T.offp[:, 0:128]), "offp"), x=["vew", "vewp"])
+    ts(A("sel"), A("prow"), PSL, eq, 256.0, mul)
+    ms(A("low"), -1e9)
+    ms(C("base", 16, 48, key="basep"), -1e9)
+    ts(A("idf"), J128, PP_, eq)
+    scan((T.x0[0:96, :], "x0"), (T.rst[0:96, :], "rst"), (T.pd[0:96, 0:96], "pd"), 0.0, add, mx)
+    send(0)
+    ts(cc(8), PI, -16.0, mul, 119.0, add)
+    ts(cc(9), PI, END, eq, -1e8, mul)
+    next(cg)
+    ts(A("bt"), J16, -1.0, mul, cc(8), add)
+    ts(A("bf"), A("i16"), -1e8, mul, cc(9), add)
+    for _ in cg: pass
+    ms(C("bf", 15), -1e8)
+    ms((T.ob[:, :, 12:14, :], "ob12"), 0.0)
+    tt(C("base", 0, 16), A("bt"), A("bf"), add)
+    mm(C("pe", 0, 48), A("idf"), A("base"), True, False, x=["basep"])
+    mm(C("pe", 0, S0), (T.sel[0:96, :], "sel"), (T.x0[0:96, 7:96:8], "x0"), False, False)
+    ts(cc(11), PSL, 15.0, eq)
+    ts(cc(12), PSL, 14.0, eq)
+    ts(cc(13), PSL, 14.0, lt, PSL, mul)
+    ts(cc(15), PSL, 14.0, lt, -1.0, mul)
+    ts(A("db"), A("idb"), -2048.0, mul)
+    ts(cc(14), PSL, 14.0, lt, cc(12), sub)
+    ts(cc(16), PSL, 14.0, lt, cc(11), sub)
+    ts(A("one"), A("grow"), PG, eq, 256.0, mul)
+    ts(A("none"), A("grow"), PG, eq, -256.0, mul)
+    ts(A("w0"), A("prow"), PI, gt)
+    ts(cc(22), PI, 16.0, mul)
+    ts((T.bp[:, :, 0], "bp0"), A("blk"), 1.0, mul)
+    tt(A("tri"), A("w0"), A("one"), mul)
+    ts((T.bp[:, :, 1], "bp1"), A("blk"), -1.0, mul)
+    ts((T.bn[:, :, 0], "bp2"), A("blk"), -1.0, mul)
+    ts((T.bn[:, :, 1], "bp3"), A("blk"), 1.0, mul)
+    ts(A("ntri"), A("tri"), -1.0, mul)
+    ts(A("d16"), A("idb"), cc(22), mul)
+    ts(A("idh"), A("idb"), 1.0 / 16, mul)
+    ts(A("b16"), A("blk"), 16.0, mul)
+    ms(A("c120"), 7.5)
+    ms(A("hb"), -127.5)
+    ms(C("y0", L, L + 16, key="y0p"), 0.0)
+    ms(C("dq", 0, key="dq0"), D0)
+    ms(C("al", 128, key="alp"), 1.0)
+    ms(C("zw", 0, key="zw0"), -1e9)
+    ms(C("mm", 129, 136, key="mmp"), PADV)
+
+    KN, CN = C("kk", 0, key="kn"), C("kk", 1, key="cn")
+
+    def winner(t):
+        for r in reversed(peers):
+            arrived(t, r)
+            fin = r == peers[0]
+            if t == 0:
+                mm(C("pe", 0, S0), (T.sel[0:96, :], "sel"), (T.l0[0:96, r, 7:96:8], "l0"), False, fin)
+            else:
+                mm(C("pe", 0, 16), A("lhr"), (T["l%d" % t][:, r, 0:16], "l"), False, False)
+                mm(C("pe", 0, 16), A("lhl"), (T["l%d" % t][:, r, 16:32], "l"), False, fin)
+        scan(A("rm"), C("pe", 0, 48), A("low"), -1e9, mx, mx)
+        op("V", lambda q: q.transpose(T.tr[:], T.rm[:, 16:48]), ["rm"], ["tr"])
+        op("V", lambda q: q.tensor_reduce(KN[0], T.tr[:], AX.X, mx, negate=True), ["tr"], ["kn"])
+        ts(CN, KN, M256, add, M256, sub)
+
+    def decode(t):
+        a, b = C("mgb", 3 * t, key="a%d" % t), C("mgb", 3 * t + 1, key="b%d" % t)
+        k2, k3 = C("kk", 2, key="k2"), C("kk", 3, key="k3")
+        ts(k2, KN, CN, sub, 111.5, add)
+        ts(C("mgb", 3 * t + 2, key="n%d" % t), CN, -1.0 / 256, mul)
+        ts(k3, k2, M16, add, M16, sub)
+        yield
+        ts(a, k3, 1.0 / 16, mul)
+        ts(b, k2, k3, sub, 7.5, add)
+
+    def turn(h, src, bank, eng):
+        for gg in range(8):
+            o = (T["lt%d" % h][:, :, gg, :], "lt%d_%d" % (h, gg))
+            if eng[gg] == "S": act(o, src, AF.Copy, 0.0, C("blk", gg))
+            else: ts(o, src, C("blk", gg), mul)
+        return lambda: [mm(C(bank, u, 128, 8), (T["lt%d" % h][:, u], "lt%d_0" % h), A("i16"), True, True,
+                           x=keys("lt%d_" % h, 8)) for u in range(8)]
+
+    for t in range(R - 1):
+        c = S0 + t
+        X = "x%d" % (t + 1)
+        a, b = C("mgb", 3 * t, key="a%d" % t), C("mgb", 3 * t + 1, key="b%d" % t)
+        mm(C("pd", 0, 16), A("idb"), C("bias", 0, 16), True, False)
+        winner(t)
+        dg = decode(t)
+        for h in range(2):
+            ts((T.ob[:, h, 14:18, :], "fl%d" % h), (T.cd[:, :, H + 64 * h:H + 64 * h + 64], "cd0"), CN, add, KN, eq, x=keys("cd", 4))
+            if h == 0: next(dg)
+            for k in range(8):
+                mm(C("pd", 0, 16), (T.ob[:, h, 0:16, k:64:8], "fl%d" % h), (T.ob[:, h, 16:18, k:64:8], "fl%d" % h), False,
+                   h == 1 and k == 7, x=keys("ob", 14))
+        for _ in dg: pass
+        for h in range(2): ts((T.hh[:, h], "hh%d" % h), (T.cd[:, 0:2, (H + 128) * h:(H + 128) * h + H], "cd0"), CN, add, KN, eq)
+        act(cc(17), a, AF.Identity, float(c), -1.0)
+        act(A("da"), A("idb"), AF.Copy, 0.0, cc(17))
+        for lo, n, hit, drop, key in [(H, 64, T.ob[:, 0, 14, :], T.ob[:, 0, 15, :], "fl0"), (H + 64, 64, T.ob[:, 1, 14, :], T.ob[:, 1, 15, :], "fl1"),
+                                      (0, H, T.hh[:, 0, 0, :], T.hh[:, 0, 1, :], "hh0"), (H + 128, H, T.hh[:, 1, 0, :], T.hh[:, 1, 1, :], "hh1")]:
+            mm(C("pa", lo, lo + n), A("db"), (drop, key), True, False)
+            mm(C("pa", lo, lo + n), A("da"), (hit, key), False, True)
+        ts(cc(18), a, cc(12), mul, cc(13), add)
+        ts(A("ml"), J16, a, eq, cc(15), mul)
+        ts(cc(19), b, cc(11), mul, cc(13), add)
+        ts(A("mr"), J16, cc(18), eq, cc(14), mul)
+        cp(C("ml", c), cc(16))
+        ts(A("bf"), C("pe", 0, 16), KN, add, 0.0, ne)
+        ts(A("lhr"), A("prow"), b, eq, -256.0, mul)
+        ts(A("lhl"), A("prow"), cc(19), eq, 256.0, mul)
+        scan(A("so"), C("rst", 0, 16), C("pd", 0, 16), 0.0, add, mx)
+        ts(C(X, 0, 16, key=X + "r"), A("mr"), C("so", 7), mul)
+        ts(C(X, 16, 32, key=X + "l"), A("ml"), C("so", 15), mul)
+        send(t + 1)
+        tt(C("base", 0, 16), C("pe", 0, 16), A("bf"), mul)
+        ms(C("lhr", c, 128, 16), 256.0)
+        tt(A("s"), C("pa", 0, W), A("s"), add)
+        last = t == R - 2
+        cg = codes(last)
+        next(cg)
+        mm(C("pe", 0, 48), A("idf"), A("base"), True, False, x=["basep"])
+        mm(C("pe", 0, 16), A("lhr"), C(X, 0, 16, key=X + "r"), False, False)
+        mm(C("pe", 0, 16), A("lhl"), C(X, 16, 32, key=X + "l"), False, False)
+        if not last:
+            oh = onehots(c + 1, 5)
+            next(cg)
+            oh(0, 2)
+            for _ in cg: pass
+            oh(2, 16)
+        if t == 0:
+            ts(cc(20), PI, 256.0 * 4096, mul, (128 + D0) * 4096, add)
+            ts(cc(21), PI, -256.0 * 4096, mul, -(4096 + 128 + D0) * 4096, add)
+            ts(cc(24), PI, 4096.0, mul, 256.0 * 15 + 128 + D0, add)
+            ts(cc(25), cc(23), -D0 / 256 - L, add)
+        if t == 1:
+            ts(A("th"), C("jf", 0, 8), 65536.0, mul, cc(24), add)
+            ts(cc(26), cc(6), -32.0, mul, -32.0 * H - 1, add)
+
+    turn(2, SO, "pg", "SSSSSSSS")()
+    next(cg)
+    turn(0, (T.cd[:, 0, own], "cd0"), "ph", "VVVVVVVV")()
+    m1 = turn(1, (T.cd[:, 1, own], "cd1"), "pd", "VVVVVVSS")
+    act(C("ci", 0, 128, key="ci0"), C("ph", 0, 128))
+    ts(C("al", 0, 128), C("pg", 0, 128), 0.0, ge)
+    ts(A("sa"), C("pg", 0, 128), 0.0, mx, -128.0, add)
+    ts(C("pa", 0, 128), C("pg", 0, 128), -1.0, mul, END, add)
+    ts(C("pa", 128, 256), C("pg", 0, 128), cc(22), add, -1.0, mul)
+
+    winner(R - 1)
+    m1()
+    act(C("ci", 128, 256), C("pd", 0, 128))
+    mm(C("pb", 0, 129), A("one"), C("al", 0, 129), True, False, x=["alp"])
+    mm(C("pc", 0, 128), A("tri"), C("al", 0, 128), True, False)
+    mm(C("pc", 0, 128), A("d16"), C("al", 0, 128), False, False)
+    mm(C("pc", 0, 128), A("idb"), A("sa"), False, False)
+    ts(A("fi"), A("ci"), CN, add, KN, eq, x=["ci0"])
+    DR = C("fi", 128, 256)
+    mm(C("pb", 0, 128), A("none"), DR, False, True)
+    mm(C("pc", 0, 128), A("ntri"), DR, False, False)
+    tt(A("hd"), C("pa", 0, 256), A("fi"), mul)
+    mm(C("pc", 0, 128), A("idb"), C("hd", 0, 128), False, False)
+    mm(C("pc", 0, 128), A("idb"), C("hd", 128, 256), False, True)
+    P3 = (T.p3[:, 0:8, :], "p3")
+    mm(P3, A("idb"), A("hb"), True, False)
+    mm(C("pg", 0, 129), A("idb"), C("qb", 0, 129), True, False)
+    mm(C("pg", 0, 129), A("idb"), C("c120", 0, 129), False, False)
+    scan(C("dq", 1, 130), C("pb", 0, 129), C("zero", 0, 129), D0, add, add)
+    for c in range(8):
+        act((T.sg[:, c, 0:129], "sg%d" % c), C("dq", 1, 130), AF.Sign, C("th", c), -1.0, acc=C("acc", c, key="acc%d" % c))
+    ts(C("pd", 0, 129), C("dq", 0, 129), M4096, add, M4096, sub, x=["dq0"])
+    tt(C("e1", 0, 129), C("pd", 0, 129), C("dq", 0, 129), sub)
+    tt(C("ph", 0, 128), C("pc", 0, 128), C("dq", 0, 128), add, x=["dq0"])
+    ts(A("dk"), C("ph", 0, 128), M4096, add, M4096, sub)
+    tt(A("xc"), C("ph", 0, 128), A("dk"), sub)
+    for n, k in enumerate([1, 16, 2, 17, 3, 18, 4, 19, 5, 20, 6, 21, 7, 22, 8, 23]):
+        sg = k if k <= 8 else k - 8
+        o = (T.rp[:, n, :], "rp%d" % n)
+        ts(o, A("xc"), 256.0 * sg - 2048, sub, 0.0, mn if k <= 8 else mx)
+        if k == 8: dst, r = T.p3[:, 0:8, 7], T.bp[:, :, 0]
+        elif k == 16: dst, r = T.p3[:, 0:8, 8], T.bp[:, :, 0]
+        else: dst, r = T.p3[:, 0:8, sg - 1:sg + 1], (T.bp[:] if k < 8 else T.bn[:])
+        mm((dst, "p3"), o, (r, "bp0"), False, n == 15, x=keys("bp", 4))
+    tt(A("e2"), C("pd", 0, 128), C("dq", 1, 129), sub)
+    ts(A("hi"), P3, M256, add, M256, sub)
+    tt(A("zt"), P3, A("hi"), sub)
+    mm(C("pg", 0, 128), A("zt"), A("idh"), False, True)
+    act(C("gl", 0, 129), C("e1", 0, 129), AF.Identity, cc(20), 4096.0)
+    act(A("gw"), A("e2"), AF.Identity, cc(21), -4096.0)
+    ts(A("offs"), A("acc", "acc0"), 129.0, add, 0.5, mul, x=keys("acc", 8))
+    dg = decode(R - 1)
+    next(dg)
+    tt(C("zl", 0, 129), C("pg", 0, 129), C("gl", 0, 129), mn)
+    tt(C("zw", 1, 129), C("pg", 0, 128), A("gw"), mn)
+    scan(C("mm", 0, 129), C("zl", 0, 129), C("zw", 0, 129), -1e9, mx, mx, x=["zw0"])
+    cp(A("vw"), (T.mm[:, 0:136].indirect(T.offs[:, 0:8]), "mm"), x=["offs", "mmp"])
+    ts(A("offy"), A("vw"), M16 / 16, add, M16 / 16, sub)
+
+    def ygather(k):
+        a, b, e = YCUT[k]
+        o = C("yo", 16 * a, 16 * b, key="yo%d" % k)
+        i = (T.y0[:, 0:L + 16].indirect(T.offy[:, a:b]), "offy")
+        if e == "V": cp(o, i, x=["y0", "y0p"])
+        else: act(o, i, x=["y0", "y0p"])
+        return lambda: dma("S" if k == 2 else "Y", T.y[:, 16 * a:16 * b], o[0], ["yo%d" % k], [], "y%d" % k)
+    ygather(0)()
+    d4 = ygather(4)
+    ygather(2)()
+    ts(A("g0"), A("vw"), M16 / 16, add, M16 / 16, sub)
+    ts(C("flb", 0), C("dq", 128), 1.0 / 256, mul, cc(25), add)
+    tt(A("fsb"), A("vw"), A("g0"), sub)
+    ts(C("flb", 1, key="fl32"), C("flb", 0), 32.0, mul, cc(26), add)
+    for _ in dg: pass
+    dma("Y", T.fl[:], T.flb[0:128:16, 0:1], ["flb"], [], "fl")
+    dma("Y", T.mg[:], T.mgb[0:1, :], [k + str(t) for k in "abn" for t in range(R)], [], "mg")
+    d4()
+    for gg in range(8): ts((T.lf[:, gg, :], "lf%d" % gg), A("fsb"), 7.5 / 16, add, C("b16", gg), mul)
+    for u in range(8):
+        mm(C("pa", 16 * u, 16 * u + 16), (T.lf[:, :, u:128:8], "lf0"), A("i16"), True, True, x=keys("lf", 8))
+    ts(A("emx"), A("nj"), C("flb", 1, key="fl32"), add, -1.0, mx)
+    d1 = ygather(1)
+    tt(A("fso"), C("pa", 0, 128), A("emx"), mn)
+    d1()
+    dma("Y", T.fs[:], T.fso[:], ["fso"], [], "fs")
+    ygather(3)()
+    emit(g, T, ops, [("sent", R * neng)])

@@ -1,8 +1,10 @@
+import math
+import numpy as np
 from concourse.bass import DstId, RemoteDMATransfer
 from concourse.mybir import AluOpType as ALU, AxisListType as AX, ActivationFunctionType as AF
 
 N, L, M, S0, R = 4, 2048, 4096, 12, 4
-H = 16
+H = 12
 W = 128 + 2 * H
 END = 15.0
 M16, M256, M4096 = 1.5 * 2.0 ** 27, 1.5 * 2.0 ** 31, 1.5 * 2.0 ** 35
@@ -10,54 +12,88 @@ PADV = L + 1.0
 D0 = -1920.0
 BIG = 30000.0
 F, B, I, U, HF = "float32", "bfloat16", "int32", "uint16", "float16"
-GCUT = [(0, 32, "V"), (64, 96, "S"), (32, 56, "V"), (96, 120, "S"), (56, 64, "V"), (120, 128, "S")]
-YCUT = [(0, 24, "S"), (92, 116, "V"), (60, 92, "S"), (116, 128, "V"), (24, 60, "S")]
+GCUT = [("S", 11, 16), ("V", 0, 4), ("S", 8, 11), ("V", 4, 6), ("V", 6, 7), ("S", 7, 8)]
+YCUT = [("V", 0, 24), ("S", 48, 80), ("V", 24, 48), ("S", 80, 110), ("S", 110, 128)]
+DROP = [14, 15, 15]
 BANKS = ("pa", "pb", "pc", "pd", "pe", "pg", "ph", "p3")
 SCRATCH = {"lei": ("sbuf", [8, 4], I), "lef": ("sbuf", [8, 4], F), "blkt": ("sbuf", [8, 128], F)}
 for _dt, _shape, _names in [
-        (I, [256], "sti"), (B, [256], "stb ci fi hd"), (B, [1024], "win"), (I, [128], "posi zi zu"), (B, [M + 16], "vew"),
-        (B, [L + 16], "y0"), (B, [L], "yo xs"), (U, [128], "offlo offp offy"), (U, [8], "offs"), (I, [8], "pi"),
-        (B, [128], "w0 w1 ww prow grow rv idb da db d16 sa tri ntri one none hb fsb"), (B, [8, 128], "lw lf"),
-        (F, [128], "wc idf g0 g1 dk nj j16 e2 gw vw emx fso"), (B, [144], "sb"), (F, [W], "jf"), (F, [8], "pf blk b16 kk th acc"),
-        (F, [32], "cc tr"), (B, [4, 128], "rep"), (B, [240], "iw"), (B, [8], "wb"), (B, [16], "i16"), (B, [W], "em0 s ns nx"),
-        (HF, [128], "idh sel lhl lhr zt xc"), (B, [5, 128], "ab"), (B, [4, W], "cd"), (B, [2, 18, 64], "ob"), (B, [2, 2, H], "hh"),
-        (B, [2, S0, 8], "eb"), (B, [96], "c8r bias"), (F, [96], "rst"), (F, [16], "so bt bf ml mr"), (HF, [96], "x0"),
-        (HF, [32], "x1 x2 x3"), (HF, [N, 96], "l0"), (HF, [N, 32], "l1 l2 l3"), (F, [48], "base low rm"), (F, [12], "mgb"),
-        (B, [8, 8, 16], "lt0 lt1 lt2"), (B, [136], "al"), (F, [132], "zero dq e1 gl zl zw"), (HF, [16, 128], "rp"),
-        (HF, [8, 2], "bp bn"), (B, [132], "qb c120"), (F, [8, 16], "hi"), (F, [136], "mm"), (B, [8, 132], "sg"), (F, [4], "flb")]:
+        (I, [256], "sti"), (B, [256], "stb ci fi hd"), (B, [1024], "win"), (I, [128], "posi zh zl"), (I, [W], "zi zu"),
+        (B, [M + 16], "vew"), (B, [L + 16], "y0"), (B, [L], "yo"), (B, [L + 32], "xs"), (U, [128], "offlo offp offy"),
+        (U, [8], "offs"), (I, [16], "pi"), (B, [160], "idw e0 e1 wb"), (B, [272], "lw lf"),
+        (B, [128], "grow da db d16 sa tri ntri one none hb cm fsb lhb gw nid"), (B, [8, 16], "prow"), (B, [3, 128], "lha tr3"),
+        (B, [3, 8, 16], "lhr"), (F, [128], "idf g0 g1 dk nj j16 q2 emx fso"), (F, [W], "jfs"), (F, [160], "jf"),
+        (F, [16], "pf so bt bf j7 srb"), (F, [3, 16], "sr"), (F, [8], "blk kk th acc"), (F, [40], "cc"), (F, [32], "tr"),
+        (B, [2], "wcol"), (B, [16], "i16"), (B, [W], "ns nx wc"), (HF, [128], "idh zt xc"), (B, [S0], "eb"), (B, [6, W], "cd"),
+        (B, [2, 18, 64], "ob"), (B, [2, W], "hw"), (B, [180], "c8r bias"), (F, [180], "rst so0"), (HF, [S0], "x0"),
+        (HF, [32], "x1 x2 x3"), (HF, [N, S0], "l0"), (HF, [N, 32], "l1 l2 l3"), (F, [48], "base low rm ml"), (F, [R, 3], "mgb"),
+        (F, [R, 2], "ab7"), (F, [R], "cn flb"), (B, [136], "al"), (F, [132], "dq q1"), (HF, [16, 128], "rp"), (HF, [8, 2], "bp bn"),
+        (B, [132], "qb gl"), (B, [260], "c120 zero"), (F, [8, 16], "hi"), (F, [264], "mm"), (B, [8, 132], "sg")]:
     for _n in _names.split(): SCRATCH[_n] = ("sbuf", [128] + _shape, _dt)
 for _b in BANKS: SCRATCH[_b] = ("psum", [128, 32, 16] if _b == "p3" else [128, 512], F)
-DMAS = ["pos", "st", "le", "ve", "mg", "fl", "fs", "y0", "y1", "y2", "y3", "y4"]
+DMAS = ["pos", "st", "le", "ve", "mg", "fl", "fs"] + ["y%d" % k for k in range(len(YCUT))]
 SEMAPHORES = ["V", "S", "P", "G", "sent"] + ["d" + d for d in DMAS] + ["a%d_%d" % (t, r) for t in range(R) for r in range(N)]
+CYC, PECYC, WAKE, TRIP, LOCAL, RATE = 0.83e-3, 0.42e-3, 0.2, 1.6, 1.0, 200e3
+
+
+def arrange(ops):
+    seen, waits, before = {}, [], []
+    for n, (e, fn, rd, wr, sem, cost, lat) in enumerate(ops):
+        w, o = set(), set()
+        for acc, write in [(a, False) for a in rd] + [(a, True) for a in wr]:
+            for m, mask, wrote in seen.get(acc[0], []):
+                other = ops[m][0] != e
+                if acc[0] in BANKS and e == "P" and not other: o.add(m)
+                elif (acc[0] in BANKS and other) or (mask & acc[1] and (write or wrote)): (o if ops[m][4] == "-" and not other else w).add(m)
+        for acc, write in [(a, False) for a in rd] + [(a, True) for a in wr]: seen.setdefault(acc[0], []).append((n, acc[1], write))
+        waits.append(w)
+        before.append(o)
+    gap = lambda m, n: ops[m][6] + WAKE if m in waits[n] else 0.0
+    nxt = [[] for _ in ops]
+    for n in range(len(ops)):
+        for m in waits[n] | before[n]: nxt[m].append(n)
+    chain = [0.0] * len(ops)
+    for m in reversed(range(len(ops))): chain[m] = ops[m][5] + max([gap(m, n) + chain[n] for n in nxt[m]] + [ops[m][6]])
+    miss = [len(waits[n] | before[n]) for n in range(len(ops))]
+    ready, free, order = dict((n, 0.0) for n in range(len(ops)) if not miss[n]), {}, []
+    at = [0.0] * len(ops)
+    while ready:
+        t, e = min((max(r, free.get(ops[n][0], 0.0)), ops[n][0]) for n, r in ready.items())
+        mine = [n for n in ready if ops[n][0] == e]
+        n = max((n for n in mine if ready[n] <= t), key=lambda n: (chain[n], -n))
+        soon = [m for m in mine if chain[m] > chain[n] and ready[m] < t + ops[n][5] - 0.03]
+        if soon: n = min(soon, key=lambda m: (ready[m], -chain[m]))
+        free[e] = max(ready.pop(n), t) + ops[n][5]
+        order.append(n)
+        for k in nxt[n]:
+            at[k] = max(at[k], free[e] + gap(n, k))
+            miss[k] -= 1
+            if not miss[k]: ready[k] = at[k]
+    return order, waits
 
 
 def emit(g, T, ops, tail):
     q = {"V": g.vector, "S": g.scalar, "P": g.tensor, "G": g, "Y": g.sync}
-    writer, readers, deps = {}, {}, []
-    for n, (e, fn, rd, wr, sem) in enumerate(ops):
-        d = set()
-        for k in rd:
-            if k in writer: d.add(writer[k])
-            if k in BANKS: d.update(m for m in readers.get(k, []) if ops[m][0] != e)
-        for k in wr:
-            if k in writer and not (e == "P" and ops[writer[k]][0] == "P"): d.add(writer[k])
-            d.update(m for m in readers.get(k, []) if ops[m][0] != e or ops[m][4])
-        for k in rd: readers.setdefault(k, []).append(n)
-        for k in wr:
-            writer[k] = n
-            readers[k] = []
-        d.discard(n)
-        deps.append(d)
-    needed = set(m for d in deps for m in d)
-    count, token, seen = {}, {}, {}
-    for n, (e, fn, rd, wr, sem) in enumerate(ops):
-        want = {}
-        for m in deps[n]:
-            if m in token: want[token[m][0]] = max(want.get(token[m][0], 0), token[m][1])
-        for name, v in want.items():
-            if seen.get((e, name), 0) < v:
-                q[e].wait_ge(T.sem[name], v)
-                seen[(e, name)] = v
+    order, deps = arrange(ops)
+    place = dict((n, k) for k, n in enumerate(order))
+    done, upto, after, waits = dict.fromkeys(q, 0), dict.fromkeys(q, 0), {}, {}
+    for n in order:
+        e, sem = ops[n][0], ops[n][4]
+        waits[n] = []
+        for m in sorted(deps[n], key=place.get, reverse=True):
+            if m in after and not done[e] >> m & 1:
+                waits[n].append(m)
+                done[e] |= after[m]
+        if sem == "-": continue
+        if not sem: upto[e] |= 1 << n
+        after[n] = done[e] | (1 << n if sem else upto[e])
+    needed = set(m for w in waits.values() for m in w)
+    count, token, top = {}, {}, {}
+    for n in order:
+        e, fn, sem = ops[n][0], ops[n][1], ops[n][4]
+        for m in waits[n]:
+            q[e].wait_ge(T.sem[token[m][0]], token[m][1])
+            top[token[m][0]] = max(top.get(token[m][0], 0), token[m][1])
         ins = fn(q[e])
         if sem == "-": continue
         if sem:
@@ -69,7 +105,7 @@ def emit(g, T, ops, tail):
             ins.then_inc(T.sem[e], 1)
             token[n] = (e, count[e])
     for name, v in list(count.items()) + tail:
-        if max([w for (e, k), w in seen.items() if k == name] + [0]) < v: g.wait_ge(T.sem[name], v)
+        if top.get(name, 0) < v: g.wait_ge(T.sem[name], v)
 
 
 def rank_program(g, core, T, topo):
@@ -77,54 +113,72 @@ def rank_program(g, core, T, topo):
     if rank is None:
         return
     ops = []
+    s_ = np.s_
 
-    def nm(x):
-        return [] if isinstance(x, (int, float)) or x is None else [x[1]]
+    def X(name, ix=s_[:]):
+        where, shape, dt = SCRATCH[name]
+        cols = np.arange(int(np.prod(shape[1:]))).reshape([1] + shape[1:])[(slice(None),) + (ix[1:] if isinstance(ix, tuple) else ())].reshape(-1)
+        bits = np.zeros(int(np.prod(shape[1:])), np.uint8)
+        bits[cols] = 1
+        mask = int.from_bytes(np.packbits(bits, bitorder="little").tobytes(), "little")
+        return (T[name][ix], [(name, mask)], len(cols), 4 if dt in (F, I) else 2, False)
+
+    def C(name, a, b=None, st=1):
+        return X(name, s_[:, a:(a + 1 if b is None else b):st])
+
+    def pick(win, off):
+        return (win[0].indirect(off[0]), win[1] + off[1], 16 * off[2], win[3], True)
+
+    def nm(*xs):
+        return [a for x in xs if isinstance(x, tuple) for a in x[1]]
 
     def ap(x):
-        return x if isinstance(x, (int, float)) or x is None else x[0]
+        return x[0] if isinstance(x, tuple) else x
 
-    def A(name, key=None):
-        return (T[name][:], key or name)
+    def op(e, fn, rd, wr, cost, sem=None, lat=0.0):
+        ops.append((e, fn, rd, wr, sem, cost, lat))
 
-    def C(name, a, b=None, st=1, key=None):
-        return (T[name][:, a:(a + 1 if b is None else b):st], key or name)
+    def vec(fn, o, ins, more=(), two=False):
+        rate = 0.5 if all(x[3] == 2 for x in [o] + ins) else 1.0
+        if two: rate = 1.0 if any(x[1][0][0] in BANKS for x in ins) else 2.0
+        op("V", fn, nm(*ins) + nm(*more), nm(o), 0.05 + 1.56 * o[2] * CYC if ins and ins[0][4] else max(64, rate * (ins or [o])[0][2]) * CYC)
 
-    def op(e, fn, rd, wr, sem=None):
-        ops.append((e, fn, rd, wr, sem))
+    def ts(o, i, s1, o0, s2=None, o1=None):
+        if o1 is None: vec(lambda q: q.tensor_scalar(o[0], i[0], ap(s1), None, o0), o, [i], [s1])
+        else: vec(lambda q: q.tensor_scalar(o[0], i[0], ap(s1), ap(s2), o0, o1), o, [i], [s1, s2])
 
-    def ts(o, i, s1, o0, s2=None, o1=None, x=()):
-        if o1 is None: op("V", lambda q: q.tensor_scalar(o[0], i[0], ap(s1), None, o0), nm(i) + nm(s1) + list(x), nm(o))
-        else: op("V", lambda q: q.tensor_scalar(o[0], i[0], ap(s1), ap(s2), o0, o1), nm(i) + nm(s1) + nm(s2) + list(x), nm(o))
+    def tt(o, a, b, o0):
+        vec(lambda q: q.tensor_tensor(o[0], a[0], b[0], o0), o, [a, b], two=True)
 
-    def tt(o, a, b, o0, x=()):
-        op("V", lambda q: q.tensor_tensor(o[0], a[0], b[0], o0), nm(a) + nm(b) + list(x), nm(o))
-
-    def cp(o, i, x=()):
-        op("V", lambda q: q.tensor_copy(o[0], i[0]), nm(i) + list(x), nm(o))
+    def cp(o, i):
+        vec(lambda q: q.tensor_copy(o[0], i[0]), o, [i])
 
     def ms(o, v):
-        op("V", lambda q: q.memset(o[0], v), [], nm(o))
+        vec(lambda q: q.memset(o[0], v), o, [])
 
-    def scan(o, a, b, init, o0, o1, x=()):
-        op("V", lambda q: q.tensor_tensor_scan(o[0], a[0], b[0], init, o0, o1), nm(a) + nm(b) + list(x), nm(o))
+    def scan(o, a, b, init, o0, o1):
+        vec(lambda q: q.tensor_tensor_scan(o[0], a[0], b[0], init, o0, o1), o, [a, b])
 
-    def act(o, i, func=AF.Copy, bias=0.0, scale=1.0, x=(), acc=None):
+    def vtr(o, i):
+        vec(lambda q: q.transpose(o[0], i[0]), o, [i])
+
+    def act(o, i, func=AF.Copy, bias=0.0, scale=1.0, acc=None, more=0.0):
         kw = {} if acc is None else {"accum_out": acc[0]}
-        op("S", lambda q: q.activation(o[0], i[0], func, bias=ap(bias), scale=ap(scale), **kw),
-           nm(i) + nm(bias) + nm(scale) + list(x), nm(o) + nm(acc))
+        op("S", lambda q: q.activation(o[0], i[0], func, bias=ap(bias), scale=ap(scale), **kw), nm(i, bias, scale), nm(o, acc),
+           more + (0.065 + 1.56 * o[2] * CYC if i[4] else max(64, i[2]) * CYC))
 
-    def mm(o, l, r, start, stop, x=()):
-        op("P", lambda q: q.matmul(o[0], l[0], r[0], start, stop), nm(l) + nm(r) + list(x), nm(o))
+    def mm(o, l, r, start, stop):
+        op("P", lambda q: q.matmul(o[0], l[0], r[0], start, stop), nm(l, r), nm(o), max(min(64, l[2]), r[2]) * PECYC * (l[3] // 2) ** 2)
 
-    def iota(o, pat, base=0):
-        op("G", lambda q: q.iota(o[0], pat, base, 0, allow_small_or_imprecise_dtypes=True), [], nm(o))
+    def iota(o, pat, base=0, step=0):
+        kw = {} if o[1][0][0] == "pi" else {"allow_small_or_imprecise_dtypes": True}
+        op("G", lambda q: q.iota(o[0], pat, base, step, **kw), [], nm(o), 0.13 + 2 * o[2] * CYC)
 
-    def dma(e, o, i, rd, wr, sem):
-        op(e, lambda q: q.dma_start(o, i), rd, wr, "d" + sem)
+    def load(e, o, i, sem):
+        op(e, lambda q: q.dma_start(o[0], i), [], nm(o) + [("queue" + e, 1)], 0.05, "d" + sem, LOCAL + 128 * o[2] * o[3] / RATE)
 
-    def keys(name, n):
-        return ["%s%d" % (name, k) for k in range(n)]
+    def store(e, o, i, sem):
+        op(e, lambda q: q.dma_start(o, i[0]), nm(i), [], 0.05, "d" + sem, LOCAL + 128 * i[2] * i[3] / RATE)
 
     peers = [(rank + k) % N for k in range(1, N)]
     emask = topo.mask(core, T.cores[peers[0]])
@@ -135,350 +189,305 @@ def rank_program(g, core, T, topo):
         tr = RemoteDMATransfer(dst_ids=[DstId(rid=topo.addr(T.cores[r])[0], pnc=topo.addr(T.cores[r])[1]) for r in peers],
                                dma_engine_mask=emask, remote_sem=T.sem["a%d_%d" % (t, rank)], srcs=[T["x%d" % t][:]],
                                dsts=[T["l%d" % t][:, rank, :] for r in peers])
-        op("G", lambda q: q.remote_dma_fused([tr], local_sem=T.sem.sent), ["x%d" % t, "x%dr" % t, "x%dl" % t], [], "-")
+        op("G", lambda q: q.remote_dma_fused([tr], local_sem=T.sem.sent), nm(X("x%d" % t)), [("trip%d" % t, 1)], 0.3, "-", TRIP)
 
     def arrived(t, r):
-        op("P", lambda q: q.wait_ge(T.sem["a%d_%d" % (t, r)], neng), [], [], "-")
+        op("P", lambda q: q.wait_ge(T.sem["a%d_%d" % (t, r)], neng), [("trip%d" % t, 1)], nm(X("l%d" % t, s_[:, r])), 0.0, "-")
 
     add, sub, mul, mx, mn = ALU.add, ALU.subtract, ALU.mult, ALU.max, ALU.min
     eq, ge, gt, lt, ne = ALU.is_equal, ALU.is_ge, ALU.is_gt, ALU.is_lt, ALU.not_equal
-    cc = lambda k: C("cc", k, key="cc%d" % k)
-    PG, PI, PSL, PC8, PP_ = C("pf", 0), C("pf", 1), C("pf", 2), C("pf", 3), C("pf", 4)
-    own = slice(H, H + 128)
-    J128, J16, SO = C("jf", 0, 128), C("jf", 0, 16), C("s", H, H + 128)
+    band, shr = ALU.bitwise_and, ALU.arith_shift_right
+    cc = lambda k: C("cc", k)
+    PP, P16, PI, P3, P12, PK, PO, PG, PSL, PC8 = [C("pf", k) for k in range(10)]
+    J128, J16 = C("jf", 0, 128), C("jf", 0, 16)
+    IDB, PROW, J7 = C("idw", 16, 144), X("prow"), X("prow", s_[:, 0, :])
+    cd = lambda k, a=0, b=W: X("cd", s_[:, k, a:b])
+    own = lambda k: cd(k, H, H + 128)
 
-    dma("S", T.sti[:], T.st[:], [], ["sti"], "st")
-    dma("Y", T.posi[:], T.pos[:], [], ["posi"], "pos")
-    dma("Y", T.lei[:, 0:1], T.le[:], [], ["lei"], "le")
-    dma("Y", T.vew[:, 0:M], T.ve[:], ["posi", "sti"], ["vew"], "ve")
+    op("S", lambda q: q.dma_start(T.sti[:], T.st[:]), [], nm(X("sti")), 0.05, "dst", LOCAL + 0.6)
+    op("Y", lambda q: q.dma_start(T.posi[:], T.pos[:]), [], nm(X("posi")) + [("pos", 1)], 0.05, "dpos", LOCAL + 1.0)
+    op("Y", lambda q: q.dma_start(T.lei[:, 0:1], T.le[:]), [], nm(X("lei")), 0.05, "dle", LOCAL + 1.0)
+    op("Y", lambda q: q.dma_start(T.vew[:, 0:M], T.ve[:]), [("pos", 1)], nm(C("vew", 0, M)), 0.05, "dve", LOCAL + 6.0)
 
-    op("G", lambda q: q.iota(T.pi[:, 4:5], [[0, 1]], 0, 1), [], ["pi4"])
-    iota(A("rv"), [[16, 8], [0, 4], [4, 4]])
-    iota(A("jf"), [[1, W]])
-    iota(A("grow"), [[1, 8], [0, 16]])
-    iota(A("prow"), [[0, 8], [1, 16]])
-    iota(A("c8r"), [[0, 12], [1, 8]])
-    iota(A("j16"), [[16, 128]])
-    iota(A("qb"), [[16, 132]])
-    iota(A("nj"), [[-32, 128]])
-    iota(A("zero"), [[0, 132]])
-    ms(A("iw"), 0.0)
-    ms(A("sb"), 0.0)
-    for k, (o, v) in enumerate([(ALU.arith_shift_right, 4), (ALU.bitwise_and, 15), (ALU.arith_shift_right, 3), (ALU.bitwise_and, 7)]):
-        ts(C("pi", k, key="pi%d" % k), C("pi", 4, key="pi4"), v, o)
-    cp(C("pf", 0, 5), C("pi", 0, 5, key="pi0"), x=keys("pi", 5))
-    ts(cc(1), PI, 1.0, eq, 31.0, mul)
-    ts(cc(2), PI, 2.0, eq, 1023.0, mul)
-    ts(cc(3), PI, 3.0, eq, 32767.0, mul)
-    for u in range(4):
-        ts((T.rep[:, u, :], "rep%d" % u), A("rv"), float(u), add, PP_, eq)
-    ts(cc(4), PI, 4.0, lt, cc(1), add)
-    ts(A("blk"), C("jf", 0, 8), PG, eq)
-    ts(A("i16"), J16, PI, eq)
-    ts(C("iw", 112, 128), J16, PI, eq)
-    ts(cc(5), cc(4), cc(2), add, cc(3), add)
+    iota(C("pi", 0, 2), [[16, 2]], 0, 1)
+    iota(X("jf"), [[1, 160]])
+    iota(X("grow"), [[1, 8], [0, 16]])
+    iota(C("c8r", 0, 96), [[0, 12], [1, 8]])
+    iota(C("c8r", 96, 180), [[0, 12], [1, 7]])
+    iota(PROW, [[0, 8], [1, 16]], -7)
+    iota(X("j16"), [[16, 128]])
+    iota(X("qb"), [[16, 132]], -16)
+    iota(X("nj"), [[-32, 128]])
+    for o, v in [(X("zero"), 0), (X("cm"), -128), (X("lw"), 0), (X("lhr"), 0), (X("low"), -10 ** 7), (C("base", 16, 48), -10 ** 7),
+                 (X("ob", s_[:, 0, 12:14, :]), 0), (X("ob", s_[:, 1, 12:14, :]), 0)]:
+        iota(o, [[0, o[2]]], v)
+    for o, v in [(C("xs", 0, 16), 0.0), (C("xs", L + 16, L + 32), 0.0), (C("nx", W - 1), END), (cd(2, 0, 1), 136.0), (X("ml"), 0.0),
+                 (C("ml", 12, 48, 17), -1.0), (C("vew", M, M + 16), 0.0), (C("y0", L, L + 16), 0.0), (X("c120"), 7.5), (X("hb"), -127.5),
+                 (C("dq", 0), D0), (C("al", 128), 1.0), (C("mm", 258, 264), PADV)] + [(X("lhr", s_[:, t, :, S0 + t]), 256.0) for t in range(R - 1)]:
+        ms(o, v)
+    for k, (s, o, v) in enumerate([(0, band, 15), (0, band, 3), (0, band, 12), (1, band, 240), (0, band, 16), (0, shr, 4), (0, shr, 3), (0, band, 7)]):
+        ts(C("pi", 2 + k), C("pi", s), v, o)
+    cp(C("pf", 0, 7), C("pi", 0, 7))
+    cp(C("pf", 7, 10), C("pi", 7, 10))
+    act(C("wcol", 0), P12, AF.Exp, 0.0, 1.25 * math.log(2), more=1.3)
+    ts(X("idw"), X("jf"), P16, eq)
+    ts(C("wcol", 1), P3, 1000.0, mul, PK, add)
+    ts(X("wb"), X("jf"), C("wcol", 1), eq, C("wcol", 0), mul)
+    ts(X("i16"), J16, PI, eq)
+    ts(C("cc", 2, 4), C("jf", 0, 32, 16), PO, eq)
     ts(cc(6), PI, 128.0, mul, float(-H), add)
-    ts(A("idb"), J128, PP_, eq)
-    ts(A("wb"), A("blk"), cc(5), mul)
-    ts(cc(27), PI, 0.0, eq, END, mul)
-    ts(A("blkt"), (T.grow[0:8, :], "grow"), (T.pf[0:8, 4:5], "pf"), eq)
-
-    cp(A("stb"), A("sti"))
-    rb = ["pa", "pb", "pc", "pg"]
-    for u in range(4): mm(C(rb[u], 0, 256), (T.rep[:, u, :], "rep%d" % u), A("stb"), True, True)
-    for u in range(4): act(C("win", 256 * u, 256 * u + 256, key="win%d" % u), C(rb[u], 0, 256))
-    ts(A("zi"), A("posi"), 1024, ALU.bitwise_and)
-    ts(A("w1"), A("posi"), 2048.0, lt, 2.0 ** -10, mx)
-    ts(A("w0"), A("zi"), 1.0, lt, 2.0 ** -5, mx)
-    ts(A("zu"), A("posi"), 1023, ALU.bitwise_and)
-    tt(A("ww"), A("w0"), A("w1"), mul)
-    cp((T.lef[:, 0:1], "lef"), (T.lei[:, 0:1], "lei"))
-    for gg in range(8): ts((T.lw[:, gg, :], "lw%d" % gg), A("ww"), C("blk", gg), mul)
-    cp(A("offlo"), A("zu"))
-    for u in range(8):
-        mm(C("pd", 0, 128), C("iw", 112 - 16 * u, 240 - 16 * u), (T.lw[:, :, u:128:8], "lw0"), u == 0, u == 7, x=keys("lw", 8))
-    mm(C("pe", 0), A("blkt"), (T.lef[:, 0:1], "lef"), True, True)
-    for k, (a, b, e) in enumerate(GCUT):
-        o = C("xs", 16 * a, 16 * b, key="xs%d" % k)
-        i = (T.win[:, 0:1024].indirect(T.offlo[:, a:b]), "offlo")
-        if e == "V": cp(o, i, x=keys("win", 4))
-        else: act(o, i, x=keys("win", 4))
-        for i in range(a // 8, b // 8):
-            mm(C("ph", i, 128, 16), C("xs", 128 * i, 128 * i + 128, key="xs%d" % k), A("wb"), True, True)
-        if k == 1: act(A("wc"), C("pd", 0, 128))
-    ts(cc(7), C("pe", 0), cc(6), sub)
-    ts(cc(23), C("pe", 0), 1.0, mul)
-    tt(A("zi"), C("ph", 0, 128), A("wc"), mul)
-    ts(A("zu"), A("zi"), 31, ALU.bitwise_and)
-    cp(C("sb", 8, 136), A("zu"))
-    mm(C("pa", H, H + 128), C("sb", 8, 136), A("idb"), True, True)
-    mm(C("pa", 0, H), C("sb", 7, 135), C("idb", 128 - H, 128), True, True)
-    mm(C("pa", H + 128, W), C("sb", 9, 137), C("idb", 0, H), True, True)
-    ts(A("em0"), A("jf"), cc(7), ge, END, mul)
-    ts(A("bias"), A("c8r"), PC8, ne, -BIG, mul)
-    ts(C("em0", 0, H), C("em0", 0, H), cc(27), mx)
-    mm((T.pd[0:96, 0:96], "pd"), (T.idb[0:96, 0:96], "idb"), (T.bias[0:96, :], "bias"), True, False)
-    tt(A("s"), C("pa", 0, W), A("em0"), mx)
-
-    def onehots(n, ns_):
-        for k in range(ns_): act((T.ab[:, k, :], "ab%d" % k), SO, AF.Abs, float(k + 1 - n))
-        for k in range(ns_): act((T.ob[:, :, n - 1 - k, :], "ob%d" % (n - 1 - k)), (T.ab[:, k, :], "ab%d" % k), AF.Relu, 1.0, -1.0)
-        return lambda lo, up: [ts((T.ob[:, :, p, :], "ob%d" % p), SO, float(p), eq) for p in range(lo, min(up, n - ns_))]
-
-    onehots(S0, 2)(0, S0)
-    for h in range(2): cp((T.eb[:, h, :, 0:7], "eb%d" % h), (T.ob[:, h, 0:S0, 8:64:8], "ob0"), x=keys("ob", S0))
-    cp((T.eb[:, 0, :, 7], "eb2"), (T.ob[:, 1, 0:S0, 0], "ob0"))
-    ts((T.eb[:, 1, :, 7], "eb3"), C("jf", 0, S0), C("s", H + 128), eq)
-    for n, (h, k) in enumerate([(h, k) for h in range(2) for k in range(7)] + [(0, 7), (1, 7)]):
-        r = (T.ob[:, h, 0:S0, k + 1:64:8], "ob0") if k < 7 else (T.eb[:, h], "eb0")
-        mm((T.pd[0:96, 0:96], "pd"), (T.ob[:, h, 0:S0, k:64:8], "ob0"), r, False, n == 15, x=keys("ob", S0) + (keys("eb", 4) if k == 7 else []))
-
-    def codes(last):
-        act(C("pb", 0, W), A("s"), AF.Identity, -119.0, 16.0)
-        ts(A("ns"), A("s"), -1.0, mul, -200.0, add)
-        yield
-        scan((T.nx[:, W - 2::-1], "nx"), (T.ns[:, W - 1:0:-1], "ns"), (T.s[:, W - 1:0:-1], "s"), END, mn, mx)
-        scan(C("pc", 1, W), C("ns", 0, W - 1), C("pb", 0, W - 1), 16 * END - 119, mn, mx)
-        tt((T.cd[:, 0, :], "cd0"), C("pb", 0, W), A("nx"), add)
-        tt((T.cd[:, 1, 1:W], "cd1"), C("pc", 1, W), C("s", 1, W), add)
-        yield
-        if last: return
-        scan((T.cd[:, 3, W - 2::-1], "cd3"), (T.ns[:, W - 1:0:-1], "ns"), (T.cd[:, 0, W - 1:0:-1], "cd0"), 136.0, mn, mx)
-        scan((T.cd[:, 2, 1:W], "cd2"), C("ns", 0, W - 1), (T.cd[:, 1, 0:W - 1], "cd1"), 136.0, mn, mx)
-
-    ts(A("rst"), A("c8r"), 0.0, eq, -2 * BIG, mul)
-    ts((T.x0[96:128, :], "x0r"), (T.jf[96:128, 0:96], "jf"), 0.0, mul)
-    ts(cc(0), cc(23), PI, sub)
-    ts(A("g0"), A("j16"), cc(0), ge, float(M), mul)
-    ms(C("vew", M, M + 16, key="vewp"), 0.0)
-    tt(A("g1"), A("g0"), A("posi"), mx)
-    ms(C("nx", W - 1), END)
-    ms((T.cd[:, 1:3, 0:1], "cd1"), 136.0)
-    ms((T.cd[:, 3, W - 1:W], "cd3"), 136.0)
-    cp(A("offp"), A("g1"))
-    cg = codes(False)
-    next(cg)
-    act(C("y0", 0, L), (T.vew[:, 0:M + 16].indirect(T.offp[:, 0:128]), "offp"), x=["vew", "vewp"])
-    ts(A("sel"), A("prow"), PSL, eq, 256.0, mul)
-    ms(A("low"), -1e9)
-    ms(C("base", 16, 48, key="basep"), -1e9)
-    ts(A("idf"), J128, PP_, eq)
-    scan((T.x0[0:96, :], "x0"), (T.rst[0:96, :], "rst"), (T.pd[0:96, 0:96], "pd"), 0.0, add, mx)
-    send(0)
+    ts(cc(27), PI, 0.0, eq, 1e4, mul)
+    ts(X("blkt"), X("grow", s_[0:8]), X("pf", s_[0:8, 0:1]), eq)
+    ts(X("jfs"), C("jf", 0, W), cc(6), add)
+    ts(C("jfs", 0, H), C("jfs", 0, H), cc(27), add)
+    ts(X("bias"), X("c8r"), PC8, ne, -BIG, mul)
+    ts(X("rst"), X("c8r"), 0.0, ne)
+    ts(X("x0", s_[96:128]), X("jf", s_[96:128, 0:S0]), 0.0, mul)
     ts(cc(8), PI, -16.0, mul, 119.0, add)
     ts(cc(9), PI, END, eq, -1e8, mul)
-    next(cg)
-    ts(A("bt"), J16, -1.0, mul, cc(8), add)
-    ts(A("bf"), A("i16"), -1e8, mul, cc(9), add)
-    for _ in cg: pass
+    ts(X("bt"), J16, -1.0, mul, cc(8), add)
+    ts(X("bf"), X("i16"), -1e8, mul, cc(9), add)
     ms(C("bf", 15), -1e8)
-    ms((T.ob[:, :, 12:14, :], "ob12"), 0.0)
-    tt(C("base", 0, 16), A("bt"), A("bf"), add)
-    mm(C("pe", 0, 48), A("idf"), A("base"), True, False, x=["basep"])
-    mm(C("pe", 0, S0), (T.sel[0:96, :], "sel"), (T.x0[0:96, 7:96:8], "x0"), False, False)
-    ts(cc(11), PSL, 15.0, eq)
-    ts(cc(12), PSL, 14.0, eq)
-    ts(cc(13), PSL, 14.0, lt, PSL, mul)
-    ts(cc(15), PSL, 14.0, lt, -1.0, mul)
-    ts(A("db"), A("idb"), -2048.0, mul)
-    ts(cc(14), PSL, 14.0, lt, cc(12), sub)
-    ts(cc(16), PSL, 14.0, lt, cc(11), sub)
-    ts(A("one"), A("grow"), PG, eq, 256.0, mul)
-    ts(A("none"), A("grow"), PG, eq, -256.0, mul)
-    ts(A("w0"), A("prow"), PI, gt)
-    ts(cc(22), PI, 16.0, mul)
-    ts((T.bp[:, :, 0], "bp0"), A("blk"), 1.0, mul)
-    tt(A("tri"), A("w0"), A("one"), mul)
-    ts((T.bp[:, :, 1], "bp1"), A("blk"), -1.0, mul)
-    ts((T.bn[:, :, 0], "bp2"), A("blk"), -1.0, mul)
-    ts((T.bn[:, :, 1], "bp3"), A("blk"), 1.0, mul)
-    ts(A("ntri"), A("tri"), -1.0, mul)
-    ts(A("d16"), A("idb"), cc(22), mul)
-    ts(A("idh"), A("idb"), 1.0 / 16, mul)
-    ts(A("b16"), A("blk"), 16.0, mul)
-    ms(A("c120"), 7.5)
-    ms(A("hb"), -127.5)
-    ms(C("y0", L, L + 16, key="y0p"), 0.0)
-    ms(C("dq", 0, key="dq0"), D0)
-    ms(C("al", 128, key="alp"), 1.0)
-    ms(C("zw", 0, key="zw0"), -1e9)
-    ms(C("mm", 129, 136, key="mmp"), PADV)
+    tt(C("base", 0, 16), X("bt"), X("bf"), add)
+    ts(X("idf"), J128, PP, eq)
+    ts(C("cc", 28, 32), C("jf", 12, 16), PSL, eq)
+    m12, m13, m14, m15 = [cc(28 + k) for k in range(4)]
+    ts(cc(4), PSL, -7.0, add)
+    ts(cc(10), m14, -2.0, mul, cc(4), add)
+    ts(cc(5), m14, 100.0, mul, cc(4), add)
+    ts(cc(11), m15, -2.0, mul, cc(5), add)
+    ts(cc(12), cc(5), m15, sub)
+    ts(cc(13), PSL, 12.0, lt, 100.0, mul)
+    for t in range(R - 1): ts(X("lha", s_[:, t]), PROW, cc(10 + t), eq, 256.0, mul)
+    ts(X("sr", s_[:, 0]), J7, cc(5), eq)
+    ts(X("j7"), J7, 16.0, mul)
+    ts(X("db"), IDB, -2048.0, mul)
+    ts(X("blk"), C("jf", 0, 8), PG, eq)
+    ts(X("one"), X("grow"), PG, eq, 256.0, mul)
+    ts(X("none"), X("grow"), PG, eq, -256.0, mul)
+    ts(X("fsb"), PROW, PI, sub, -7.0, gt)
+    tt(X("tri"), X("fsb"), X("one"), mul)
+    ts(X("ntri"), X("tri"), -1.0, mul)
+    ts(cc(22), PI, -16.0, mul)
+    ts(cc(7), PI, 16.0, mul, -1.0, add)
+    for b_, k, sg in [("bp", 0, 1.0), ("bp", 1, -1.0), ("bn", 0, -1.0), ("bn", 1, 1.0)]: ts(X(b_, s_[:, :, k]), X("blk"), sg, mul)
+    ts(X("d16"), IDB, cc(7), mul)
+    ts(X("nid"), IDB, -1.0, mul)
+    for k in range(2): ts(X("e%d" % k), X("idw"), cc(2 + k), mul)
+    ts(X("idh"), IDB, 1.0 / 16, mul)
+    ts(C("cc", 32, 34), C("cc", 2, 4), 16.0, mul)
+    ts(cc(20), PI, -256.0 * 4096, mul, -(128 + D0) * 4096, add)
+    ts(cc(21), PI, 256.0 * 4096, mul, (4096 + 128 + D0) * 4096, add)
+    ts(cc(24), PI, 4096.0, mul, 256.0 * 15 + 128 + D0, add)
+    ts(cc(26), cc(6), -32.0, mul, -32.0 * H - 1, add)
+    ts(X("th"), C("jf", 0, 8), 65536.0, mul, cc(24), add)
 
-    KN, CN = C("kk", 0, key="kn"), C("kk", 1, key="cn")
+    cp(X("stb"), X("sti"))
+    for u in range(4): mm(C("pa" if u < 2 else "pb", 256 * (u % 2), 256 * (u % 2) + 256), C("idw", 16 + u, 144 + u), X("stb"), True, True)
+    act(C("win", 0, 512), X("pa"))
+    cp(C("win", 512, 1024), X("pb"))
+    ts(X("zl"), X("posi"), 1023, band)
+    ts(X("zh"), X("posi"), 3072, band)
+    cp(X("offlo"), X("zl"))
+    for k in range(2): ts(C("lw", 8 + 128 * k, 136 + 128 * k), X("zh"), cc(2 + k), mul)
+    cp(X("lef", s_[:, 0:1]), X("lei", s_[:, 0:1]))
+
+    def unturn(bank, src, u, a, b, lo):
+        for h in range(4):
+            p = slice(32 * h, 32 * h + 32)
+            mm(X(bank, s_[p, lo:lo + b - a]), X(src, s_[p, u:u + 249:8]), X("i16", s_[p, a:b]), True, True)
+    for u in range(8): unturn("pg", "lw", 8 + u, 0, 16, H + 16 * u)
+    unturn("pg", "lw", 7, 16 - H, 16, 0)
+    unturn("pg", "lw", 16, 0, H, H + 128)
+    act(X("wc"), C("pg", 0, W), AF.Exp, 0.0, -5 * math.log(2) / 1024)
+    mm(C("pe", 0), X("blkt"), X("lef", s_[:, 0:1]), True, True)
+    ts(cc(23), C("pe", 0), 1.0, mul)
+    ts(C("pc", 0, W), X("jfs"), cc(23), ge, END, mul)
+    ts(C("pc", 256, 384), C("pc", H, H + 128), 8.0, mul, -6.0, add)
+    got, left = set([-1, 16]), list(range(16))
+    for e, a, b in GCUT:
+        (cp if e == "V" else act)(C("xs", 16 + 128 * a, 16 + 128 * b), pick(X("win"), C("offlo", 8 * a, 8 * b)))
+        got.update(range(a, b))
+        for i in [i for i in left if got >= set([i - 1, i, i + 1])]:
+            left.remove(i)
+            mm(C("ph", 0, W), C("wb", 16 - i, 144 - i), C("xs", 16 + 128 * i - H, 16 + 128 * i + 128 + H), len(left) == 15, not left)
+    tt(X("zi"), C("ph", 0, W), X("wc"), mul)
+    ts(X("zu"), X("zi"), 31, band)
+    tt(own(5), C("zu", H, H + 128), C("pc", 256, 384), add)
+    tt(cd(0), X("zu"), C("pc", 0, W), mx)
+    ts(cc(0), cc(23), PI, sub)
+    ts(cc(25), cc(23), -D0 / 256 - L, add)
+    ts(X("g0"), X("j16"), cc(0), ge, float(M), mul)
+    tt(X("g1"), X("g0"), X("posi"), mx)
+    cp(X("offp"), X("g1"))
+
+    mm(X("pd", s_[0:96, 0:180]), X("idw", s_[0:96, 16:112]), X("bias", s_[0:96]), True, False)
+    pl = lambda h, k: X("ob", s_[:, h, 0:S0, k:64:8])
+    for h in range(2):
+        for p in range(6): ts(X("ob", s_[:, h, p:12:6, :]), X("cd", s_[:, 0:6:5, H + 64 * h:H + 64 * h + 64]), float(p), eq)
+        mm(X("pd", s_[0:96, 96:180]), pl(h, 7), pl(h, 8), False, False)
+        if h == 1:
+            ts(X("eb"), C("jf", 0, S0), cd(0, H + 128, H + 129), eq)
+            mm(X("pd", s_[0:96, 7:96:8]), pl(0, 7), X("ob", s_[:, 1, 0:S0, 0]), False, False)
+            mm(X("pd", s_[0:96, 7:96:8]), pl(1, 7), X("eb"), False, False)
+        for k in range(7): mm(X("pd", s_[0:96, 0:96]), pl(h, k), pl(h, k + 1), False, h == 1 and k == 6)
+    scan(X("so0", s_[0:96]), X("rst", s_[0:96]), X("pd", s_[0:96, 0:180]), 0.0, mul, mx)
+    tt(X("x0", s_[0:96]), X("so0", s_[0:96, 7:96:8]), X("so0", s_[0:96, 102:180:7]), add)
+    send(0)
+
+    def codes(last):
+        act(C("pb", 0, W), cd(0), AF.Identity, -119.0, 16.0)
+        ts(X("ns"), cd(0), -1.0, mul, -200.0, add)
+        back = lambda n, *k: X(n, (slice(None),) + k + (slice(W - 1, 0, -1),))
+        scan(X("nx", s_[:, W - 2::-1]), back("ns"), back("cd", 0), END, mn, mx)
+        scan(C("pc", 1, W), C("ns", 0, W - 1), C("pb", 0, W - 1), 16 * END - 119, mn, mx)
+        tt(cd(1), C("pb", 0, W), X("nx"), add)
+        tt(cd(2, 1), C("pc", 1, W), cd(0, 1), add)
+        if last: return
+        scan(X("cd", s_[:, 4, W - 2::-1]), back("ns"), back("cd", 1), 136.0, mn, mx)
+        scan(cd(3, 1), C("ns", 0, W - 1), cd(2, 0, W - 1), 136.0, mn, mx)
+
+    KN, R16 = C("kk", 0), C("kk", 1)
+
+    def table(t, src, fin):
+        if t == 0: return mm(C("pe", 0, S0), X("lha", s_[0:96, 0]), src(0, S0, 96), False, fin)
+        mm(C("pe", 0, 16), X("lhr", s_[:, t - 1]), src(0, 16, 128), False, False)
+        mm(C("pe", 0, 16), X("lha", s_[:, t - 1]), src(16, 32, 128), False, False)
+        mm(C("pe", 0, 16), X("lhb"), src(16, 32, 128), False, fin)
 
     def winner(t):
+        mm(C("pe", 0, 48), X("idf"), X("base"), True, False)
+        table(t, lambda a, b, p: X("x%d" % t, s_[0:p, a:b]), False)
         for r in reversed(peers):
             arrived(t, r)
-            fin = r == peers[0]
-            if t == 0:
-                mm(C("pe", 0, S0), (T.sel[0:96, :], "sel"), (T.l0[0:96, r, 7:96:8], "l0"), False, fin)
-            else:
-                mm(C("pe", 0, 16), A("lhr"), (T["l%d" % t][:, r, 0:16], "l"), False, False)
-                mm(C("pe", 0, 16), A("lhl"), (T["l%d" % t][:, r, 16:32], "l"), False, fin)
-        scan(A("rm"), C("pe", 0, 48), A("low"), -1e9, mx, mx)
-        op("V", lambda q: q.transpose(T.tr[:], T.rm[:, 16:48]), ["rm"], ["tr"])
-        op("V", lambda q: q.tensor_reduce(KN[0], T.tr[:], AX.X, mx, negate=True), ["tr"], ["kn"])
+            table(t, lambda a, b, p, r=r: X("l%d" % t, s_[0:p, r, a:b]), r == peers[0])
+        scan(X("rm"), C("pe", 0, 48), X("low"), -1e9, mx, mx)
+        vtr(X("tr"), C("rm", 16, 48))
+        vec(lambda q: q.tensor_reduce(KN[0], T.tr[:], AX.X, mx, negate=True), KN, [X("tr")])
+        CN, a7, b7 = C("cn", t), X("ab7", s_[:, t, 0:1]), X("ab7", s_[:, t, 1:2])
         ts(CN, KN, M256, add, M256, sub)
+        ts(R16, KN, M16, add, M16, sub)
+        ts(a7, R16, CN, sub, 1.0 / 16, mul)
+        ts(b7, KN, R16, sub)
+        return CN, a7, b7
 
-    def decode(t):
-        a, b = C("mgb", 3 * t, key="a%d" % t), C("mgb", 3 * t + 1, key="b%d" % t)
-        k2, k3 = C("kk", 2, key="k2"), C("kk", 3, key="k3")
-        ts(k2, KN, CN, sub, 111.5, add)
-        ts(C("mgb", 3 * t + 2, key="n%d" % t), CN, -1.0 / 256, mul)
-        ts(k3, k2, M16, add, M16, sub)
-        yield
-        ts(a, k3, 1.0 / 16, mul)
-        ts(b, k2, k3, sub, 7.5, add)
+    def turn(bank, a, b):
+        for k in range(a, b): vtr(X("tr3", s_[:, k]), own(k))
+        for w in range(4):
+            for u in range(2):
+                for k in range(2):
+                    lo = 16 - 16 * (k - u)
+                    mm(C(bank, 2 * w + u, 128 * (b - a), 8), C("e%d" % u, lo, lo + 128),
+                       X("tr3", s_[:, a:b, 32 * w + 16 * k:32 * w + 16 * k + 16]), k == 0, k == 1)
 
-    def turn(h, src, bank, eng):
-        for gg in range(8):
-            o = (T["lt%d" % h][:, :, gg, :], "lt%d_%d" % (h, gg))
-            if eng[gg] == "S": act(o, src, AF.Copy, 0.0, C("blk", gg))
-            else: ts(o, src, C("blk", gg), mul)
-        return lambda: [mm(C(bank, u, 128, 8), (T["lt%d" % h][:, u], "lt%d_0" % h), A("i16"), True, True,
-                           x=keys("lt%d_" % h, 8)) for u in range(8)]
-
+    codes(False)
+    wv = cc(13)
     for t in range(R - 1):
-        c = S0 + t
-        X = "x%d" % (t + 1)
-        a, b = C("mgb", 3 * t, key="a%d" % t), C("mgb", 3 * t + 1, key="b%d" % t)
-        mm(C("pd", 0, 16), A("idb"), C("bias", 0, 16), True, False)
-        winner(t)
-        dg = decode(t)
+        c, d, x = S0 + t, DROP[t], "x%d" % (t + 1)
+        mm(C("pd", 0, 16), IDB, C("bias", 0, 16), True, False)
+        CN, a7, b7 = winner(t)
         for h in range(2):
-            ts((T.ob[:, h, 14:18, :], "fl%d" % h), (T.cd[:, :, H + 64 * h:H + 64 * h + 64], "cd0"), CN, add, KN, eq, x=keys("cd", 4))
-            if h == 0: next(dg)
+            ts(X("ob", s_[:, h, d:d + 3, :]), X("cd", s_[:, 2:5, H + 64 * h:H + 64 * h + 64]), CN, add, KN, eq)
             for k in range(8):
-                mm(C("pd", 0, 16), (T.ob[:, h, 0:16, k:64:8], "fl%d" % h), (T.ob[:, h, 16:18, k:64:8], "fl%d" % h), False,
-                   h == 1 and k == 7, x=keys("ob", 14))
-        for _ in dg: pass
-        for h in range(2): ts((T.hh[:, h], "hh%d" % h), (T.cd[:, 0:2, (H + 128) * h:(H + 128) * h + H], "cd0"), CN, add, KN, eq)
-        act(cc(17), a, AF.Identity, float(c), -1.0)
-        act(A("da"), A("idb"), AF.Copy, 0.0, cc(17))
-        for lo, n, hit, drop, key in [(H, 64, T.ob[:, 0, 14, :], T.ob[:, 0, 15, :], "fl0"), (H + 64, 64, T.ob[:, 1, 14, :], T.ob[:, 1, 15, :], "fl1"),
-                                      (0, H, T.hh[:, 0, 0, :], T.hh[:, 0, 1, :], "hh0"), (H + 128, H, T.hh[:, 1, 0, :], T.hh[:, 1, 1, :], "hh1")]:
-            mm(C("pa", lo, lo + n), A("db"), (drop, key), True, False)
-            mm(C("pa", lo, lo + n), A("da"), (hit, key), False, True)
-        ts(cc(18), a, cc(12), mul, cc(13), add)
-        ts(A("ml"), J16, a, eq, cc(15), mul)
-        ts(cc(19), b, cc(11), mul, cc(13), add)
-        ts(A("mr"), J16, cc(18), eq, cc(14), mul)
-        cp(C("ml", c), cc(16))
-        ts(A("bf"), C("pe", 0, 16), KN, add, 0.0, ne)
-        ts(A("lhr"), A("prow"), b, eq, -256.0, mul)
-        ts(A("lhl"), A("prow"), cc(19), eq, 256.0, mul)
-        scan(A("so"), C("rst", 0, 16), C("pd", 0, 16), 0.0, add, mx)
-        ts(C(X, 0, 16, key=X + "r"), A("mr"), C("so", 7), mul)
-        ts(C(X, 16, 32, key=X + "l"), A("ml"), C("so", 15), mul)
+                mm(X("pd", s_[0:8 * d + 8, 0:16]), X("ob", s_[:, h, 0:d + 1, k:64:8]), X("ob", s_[:, h, d + 1:d + 3, k:64:8]), False, h == 1 and k == 7)
+        ts(C("ml", 16 * t, 16 * t + c), C("j7", 0, c), CN, add, R16, eq)
+        scan(X("so"), C("rst", 0, 16), C("pd", 0, 16), 0.0, mul, mx)
+        ts(C(x, 0, 16), X("sr", s_[:, t]), C("so", 7), mul)
+        ts(C(x, 16, 32), C("ml", 16 * t, 16 * t + 16), C("so", 15), mul, -1.0, mul)
         send(t + 1)
-        tt(C("base", 0, 16), C("pe", 0, 16), A("bf"), mul)
-        ms(C("lhr", c, 128, 16), 256.0)
-        tt(A("s"), C("pa", 0, W), A("s"), add)
-        last = t == R - 2
-        cg = codes(last)
-        next(cg)
-        mm(C("pe", 0, 48), A("idf"), A("base"), True, False, x=["basep"])
-        mm(C("pe", 0, 16), A("lhr"), C(X, 0, 16, key=X + "r"), False, False)
-        mm(C("pe", 0, 16), A("lhl"), C(X, 16, 32, key=X + "l"), False, False)
-        if not last:
-            oh = onehots(c + 1, 5)
-            next(cg)
-            oh(0, 2)
-            for _ in cg: pass
-            oh(2, 16)
-        if t == 0:
-            ts(cc(20), PI, 256.0 * 4096, mul, (128 + D0) * 4096, add)
-            ts(cc(21), PI, -256.0 * 4096, mul, -(4096 + 128 + D0) * 4096, add)
-            ts(cc(24), PI, 4096.0, mul, 256.0 * 15 + 128 + D0, add)
-            ts(cc(25), cc(23), -D0 / 256 - L, add)
+        ts(X("hw"), X("cd", s_[:, 1:3]), CN, add, KN, eq)
+        act(cc(17), a7, AF.Identity, c - 7.0, -1.0)
+        act(X("da"), IDB, AF.Copy, 0.0, cc(17))
+        mm(C("pa", 0, W), X("db"), X("hw", s_[:, 1]), True, False)
+        mm(C("pa", 0, W), X("da"), X("hw", s_[:, 0]), False, True)
+        tt(cd(0), C("pa", 0, W), cd(0), add)
+        ts(X("bf"), C("pe", 0, 16), KN, add, 0.0, ne)
+        tt(C("base", 0, 16), C("pe", 0, 16), X("bf"), mul)
+        ts(cc(14 + t), b7, m14 if t == 0 else m15, mul, wv, add)
+        ts(X("lhr", s_[:, t, :, 0:c]), X("prow", s_[:, :, 0:c]), b7, eq, -256.0, mul)
+        ts(X("lhb"), PROW, cc(14 + t), eq, -256.0, mul)
+        codes(t == R - 2)
+        if t == R - 2: break
         if t == 1:
-            ts(A("th"), C("jf", 0, 8), 65536.0, mul, cc(24), add)
-            ts(cc(26), cc(6), -32.0, mul, -32.0 * H - 1, add)
+            act(C("pa", 0, 128), own(0), AF.Identity, -200.0, -1.0)
+            for k in (3, 4): tt(own(k), own(k), C("pa", 0, 128), mx)
+        cp(X("ob", s_[:, :, 12 + t, :]), X("hw", s_[:, 0, H:H + 128]))
+        ts(cc(18 + t), a7, (m12, m13)[t], mul, cc(14) if t == 0 else wv, add)
+        wv = cc(18 + t)
+        ts(X("srb"), J7, wv, eq)
+        tt(X("sr", s_[:, t + 1]), X("sr", s_[:, 0]), X("srb"), sub)
+        for k in (2 * t, 2 * t + 1):
+            o = C("y0", 512 * k, 512 * k + 512)
+            i = pick(X("vew"), C("offp", 32 * k, 32 * k + 32))
+            act(o, (i[0], i[1] + nm(C("pb", 0, 1)), i[2], i[3], True))
 
-    turn(2, SO, "pg", "SSSSSSSS")()
-    next(cg)
-    turn(0, (T.cd[:, 0, own], "cd0"), "ph", "VVVVVVVV")()
-    m1 = turn(1, (T.cd[:, 1, own], "cd1"), "pd", "VVVVVVSS")
-    act(C("ci", 0, 128, key="ci0"), C("ph", 0, 128))
-    ts(C("al", 0, 128), C("pg", 0, 128), 0.0, ge)
-    ts(A("sa"), C("pg", 0, 128), 0.0, mx, -128.0, add)
-    ts(C("pa", 0, 128), C("pg", 0, 128), -1.0, mul, END, add)
-    ts(C("pa", 128, 256), C("pg", 0, 128), cc(22), add, -1.0, mul)
+    turn("pg", 0, 1)
+    turn("ph", 1, 3)
+    act(X("sa"), C("pg", 0, 128), AF.Relu, 1.0)
+    act(C("pa", 0, 128), C("pg", 0, 128), AF.Identity, END, -1.0)
+    act(C("pa", 128, 256), C("pg", 0, 128), AF.Identity, cc(22), -1.0)
+    act(X("ci"), C("ph", 0, 256))
+    ts(C("al", 0, 128), X("sa"), 1.0, mn)
+    mm(C("pb", 0, 129), X("one"), C("al", 0, 129), True, False)
+    mm(C("pc", 0, 128), X("tri"), C("al", 0, 128), True, False)
+    mm(C("pc", 0, 128), X("d16"), C("al", 0, 128), False, False)
+    mm(C("pc", 0, 128), IDB, X("sa"), False, False)
+    mm(C("pc", 0, 128), IDB, X("cm"), False, False)
+    ROT = X("p3", s_[:, 0:8, :])
+    mm(ROT, IDB, X("hb"), True, False)
+    mm(C("pg", 0, 258), IDB, C("c120", 0, 258), True, False)
+    mm(C("pg", 0, 258, 2), IDB, C("qb", 0, 129), False, False)
+    mm(C("pg", 1, 258, 2), IDB, C("qb", 1, 130), False, False)
 
-    winner(R - 1)
-    m1()
-    act(C("ci", 128, 256), C("pd", 0, 128))
-    mm(C("pb", 0, 129), A("one"), C("al", 0, 129), True, False, x=["alp"])
-    mm(C("pc", 0, 128), A("tri"), C("al", 0, 128), True, False)
-    mm(C("pc", 0, 128), A("d16"), C("al", 0, 128), False, False)
-    mm(C("pc", 0, 128), A("idb"), A("sa"), False, False)
-    ts(A("fi"), A("ci"), CN, add, KN, eq, x=["ci0"])
+    CN, a7, b7 = winner(R - 1)
+    ts(X("fi"), X("ci"), CN, add, KN, eq)
     DR = C("fi", 128, 256)
-    mm(C("pb", 0, 128), A("none"), DR, False, True)
-    mm(C("pc", 0, 128), A("ntri"), DR, False, False)
-    tt(A("hd"), C("pa", 0, 256), A("fi"), mul)
-    mm(C("pc", 0, 128), A("idb"), C("hd", 0, 128), False, False)
-    mm(C("pc", 0, 128), A("idb"), C("hd", 128, 256), False, True)
-    P3 = (T.p3[:, 0:8, :], "p3")
-    mm(P3, A("idb"), A("hb"), True, False)
-    mm(C("pg", 0, 129), A("idb"), C("qb", 0, 129), True, False)
-    mm(C("pg", 0, 129), A("idb"), C("c120", 0, 129), False, False)
+    mm(C("pb", 0, 128), X("none"), DR, False, True)
+    mm(C("pc", 0, 128), X("ntri"), DR, False, False)
+    tt(X("hd"), C("pa", 0, 256), X("fi"), mul)
+    mm(C("pc", 0, 128), IDB, C("hd", 0, 128), False, False)
+    mm(C("pc", 0, 128), IDB, C("hd", 128, 256), False, True)
     scan(C("dq", 1, 130), C("pb", 0, 129), C("zero", 0, 129), D0, add, add)
     for c in range(8):
-        act((T.sg[:, c, 0:129], "sg%d" % c), C("dq", 1, 130), AF.Sign, C("th", c), -1.0, acc=C("acc", c, key="acc%d" % c))
-    ts(C("pd", 0, 129), C("dq", 0, 129), M4096, add, M4096, sub, x=["dq0"])
-    tt(C("e1", 0, 129), C("pd", 0, 129), C("dq", 0, 129), sub)
-    tt(C("ph", 0, 128), C("pc", 0, 128), C("dq", 0, 128), add, x=["dq0"])
-    ts(A("dk"), C("ph", 0, 128), M4096, add, M4096, sub)
-    tt(A("xc"), C("ph", 0, 128), A("dk"), sub)
+        act(X("sg", s_[:, c, 0:129]), C("dq", 1, 130), AF.Sign, C("th", c), -1.0, acc=C("acc", c), more=0.02)
+    ts(X("offs"), X("acc"), 130.0, add)
+    tt(C("ph", 0, 128), C("pc", 0, 128), C("dq", 0, 128), add)
+    ts(X("dk"), C("ph", 0, 128), M4096, add, M4096, sub)
+    tt(X("xc"), C("ph", 0, 128), X("dk"), sub)
+    ts(C("pe", 0, 129), C("dq", 0, 129), M4096, add, M4096, sub)
+    tt(C("q1", 0, 129), C("pe", 0, 129), C("dq", 0, 129), sub)
+    tt(X("q2"), C("pe", 0, 128), C("dq", 1, 129), sub)
+    act(C("gl", 0, 129), C("q1", 0, 129), AF.Relu, cc(20), -4096.0)
+    act(X("gw"), X("q2"), AF.Relu, cc(21), 4096.0)
+    mm(C("pg", 1, 258, 2), X("nid"), C("gl", 0, 129), False, False)
+    mm(C("pg", 2, 258, 2), X("nid"), X("gw"), False, False)
     for n, k in enumerate([1, 16, 2, 17, 3, 18, 4, 19, 5, 20, 6, 21, 7, 22, 8, 23]):
         sg = k if k <= 8 else k - 8
-        o = (T.rp[:, n, :], "rp%d" % n)
-        ts(o, A("xc"), 256.0 * sg - 2048, sub, 0.0, mn if k <= 8 else mx)
-        if k == 8: dst, r = T.p3[:, 0:8, 7], T.bp[:, :, 0]
-        elif k == 16: dst, r = T.p3[:, 0:8, 8], T.bp[:, :, 0]
-        else: dst, r = T.p3[:, 0:8, sg - 1:sg + 1], (T.bp[:] if k < 8 else T.bn[:])
-        mm((dst, "p3"), o, (r, "bp0"), False, n == 15, x=keys("bp", 4))
-    tt(A("e2"), C("pd", 0, 128), C("dq", 1, 129), sub)
-    ts(A("hi"), P3, M256, add, M256, sub)
-    tt(A("zt"), P3, A("hi"), sub)
-    mm(C("pg", 0, 128), A("zt"), A("idh"), False, True)
-    act(C("gl", 0, 129), C("e1", 0, 129), AF.Identity, cc(20), 4096.0)
-    act(A("gw"), A("e2"), AF.Identity, cc(21), -4096.0)
-    ts(A("offs"), A("acc", "acc0"), 129.0, add, 0.5, mul, x=keys("acc", 8))
-    dg = decode(R - 1)
-    next(dg)
-    tt(C("zl", 0, 129), C("pg", 0, 129), C("gl", 0, 129), mn)
-    tt(C("zw", 1, 129), C("pg", 0, 128), A("gw"), mn)
-    scan(C("mm", 0, 129), C("zl", 0, 129), C("zw", 0, 129), -1e9, mx, mx, x=["zw0"])
-    cp(A("vw"), (T.mm[:, 0:136].indirect(T.offs[:, 0:8]), "mm"), x=["offs", "mmp"])
-    ts(A("offy"), A("vw"), M16 / 16, add, M16 / 16, sub)
-
-    def ygather(k):
-        a, b, e = YCUT[k]
-        o = C("yo", 16 * a, 16 * b, key="yo%d" % k)
-        i = (T.y0[:, 0:L + 16].indirect(T.offy[:, a:b]), "offy")
-        if e == "V": cp(o, i, x=["y0", "y0p"])
-        else: act(o, i, x=["y0", "y0p"])
-        return lambda: dma("S" if k == 2 else "Y", T.y[:, 16 * a:16 * b], o[0], ["yo%d" % k], [], "y%d" % k)
-    ygather(0)()
-    d4 = ygather(4)
-    ygather(2)()
-    ts(A("g0"), A("vw"), M16 / 16, add, M16 / 16, sub)
+        o = X("rp", s_[:, n])
+        ts(o, X("xc"), 256.0 * sg - 2048, sub, 0.0, mn if k <= 8 else mx)
+        if k in (8, 16): mm(X("p3", s_[:, 0:8, 7 if k == 8 else 8]), o, X("bp", s_[:, :, 0]), False, False)
+        else: mm(X("p3", s_[:, 0:8, sg - 1:sg + 1]), o, X("bp" if k < 8 else "bn"), False, n == 15)
+    ts(X("hi"), ROT, M256, add, M256, sub)
+    tt(X("zt"), ROT, X("hi"), sub)
+    mm(C("pg", 1, 256, 2), X("zt"), X("idh"), False, False)
+    mm(C("pg", 2, 258, 2), X("zt"), X("idh"), False, True)
+    scan(C("mm", 0, 258), C("pg", 0, 258), C("zero", 0, 258), -1e9, mx, add)
+    PICK = pick(X("mm"), X("offs"))
+    ts(X("offy"), PICK, M16 / 16, add, M16 / 16, sub)
+    for k, (e, a, b) in enumerate(YCUT):
+        (cp if e == "V" else act)(C("yo", 16 * a, 16 * b), pick(X("y0"), C("offy", a, b)))
+        store("S" if k == len(YCUT) - 1 else "Y", T.y[:, 16 * a:16 * b], C("yo", 16 * a, 16 * b), "y%d" % k)
     ts(C("flb", 0), C("dq", 128), 1.0 / 256, mul, cc(25), add)
-    tt(A("fsb"), A("vw"), A("g0"), sub)
-    ts(C("flb", 1, key="fl32"), C("flb", 0), 32.0, mul, cc(26), add)
-    for _ in dg: pass
-    dma("Y", T.fl[:], T.flb[0:128:16, 0:1], ["flb"], [], "fl")
-    dma("Y", T.mg[:], T.mgb[0:1, :], [k + str(t) for k in "abn" for t in range(R)], [], "mg")
-    d4()
-    for gg in range(8): ts((T.lf[:, gg, :], "lf%d" % gg), A("fsb"), 7.5 / 16, add, C("b16", gg), mul)
-    for u in range(8):
-        mm(C("pa", 16 * u, 16 * u + 16), (T.lf[:, :, u:128:8], "lf0"), A("i16"), True, True, x=keys("lf", 8))
-    ts(A("emx"), A("nj"), C("flb", 1, key="fl32"), add, -1.0, mx)
-    d1 = ygather(1)
-    tt(A("fso"), C("pa", 0, 128), A("emx"), mn)
-    d1()
-    dma("Y", T.fs[:], T.fso[:], ["fso"], [], "fs")
-    ygather(3)()
+    store("Y", T.fl[:], X("flb", s_[0:128:16, 0:1]), "fl")
+    ts(X("mgb", s_[:, :, 0:2]), X("ab7"), 7.0, add)
+    ts(X("mgb", s_[:, :, 2]), X("cn"), -1.0 / 256, mul)
+    store("Y", T.mg[:], X("mgb", s_[0:1]), "mg")
+    cp(X("g0"), X("offy"))
+    tt(X("fsb"), PICK, X("g0"), sub)
+    ts(C("flb", 1), C("flb", 0), 32.0, mul, cc(26), add)
+    ts(X("emx"), X("nj"), C("flb", 1), add, -1.0, mx)
+    for k in range(2): ts(C("lf", 128 * k, 128 * k + 128), X("fsb"), 7.5 / 16, add, cc(32 + k), mul)
+    for u in range(8): unturn("pa", "lf", u, 0, 16, 16 * u)
+    tt(X("fso"), C("pa", 0, 128), X("emx"), mn)
+    store("Y", T.fs[:], X("fso"), "fs")
     emit(g, T, ops, [("sent", R * neng)])

@@ -12,28 +12,29 @@ PADV = L + 1.0
 D0 = -1920.0
 BIG = 30000.0
 F, B, I, U, HF = "float32", "bfloat16", "int32", "uint16", "float16"
-GCUT = [("S", 11, 16), ("V", 0, 4), ("S", 8, 11), ("V", 4, 6), ("V", 6, 7), ("S", 7, 8)]
-YCUT = [("V", 0, 24), ("S", 48, 80), ("V", 24, 48), ("S", 80, 110), ("S", 110, 128)]
+GCUT = [("S", 12, 16), ("V", 0, 4), ("S", 9, 12), ("V", 4, 7), ("S", 8, 9), ("V", 7, 8)]
+YCUT = [("V", 0, 14), ("S", 50, 74), ("V", 14, 26), ("V", 26, 38), ("S", 74, 104), ("V", 38, 50), ("S", 104, 128)]
 DROP = [14, 15, 15]
 BANKS = ("pa", "pb", "pc", "pd", "pe", "pg", "ph", "p3")
 SCRATCH = {"lei": ("sbuf", [8, 4], I), "lef": ("sbuf", [8, 4], F), "blkt": ("sbuf", [8, 128], F)}
 for _dt, _shape, _names in [
-        (I, [256], "sti"), (B, [256], "stb ci fi hd"), (B, [1024], "win"), (I, [128], "posi zh zl"), (I, [W], "zi zu"),
+        (I, [256], "sti"), (B, [256], "stb fi hd"), (B, [1024], "win"), (I, [128], "posi zh zl"), (I, [W], "zi zu"),
         (B, [M + 16], "vew"), (B, [L + 16], "y0"), (B, [L], "yo"), (B, [L + 32], "xs"), (U, [128], "offlo offp offy"),
         (U, [8], "offs"), (I, [16], "pi"), (B, [160], "idw e0 e1 wb"), (B, [272], "lw lf"),
         (B, [128], "grow da db d16 sa tri ntri one none hb cm fsb lhb gw nid"), (B, [8, 16], "prow"), (B, [3, 128], "lha tr3"),
         (B, [3, 8, 16], "lhr"), (F, [128], "idf g0 g1 dk nj j16 q2 emx fso"), (F, [W], "jfs"), (F, [160], "jf"),
-        (F, [16], "pf so bt bf j7 srb"), (F, [3, 16], "sr"), (F, [8], "blk kk th acc"), (F, [40], "cc"), (F, [32], "tr"),
+        (F, [16], "pf so bt bf"), (F, [9, 16], "sr"), (F, [8], "blk kk th acc"), (F, [40], "cc"), (F, [36], "tr"), (F, [R, 100], "ks"), (F, [100], "mk"),
         (B, [2], "wcol"), (B, [16], "i16"), (B, [W], "ns nx wc"), (HF, [128], "idh zt xc"), (B, [S0], "eb"), (B, [6, W], "cd"),
         (B, [2, 18, 64], "ob"), (B, [2, W], "hw"), (B, [180], "c8r bias"), (F, [180], "rst so0"), (HF, [S0], "x0"),
-        (HF, [32], "x1 x2 x3"), (HF, [N, S0], "l0"), (HF, [N, 32], "l1 l2 l3"), (F, [48], "base low rm ml"), (F, [R, 3], "mgb"),
-        (F, [R, 2], "ab7"), (F, [R], "cn flb"), (B, [136], "al"), (F, [132], "dq q1"), (HF, [16, 128], "rp"), (HF, [8, 2], "bp bn"),
+        (HF, [48], "x1 x2 x3"), (HF, [N, S0], "l0"), (HF, [N, 48], "l1 l2 l3"), (F, [48], "base low rm tm"), (F, [R, 3], "mgb"),
+        (F, [96], "ml"), (F, [3, 128], "sel"), (B, [6, 128], "lh"), (B, [3, 32], "ckey"), (B, [6, 128], "dc"),
+        (F, [R, 2], "ab7"), (F, [R], "flb"), (B, [136], "al"), (F, [132], "dq q1"), (HF, [16, 128], "rp"), (HF, [8, 2], "bp bn"),
         (B, [132], "qb gl"), (B, [260], "c120 zero"), (F, [8, 16], "hi"), (F, [264], "mm"), (B, [8, 132], "sg")]:
     for _n in _names.split(): SCRATCH[_n] = ("sbuf", [128] + _shape, _dt)
 for _b in BANKS: SCRATCH[_b] = ("psum", [128, 32, 16] if _b == "p3" else [128, 512], F)
 DMAS = ["pos", "st", "le", "ve", "mg", "fl", "fs"] + ["y%d" % k for k in range(len(YCUT))]
 SEMAPHORES = ["V", "S", "P", "G", "sent"] + ["d" + d for d in DMAS] + ["a%d_%d" % (t, r) for t in range(R) for r in range(N)]
-CYC, PECYC, WAKE, TRIP, LOCAL, RATE = 0.83e-3, 0.42e-3, 0.2, 1.6, 1.0, 200e3
+CYC, PECYC, WAKE, TRIP, LOCAL, RATE = 0.83e-3, 0.42e-3, 0.2, 1.4, 1.0, 300e3
 
 
 def arrange(ops):
@@ -43,7 +44,7 @@ def arrange(ops):
         for acc, write in [(a, False) for a in rd] + [(a, True) for a in wr]:
             for m, mask, wrote in seen.get(acc[0], []):
                 other = ops[m][0] != e
-                if acc[0] in BANKS and e == "P" and not other: o.add(m)
+                if (acc[0] in BANKS and e == "P" and not other) or acc[0] == "order": o.add(m)
                 elif (acc[0] in BANKS and other) or (mask & acc[1] and (write or wrote)): (o if ops[m][4] == "-" and not other else w).add(m)
         for acc, write in [(a, False) for a in rd] + [(a, True) for a in wr]: seen.setdefault(acc[0], []).append((n, acc[1], write))
         waits.append(w)
@@ -177,8 +178,8 @@ def rank_program(g, core, T, topo):
     def load(e, o, i, sem):
         op(e, lambda q: q.dma_start(o[0], i), [], nm(o) + [("queue" + e, 1)], 0.05, "d" + sem, LOCAL + 128 * o[2] * o[3] / RATE)
 
-    def store(e, o, i, sem):
-        op(e, lambda q: q.dma_start(o, i[0]), nm(i), [], 0.05, "d" + sem, LOCAL + 128 * i[2] * i[3] / RATE)
+    def store(e, o, i, sem, behind=0):
+        op(e, lambda q: q.dma_start(o, i[0]), nm(i), [], 0.05, "d" + sem, LOCAL + (128 * i[2] * i[3] + behind) / RATE)
 
     peers = [(rank + k) % N for k in range(1, N)]
     emask = topo.mask(core, T.cores[peers[0]])
@@ -205,7 +206,7 @@ def rank_program(g, core, T, topo):
     own = lambda k: cd(k, H, H + 128)
 
     op("S", lambda q: q.dma_start(T.sti[:], T.st[:]), [], nm(X("sti")), 0.05, "dst", LOCAL + 0.6)
-    op("Y", lambda q: q.dma_start(T.posi[:], T.pos[:]), [], nm(X("posi")) + [("pos", 1)], 0.05, "dpos", LOCAL + 1.0)
+    op("Y", lambda q: q.dma_start(T.posi[:], T.pos[:]), [], nm(X("posi")) + [("pos", 1)], 0.05, "dpos", LOCAL + 0.7)
     op("Y", lambda q: q.dma_start(T.lei[:, 0:1], T.le[:]), [], nm(X("lei")), 0.05, "dle", LOCAL + 1.0)
     op("Y", lambda q: q.dma_start(T.vew[:, 0:M], T.ve[:]), [("pos", 1)], nm(C("vew", 0, M)), 0.05, "dve", LOCAL + 6.0)
 
@@ -218,11 +219,12 @@ def rank_program(g, core, T, topo):
     iota(X("j16"), [[16, 128]])
     iota(X("qb"), [[16, 132]], -16)
     iota(X("nj"), [[-32, 128]])
-    for o, v in [(X("zero"), 0), (X("cm"), -128), (X("lw"), 0), (X("lhr"), 0), (X("low"), -10 ** 7), (C("base", 16, 48), -10 ** 7),
+    for o, v in [(X("zero"), 0), (X("cm"), -2048), (X("lw"), 0), (X("lhr"), 0), (X("low"), -10 ** 7), (C("base", 32, 48), -10 ** 7),
+                 (C("tm", 16, 48), -10 ** 7), (X("lh", s_[:, 0]), 256), (X("lh", s_[:, 1]), -256),
                  (X("ob", s_[:, 0, 12:14, :]), 0), (X("ob", s_[:, 1, 12:14, :]), 0)]:
         iota(o, [[0, o[2]]], v)
     for o, v in [(C("xs", 0, 16), 0.0), (C("xs", L + 16, L + 32), 0.0), (C("nx", W - 1), END), (cd(2, 0, 1), 136.0), (X("ml"), 0.0),
-                 (C("ml", 12, 48, 17), -1.0), (C("vew", M, M + 16), 0.0), (C("y0", L, L + 16), 0.0), (X("c120"), 7.5), (X("hb"), -127.5),
+                 (C("ml", 28, 96, 33), -1.0), (C("vew", M, M + 16), 0.0), (C("y0", L, L + 16), 0.0), (X("c120"), 7.5), (X("hb"), -127.5),
                  (C("dq", 0), D0), (C("al", 128), 1.0), (C("mm", 258, 264), PADV)] + [(X("lhr", s_[:, t, :, S0 + t]), 256.0) for t in range(R - 1)]:
         ms(o, v)
     for k, (s, o, v) in enumerate([(0, band, 15), (0, band, 3), (0, band, 12), (1, band, 240), (0, band, 16), (0, shr, 4), (0, shr, 3), (0, band, 7)]):
@@ -257,11 +259,27 @@ def rank_program(g, core, T, topo):
     ts(cc(5), m14, 100.0, mul, cc(4), add)
     ts(cc(11), m15, -2.0, mul, cc(5), add)
     ts(cc(12), cc(5), m15, sub)
-    ts(cc(13), PSL, 12.0, lt, 100.0, mul)
+    ts(cc(34), PSL, 12.0, lt, m15, add)
+    ts(cc(13), cc(34), 100.0, mul)
+    ts(cc(35), m15, 100.0, mul, cc(5), add)
     for t in range(R - 1): ts(X("lha", s_[:, t]), PROW, cc(10 + t), eq, 256.0, mul)
-    ts(X("sr", s_[:, 0]), J7, cc(5), eq)
-    ts(X("j7"), J7, 16.0, mul)
+    sr, sel, lh = [lambda k, n=n: X(n, s_[:, k]) for n in ("sr", "sel", "lh")]
+    ts(sr(0), J7, cc(35), eq)
+    ts(sr(3), J7, 16.0, mul)
     ts(X("db"), IDB, -2048.0, mul)
+    for k, v in enumerate([5.0, 6.0, 7.0, 16.0]): ts(X("dc", s_[:, k]), IDB, v, mul)
+    C119, SL = X("dc", s_[:, 4]), X("dc", s_[:, 5])
+    iota(C119, [[0, 128]], -119)
+    ts(C("cc", 36, 38), C("cc", 30, 32), -1000.0, mul, 1000.0, add)
+    for k in range(2):
+        ts(sr(4 + k), J7, cc(36 + k), add)
+        ts(lh(2 + k), lh(0), cc(30 + k), mul)
+    ts(sel(0), C("zero", 0, 128), PI, add, -7.0, add)
+    ts(C("base", 16, 32), X("i16"), -1e8, mul)
+    iota(X("ckey", s_[:, :, 0:16]), [[-16, 3], [-1, 16]], 119 - 16 * S0)
+    iota(X("ckey", s_[:, :, 16:32]), [[-1, 3], [-16, 16]], 119 - S0)
+    for t in range(R - 1): ms(X("ckey", s_[:, t, S0 + t:S0 + t + 1]), -1e8)
+    ts(lh(5), J128, PP, gt)
     ts(X("blk"), C("jf", 0, 8), PG, eq)
     ts(X("one"), X("grow"), PG, eq, 256.0, mul)
     ts(X("none"), X("grow"), PG, eq, -256.0, mul)
@@ -271,7 +289,8 @@ def rank_program(g, core, T, topo):
     ts(cc(22), PI, -16.0, mul)
     ts(cc(7), PI, 16.0, mul, -1.0, add)
     for b_, k, sg in [("bp", 0, 1.0), ("bp", 1, -1.0), ("bn", 0, -1.0), ("bn", 1, 1.0)]: ts(X(b_, s_[:, :, k]), X("blk"), sg, mul)
-    ts(X("d16"), IDB, cc(7), mul)
+    ts(X("fsb"), IDB, cc(7), mul)
+    tt(X("d16"), X("fsb"), X("tri"), add)
     ts(X("nid"), IDB, -1.0, mul)
     for k in range(2): ts(X("e%d" % k), X("idw"), cc(2 + k), mul)
     ts(X("idh"), IDB, 1.0 / 16, mul)
@@ -283,13 +302,15 @@ def rank_program(g, core, T, topo):
     ts(X("th"), C("jf", 0, 8), 65536.0, mul, cc(24), add)
 
     cp(X("stb"), X("sti"))
-    for u in range(4): mm(C("pa" if u < 2 else "pb", 256 * (u % 2), 256 * (u % 2) + 256), C("idw", 16 + u, 144 + u), X("stb"), True, True)
-    act(C("win", 0, 512), X("pa"))
-    cp(C("win", 512, 1024), X("pb"))
+    for u, bank in enumerate(["pa", "pb", "pc", "ph"]):
+        mm(C(bank, 0, 256), C("idw", 16 + u, 144 + u), X("stb"), True, True)
+        (cp if u % 2 else act)(C("win", 256 * u, 256 * u + 256), C(bank, 0, 256))
     ts(X("zl"), X("posi"), 1023, band)
     ts(X("zh"), X("posi"), 3072, band)
     cp(X("offlo"), X("zl"))
-    for k in range(2): ts(C("lw", 8 + 128 * k, 136 + 128 * k), X("zh"), cc(2 + k), mul)
+    for k in range(2):
+        ts(C("lw", 8 + 128 * k, 136 + 128 * k), X("zh"), cc(2 + k), mul)
+        ops[-1][2].append(("order", 1))
     cp(X("lef", s_[:, 0:1]), X("lei", s_[:, 0:1]))
 
     def unturn(bank, src, u, a, b, lo):
@@ -307,6 +328,7 @@ def rank_program(g, core, T, topo):
     got, left = set([-1, 16]), list(range(16))
     for e, a, b in GCUT:
         (cp if e == "V" else act)(C("xs", 16 + 128 * a, 16 + 128 * b), pick(X("win"), C("offlo", 8 * a, 8 * b)))
+        if e == "V": ops[-1][2].append(("order", 1))
         got.update(range(a, b))
         for i in [i for i in left if got >= set([i - 1, i, i + 1])]:
             left.remove(i)
@@ -336,76 +358,110 @@ def rank_program(g, core, T, topo):
     send(0)
 
     def codes(last):
-        act(C("pb", 0, W), cd(0), AF.Identity, -119.0, 16.0)
         ts(X("ns"), cd(0), -1.0, mul, -200.0, add)
         back = lambda n, *k: X(n, (slice(None),) + k + (slice(W - 1, 0, -1),))
+        if last:
+            ts(cd(5), cd(0), 16.0, mul, -119.0, add)
+            scan(X("cd", s_[:, 1, W - 2::-1]), back("ns"), back("cd", 0), END, mn, mx)
+            return scan(cd(2, 1), C("ns", 0, W - 1), cd(5, 0, W - 1), 16 * END - 119, mn, mx)
+        act(C("pb", 0, W), cd(0), AF.Identity, -119.0, 16.0)
         scan(X("nx", s_[:, W - 2::-1]), back("ns"), back("cd", 0), END, mn, mx)
         scan(C("pc", 1, W), C("ns", 0, W - 1), C("pb", 0, W - 1), 16 * END - 119, mn, mx)
         tt(cd(1), C("pb", 0, W), X("nx"), add)
         tt(cd(2, 1), C("pc", 1, W), cd(0, 1), add)
-        if last: return
         scan(X("cd", s_[:, 4, W - 2::-1]), back("ns"), back("cd", 1), 136.0, mn, mx)
         scan(cd(3, 1), C("ns", 0, W - 1), cd(2, 0, W - 1), 136.0, mn, mx)
 
-    KN, R16 = C("kk", 0), C("kk", 1)
+    iota(C("mk", 0, 96), [[0, 96]])
+    iota(C("tr", 32, 36), [[0, 4]])
+    for k, v in enumerate([M16, -M16, M256, -M256]): ms(C("mk", 96 + k), v)
 
     def table(t, src, fin):
         if t == 0: return mm(C("pe", 0, S0), X("lha", s_[0:96, 0]), src(0, S0, 96), False, fin)
         mm(C("pe", 0, 16), X("lhr", s_[:, t - 1]), src(0, 16, 128), False, False)
-        mm(C("pe", 0, 16), X("lha", s_[:, t - 1]), src(16, 32, 128), False, False)
-        mm(C("pe", 0, 16), X("lhb"), src(16, 32, 128), False, fin)
+        mm(C("pe", 0, 16), X("lha", s_[:, t - 1]), src(32, 48, 128), False, False)
+        mm(C("pe", 0, 16), X("lhb"), src(32, 48, 128), False, fin)
+
+    def changed(t, bank, src, fin):
+        mm(C(bank, 0, 32), lh(0), src(0, 32, 128), False, False)
+        mm(C(bank, 32, 64), lh(1), src(0, 32, 128), False, False)
+        mm(C(bank, 0, 16), lh(DROP[t - 1] - 12), src(32, 48, 128), False, False)
+        mm(C(bank, 32, 48), lh(4), src(32, 48, 128), False, fin)
 
     def winner(t):
-        mm(C("pe", 0, 48), X("idf"), X("base"), True, False)
-        table(t, lambda a, b, p: X("x%d" % t, s_[0:p, a:b]), False)
-        for r in reversed(peers):
-            arrived(t, r)
-            table(t, lambda a, b, p, r=r: X("l%d" % t, s_[0:p, r, a:b]), r == peers[0])
-        scan(X("rm"), C("pe", 0, 48), X("low"), -1e9, mx, mx)
-        vtr(X("tr"), C("rm", 16, 48))
-        vec(lambda q: q.tensor_reduce(KN[0], T.tr[:], AX.X, mx, negate=True), KN, [X("tr")])
-        CN, a7, b7 = C("cn", t), X("ab7", s_[:, t, 0:1]), X("ab7", s_[:, t, 1:2])
-        ts(CN, KN, M256, add, M256, sub)
-        ts(R16, KN, M16, add, M16, sub)
-        ts(a7, R16, CN, sub, 1.0 / 16, mul)
-        ts(b7, KN, R16, sub)
-        return CN, a7, b7
+        parts = [lambda a, b, p: X("x%d" % t, s_[0:p, a:b])] + [lambda a, b, p, r=r: X("l%d" % t, s_[0:p, r, a:b]) for r in reversed(peers)]
+        bank = "pg" if t < R - 1 else "pd"
+        if t:
+            mm(C(bank, 0, 32), IDB, X("ckey", s_[:, t - 1]), True, False)
+            mm(C(bank, 96, 100), IDB, C("cm", 0, 4), False, False)
+            mm(C(bank, 32, 64), X("sel", s_[0:16, 2]), X("base", s_[0:16, 0:32]), False, False)
+            mm(C(bank, 48, 64), X("sel", s_[0:16, 1]), X("tr", s_[0:16, 0:16]), False, False)
+            scan(X("rm"), X("tm"), X("low"), -1e9, mx, mx)
+            vtr(C(bank, 64, 96), C("rm", 16, 48))
+        if t < R - 1: mm(C("pe", 0, 16 if t else 48), X("idf"), C("base", 0, 16 if t else 48), True, False)
+        for k in range(N):
+            if k: arrived(t, peers[-k])
+            if t: changed(t, bank, parts[k], k == N - 1)
+            if t < R - 1: table(t, parts[k], k == N - 1)
+        if t == 0:
+            scan(X("rm"), C("pe", 0, 48), X("low"), -1e9, mx, mx)
+            vtr(C("tr", 0, 32), C("rm", 16, 48))
+        lo = 0 if t else 64
+        scan(X("ks", s_[:, t, lo:100]), C(bank, 0, 100) if t else X("tr"), C("mk", lo, 100), -1e9, mx, add)
+        K, K16, K256 = [X("ks", s_[:, t, k:k + 1]) for k in (95, 97, 99)]
+        a7, b7 = X("ab7", s_[:, t, 0:1]), X("ab7", s_[:, t, 1:2])
+        ts(a7, K256, K16, sub, 1.0 / 16, mul)
+        ts(b7, K16, K, sub)
+        return K, K16, K256, a7, b7
 
-    def turn(bank, a, b):
+    def turn(bank, a, b, first, last):
         for k in range(a, b): vtr(X("tr3", s_[:, k]), own(k))
         for w in range(4):
             for u in range(2):
                 for k in range(2):
                     lo = 16 - 16 * (k - u)
                     mm(C(bank, 2 * w + u, 128 * (b - a), 8), C("e%d" % u, lo, lo + 128),
-                       X("tr3", s_[:, a:b, 32 * w + 16 * k:32 * w + 16 * k + 16]), k == 0, k == 1)
+                       X("tr3", s_[:, a:b, 32 * w + 16 * k:32 * w + 16 * k + 16]), first and w + u + k == 0, last and w + u + k == 5)
 
     codes(False)
     wv = cc(13)
     for t in range(R - 1):
         c, d, x = S0 + t, DROP[t], "x%d" % (t + 1)
         mm(C("pd", 0, 16), IDB, C("bias", 0, 16), True, False)
-        CN, a7, b7 = winner(t)
+        K, K16, K256, a7, b7 = winner(t)
         for h in range(2):
-            ts(X("ob", s_[:, h, d:d + 3, :]), X("cd", s_[:, 2:5, H + 64 * h:H + 64 * h + 64]), CN, add, KN, eq)
+            ts(X("ob", s_[:, h, d:d + 3, :]), X("cd", s_[:, 2:5, H + 64 * h:H + 64 * h + 64]), K, add, K256, eq)
             for k in range(8):
                 mm(X("pd", s_[0:8 * d + 8, 0:16]), X("ob", s_[:, h, 0:d + 1, k:64:8]), X("ob", s_[:, h, d + 1:d + 3, k:64:8]), False, h == 1 and k == 7)
-        ts(C("ml", 16 * t, 16 * t + c), C("j7", 0, c), CN, add, R16, eq)
+        ts(C("ml", 32 * t + 16, 32 * t + 16 + c), X("sr", s_[:, 3, 0:c]), K16, add, K256, eq)
+        ts(sr(6), sr(d - 10), K, add, K16, eq)
+        tt(C("ml", 32 * t, 32 * t + 16), sr(6), sr(t), sub)
         scan(X("so"), C("rst", 0, 16), C("pd", 0, 16), 0.0, mul, mx)
-        ts(C(x, 0, 16), X("sr", s_[:, t]), C("so", 7), mul)
-        ts(C(x, 16, 32), C("ml", 16 * t, 16 * t + 16), C("so", 15), mul, -1.0, mul)
+        ts(C(x, 0, 16), sr(t), C("so", 7), mul)
+        ts(C(x, 16, 48), C("ml", 32 * t, 32 * t + 32), C("so", 15), mul, -1.0, mul)
         send(t + 1)
-        ts(X("hw"), X("cd", s_[:, 1:3]), CN, add, KN, eq)
-        act(cc(17), a7, AF.Identity, c - 7.0, -1.0)
-        act(X("da"), IDB, AF.Copy, 0.0, cc(17))
+        ts(X("hw"), X("cd", s_[:, 1:3]), K, add, K256, eq)
         mm(C("pa", 0, W), X("db"), X("hw", s_[:, 1]), True, False)
+        ts(cc(17), K16, K256, sub, 1.0 / 16, mul)
+        act(X("da"), IDB, AF.Copy, 0.0, cc(17))
+        mm(C("pa", 0, W), X("dc", s_[:, t]), X("hw", s_[:, 0]), False, False)
         mm(C("pa", 0, W), X("da"), X("hw", s_[:, 0]), False, True)
         tt(cd(0), C("pa", 0, W), cd(0), add)
-        ts(X("bf"), C("pe", 0, 16), KN, add, 0.0, ne)
+        ts(X("bf"), C("pe", 0, 16), K, ne)
         tt(C("base", 0, 16), C("pe", 0, 16), X("bf"), mul)
-        ts(cc(14 + t), b7, m14 if t == 0 else m15, mul, wv, add)
-        ts(X("lhr", s_[:, t, :, 0:c]), X("prow", s_[:, :, 0:c]), b7, eq, -256.0, mul)
-        ts(X("lhb"), PROW, cc(14 + t), eq, -256.0, mul)
+        if t: ts(C("kk", 2), K16, K, sub, -100.0, add)
+        ts(cc(14 + t), C("kk", 2) if t else b7, m15 if t else m14, mul, wv, add)
+        if t < R - 2:
+            ts(X("lhr", s_[:, t, :, 0:c]), X("prow", s_[:, :, 0:c]), b7, eq, -256.0, mul)
+            ts(X("lhb"), PROW, cc(14 + t), eq, -256.0, mul)
+        ts(C("kk", 3), cc(10 + t), b7, eq, 256.0, mul)
+        ts(C("kk", 4), cc(14 + t), b7, eq, 256.0, mul)
+        ts(lh(4), C("zero", 0, 128), C("kk", 3), add, C("kk", 4), sub)
+        ts(sel(1), sel(0), a7, eq)
+        ts(sel(2), sel(0), b7, eq)
+        vtr(C("tr", 0, 32), C("base", 0, 32))
+        ts(sr(7), C("ml", 32 * t + 16, 32 * t + 32), X("sel", s_[:, 2, 0:1]), mx, 1.0, lt)
+        tt(C("tm", 0, 16), C("base", 0, 16), sr(7), mul)
         codes(t == R - 2)
         if t == R - 2: break
         if t == 1:
@@ -414,49 +470,55 @@ def rank_program(g, core, T, topo):
         cp(X("ob", s_[:, :, 12 + t, :]), X("hw", s_[:, 0, H:H + 128]))
         ts(cc(18 + t), a7, (m12, m13)[t], mul, cc(14) if t == 0 else wv, add)
         wv = cc(18 + t)
-        ts(X("srb"), J7, wv, eq)
-        tt(X("sr", s_[:, t + 1]), X("sr", s_[:, 0]), X("srb"), sub)
+        ts(sr(8), J7, wv, eq)
+        tt(sr(t + 1), sr(0), sr(8), sub)
         for k in (2 * t, 2 * t + 1):
             o = C("y0", 512 * k, 512 * k + 512)
             i = pick(X("vew"), C("offp", 32 * k, 32 * k + 32))
             act(o, (i[0], i[1] + nm(C("pb", 0, 1)), i[2], i[3], True))
 
-    turn("pg", 0, 1)
-    turn("ph", 1, 3)
-    act(X("sa"), C("pg", 0, 128), AF.Relu, 1.0)
-    act(C("pa", 0, 128), C("pg", 0, 128), AF.Identity, END, -1.0)
-    act(C("pa", 128, 256), C("pg", 0, 128), AF.Identity, cc(22), -1.0)
-    act(X("ci"), C("ph", 0, 256))
+    turn("pb", 0, 1, True, True)
+    act(X("sa"), C("pb", 0, 128), AF.Relu, 1.0)
+    act(SL, C("pb", 0, 128))
+    mm(C("ph", 0, 128), IDB, C119, True, False)
+    mm(C("ph", 128, 256), IDB, C("zero", 0, 128), False, False)
+    turn("ph", 1, 3, False, False)
+    mm(C("ph", 0, 128), X("dc", s_[:, 3]), SL, False, False)
+    mm(C("ph", 128, 256), IDB, SL, False, True)
+    act(C("pa", 0, 128), C("pb", 0, 128), AF.Identity, END, -1.0)
+    act(C("pa", 128, 256), C("pb", 0, 128), AF.Identity, cc(22), -1.0)
     ts(C("al", 0, 128), X("sa"), 1.0, mn)
     mm(C("pb", 0, 129), X("one"), C("al", 0, 129), True, False)
-    mm(C("pc", 0, 128), X("tri"), C("al", 0, 128), True, False)
-    mm(C("pc", 0, 128), X("d16"), C("al", 0, 128), False, False)
+    mm(C("pc", 0, 128), IDB, X("cm"), True, False)
     mm(C("pc", 0, 128), IDB, X("sa"), False, False)
-    mm(C("pc", 0, 128), IDB, X("cm"), False, False)
+    mm(C("pc", 0, 128), X("d16"), C("al", 0, 128), False, False)
+    mm(C("pe", 0, 128), C("al", 0, 128), X("one"), True, False)
     ROT = X("p3", s_[:, 0:8, :])
     mm(ROT, IDB, X("hb"), True, False)
     mm(C("pg", 0, 258), IDB, C("c120", 0, 258), True, False)
     mm(C("pg", 0, 258, 2), IDB, C("qb", 0, 129), False, False)
     mm(C("pg", 1, 258, 2), IDB, C("qb", 1, 130), False, False)
 
-    CN, a7, b7 = winner(R - 1)
-    ts(X("fi"), X("ci"), CN, add, KN, eq)
+    K, K16, K256, a7, b7 = winner(R - 1)
+    for h in (1, 0): ts(C("fi", 128 * h, 128 * h + 128), C("ph", 128 * h, 128 * h + 128), K, add, K256, eq)
     DR = C("fi", 128, 256)
+    mm(C("pe", 0, 128), DR, X("none"), False, True)
     mm(C("pb", 0, 128), X("none"), DR, False, True)
     mm(C("pc", 0, 128), X("ntri"), DR, False, False)
+    act(X("da"), C("pe", 0, 128))
     tt(X("hd"), C("pa", 0, 256), X("fi"), mul)
     mm(C("pc", 0, 128), IDB, C("hd", 0, 128), False, False)
-    mm(C("pc", 0, 128), IDB, C("hd", 128, 256), False, True)
+    mm(C("pc", 0, 128), IDB, C("hd", 128, 256), False, False)
+    mm(C("pc", 0, 128), X("da"), lh(5), False, True)
     scan(C("dq", 1, 130), C("pb", 0, 129), C("zero", 0, 129), D0, add, add)
     for c in range(8):
         act(X("sg", s_[:, c, 0:129]), C("dq", 1, 130), AF.Sign, C("th", c), -1.0, acc=C("acc", c), more=0.02)
     ts(X("offs"), X("acc"), 130.0, add)
-    tt(C("ph", 0, 128), C("pc", 0, 128), C("dq", 0, 128), add)
-    ts(X("dk"), C("ph", 0, 128), M4096, add, M4096, sub)
-    tt(X("xc"), C("ph", 0, 128), X("dk"), sub)
-    ts(C("pe", 0, 129), C("dq", 0, 129), M4096, add, M4096, sub)
-    tt(C("q1", 0, 129), C("pe", 0, 129), C("dq", 0, 129), sub)
-    tt(X("q2"), C("pe", 0, 128), C("dq", 1, 129), sub)
+    ts(X("dk"), C("pc", 0, 128), M4096, add, M4096, sub)
+    tt(X("xc"), C("pc", 0, 128), X("dk"), sub)
+    ts(C("ph", 0, 129), C("dq", 0, 129), M4096, add, M4096, sub)
+    tt(C("q1", 0, 129), C("ph", 0, 129), C("dq", 0, 129), sub)
+    tt(X("q2"), C("ph", 0, 128), C("dq", 1, 129), sub)
     act(C("gl", 0, 129), C("q1", 0, 129), AF.Relu, cc(20), -4096.0)
     act(X("gw"), X("q2"), AF.Relu, cc(21), 4096.0)
     mm(C("pg", 1, 258, 2), X("nid"), C("gl", 0, 129), False, False)
@@ -476,11 +538,12 @@ def rank_program(g, core, T, topo):
     ts(X("offy"), PICK, M16 / 16, add, M16 / 16, sub)
     for k, (e, a, b) in enumerate(YCUT):
         (cp if e == "V" else act)(C("yo", 16 * a, 16 * b), pick(X("y0"), C("offy", a, b)))
-        store("S" if k == len(YCUT) - 1 else "Y", T.y[:, 16 * a:16 * b], C("yo", 16 * a, 16 * b), "y%d" % k)
+        store("S" if k == len(YCUT) - 1 else "Y", T.y[:, 16 * a:16 * b], C("yo", 16 * a, 16 * b), "y%d" % k,
+              sum(4096 * (n - m) for _, m, n in YCUT[k + 1:]) + 65536)
     ts(C("flb", 0), C("dq", 128), 1.0 / 256, mul, cc(25), add)
     store("Y", T.fl[:], X("flb", s_[0:128:16, 0:1]), "fl")
     ts(X("mgb", s_[:, :, 0:2]), X("ab7"), 7.0, add)
-    ts(X("mgb", s_[:, :, 2]), X("cn"), -1.0 / 256, mul)
+    ts(X("mgb", s_[:, :, 2]), X("ks", s_[:, :, 99]), 1.0 / 256, mul)
     store("Y", T.mg[:], X("mgb", s_[0:1]), "mg")
     cp(X("g0"), X("offy"))
     tt(X("fsb"), PICK, X("g0"), sub)

@@ -8,33 +8,38 @@ H = 12
 W = 128 + 2 * H
 END = 15.0
 M16, M256, M4096 = 1.5 * 2.0 ** 27, 1.5 * 2.0 ** 31, 1.5 * 2.0 ** 35
-PADV = L + 1.0
+PADV = L + 2.0
 D0 = -1920.0
 BIG = 30000.0
 F, B, I, U, HF = "float32", "bfloat16", "int32", "uint16", "float16"
-GCUT = [("S", 12, 16), ("V", 0, 4), ("S", 9, 12), ("V", 4, 7), ("S", 8, 9), ("V", 7, 8)]
-YCUT = [("V", 0, 14), ("S", 50, 74), ("V", 14, 26), ("V", 26, 38), ("S", 74, 104), ("V", 38, 50), ("S", 104, 128)]
+GCUT = [("S", 64, 90), ("V", 38, 64), ("S", 90, 114), ("V", 14, 38), ("S", 114, 128), ("V", 0, 14)]
+YOUT = [("Y", 0, 12), ("Y", 48, 72), ("Y", 12, 24), ("Y", 72, 104), ("Y", 24, 48), ("S", 104, 128)]
+YCUT = [("V", 0, 12), ("V", 12, 24), ("V", 24, 48), ("S", 48, 72), ("S", 72, 104), ("S", 104, 128)]
 DROP = [14, 15, 15]
 BANKS = ("pa", "pb", "pc", "pd", "pe", "pg", "ph", "p3")
 SCRATCH = {"lei": ("sbuf", [8, 4], I), "lef": ("sbuf", [8, 4], F), "blkt": ("sbuf", [8, 128], F)}
 for _dt, _shape, _names in [
         (I, [256], "sti"), (B, [256], "stb fi hd"), (B, [1024], "win"), (I, [128], "posi zh zl"), (I, [W], "zi zu"),
         (B, [M + 16], "vew"), (B, [L + 16], "y0"), (B, [L], "yo"), (B, [L + 32], "xs"), (U, [128], "offlo offp offy"),
-        (U, [8], "offs"), (I, [16], "pi"), (B, [160], "idw e0 e1 wb"), (B, [272], "lw lf"),
-        (B, [128], "grow da db d16 sa tri ntri one none hb cm fsb lhb gw nid"), (B, [8, 16], "prow"), (B, [3, 128], "lha tr3"),
-        (B, [3, 8, 16], "lhr"), (F, [128], "idf g0 g1 dk nj j16 q2 emx fso"), (F, [W], "jfs"), (F, [160], "jf"),
-        (F, [16], "pf so bt bf"), (F, [9, 16], "sr"), (F, [8], "blk kk th acc"), (F, [40], "cc"), (F, [36], "tr"), (F, [R, 100], "ks"), (F, [100], "mk"),
-        (B, [2], "wcol"), (B, [16], "i16"), (B, [W], "ns nx wc"), (HF, [128], "idh zt xc"), (B, [S0], "eb"), (B, [6, W], "cd"),
+        (U, [8], "offs"), (I, [16], "pi"), (B, [160], "idw e0 e1 wb"), (B, [272], "lw"), (B, [4, 32], "lf"), (B, [2, 144], "srt"),
+        (B, [128], "grow da db d16 sa tri ntri one none cm fsb lhb nid"), (B, [8, 16], "prow"), (B, [3, 128], "lha tr3"),
+        (B, [3, 8, 16], "lhr"), (F, [128], "idf g0 g1 nj j16 emx fso"), (F, [160], "jf"),
+        (F, [16], "pf so bt bf"), (F, [10, 16], "sr"), (F, [8], "kk th acc"), (F, [40], "cc"), (F, [36], "tr"), (F, [R, 100], "ks"),
+        (F, [100], "mk"),
+        (F, [2], "wcol"), (B, [16], "i16"), (B, [W], "ns nx wc"), (HF, [128], "xc"), (B, [S0], "eb"), (B, [6, W], "cd"),
         (B, [2, 18, 64], "ob"), (B, [2, W], "hw"), (B, [180], "c8r bias"), (F, [180], "rst so0"), (HF, [S0], "x0"),
-        (HF, [48], "x1 x2 x3"), (HF, [N, S0], "l0"), (HF, [N, 48], "l1 l2 l3"), (F, [48], "base low rm tm"), (F, [R, 3], "mgb"),
-        (F, [96], "ml"), (F, [3, 128], "sel"), (B, [6, 128], "lh"), (B, [3, 32], "ckey"), (B, [6, 128], "dc"),
-        (F, [R, 2], "ab7"), (F, [R], "flb"), (B, [136], "al"), (F, [132], "dq q1"), (HF, [16, 128], "rp"), (HF, [8, 2], "bp bn"),
-        (B, [132], "qb gl"), (B, [260], "c120 zero"), (F, [8, 16], "hi"), (F, [264], "mm"), (B, [8, 132], "sg")]:
+        (HF, [48], "x1 x2 x3"), (HF, [N, S0], "l0"), (HF, [N, 48], "l1 l2 l3"), (F, [48], "low rm tm"), (F, [64], "base"), (F, [R, 3], "mgb"),
+        (F, [96], "ml"), (F, [5, 128], "sel"), (B, [6, 128], "lh"), (B, [3, 32], "ckey"), (B, [16, 128], "dc"),
+        (F, [R, 2], "ab7"), (F, [R], "flb"), (B, [136], "al"), (F, [132], "dq zw zo gp dk"), (HF, [16, 128], "rp"), (HF, [144], "bm"),
+        (B, [4, 132], "cnt"), (B, [132], "qb q1 zero half"), (F, [136], "mm"), (B, [8, 132], "sg")]:
     for _n in _names.split(): SCRATCH[_n] = ("sbuf", [128] + _shape, _dt)
-for _b in BANKS: SCRATCH[_b] = ("psum", [128, 32, 16] if _b == "p3" else [128, 512], F)
-DMAS = ["pos", "st", "le", "ve", "mg", "fl", "fs"] + ["y%d" % k for k in range(len(YCUT))]
+for _b in BANKS: SCRATCH[_b] = ("psum", [128, 512], F)
+DMAS = ["pos", "st", "le", "ve", "mg", "fl", "fs"] + ["y%d" % k for k in range(len(YOUT))]
 SEMAPHORES = ["V", "S", "P", "G", "sent"] + ["d" + d for d in DMAS] + ["a%d_%d" % (t, r) for t in range(R) for r in range(N)]
-CYC, PECYC, WAKE, TRIP, LOCAL, RATE = 0.83e-3, 0.42e-3, 0.2, 1.4, 1.0, 300e3
+CYC, PECYC, SLOW, WAKE, TRIP, LOCAL, RATE = 0.83e-3, 0.42e-3, 1.2, 0.2, 1.0, 1.0, 300e3
+
+
+PLAN, SWEEPS = [], 1
 
 
 def arrange(ops):
@@ -44,7 +49,7 @@ def arrange(ops):
         for acc, write in [(a, False) for a in rd] + [(a, True) for a in wr]:
             for m, mask, wrote in seen.get(acc[0], []):
                 other = ops[m][0] != e
-                if (acc[0] in BANKS and e == "P" and not other) or acc[0] == "order": o.add(m)
+                if (acc[0] in BANKS and e == "P" and not other) or acc[0][:5] == "order": o.add(m)
                 elif (acc[0] in BANKS and other) or (mask & acc[1] and (write or wrote)): (o if ops[m][4] == "-" and not other else w).add(m)
         for acc, write in [(a, False) for a in rd] + [(a, True) for a in wr]: seen.setdefault(acc[0], []).append((n, acc[1], write))
         waits.append(w)
@@ -55,27 +60,37 @@ def arrange(ops):
         for m in waits[n] | before[n]: nxt[m].append(n)
     chain = [0.0] * len(ops)
     for m in reversed(range(len(ops))): chain[m] = ops[m][5] + max([gap(m, n) + chain[n] for n in nxt[m]] + [ops[m][6]])
-    miss = [len(waits[n] | before[n]) for n in range(len(ops))]
-    ready, free, order = dict((n, 0.0) for n in range(len(ops)) if not miss[n]), {}, []
-    at = [0.0] * len(ops)
-    while ready:
-        t, e = min((max(r, free.get(ops[n][0], 0.0)), ops[n][0]) for n, r in ready.items())
-        mine = [n for n in ready if ops[n][0] == e]
-        n = max((n for n in mine if ready[n] <= t), key=lambda n: (chain[n], -n))
-        soon = [m for m in mine if chain[m] > chain[n] and ready[m] < t + ops[n][5] - 0.03]
-        if soon: n = min(soon, key=lambda m: (ready[m], -chain[m]))
-        free[e] = max(ready.pop(n), t) + ops[n][5]
-        order.append(n)
-        for k in nxt[n]:
-            at[k] = max(at[k], free[e] + gap(n, k))
-            miss[k] -= 1
-            if not miss[k]: ready[k] = at[k]
-    return order, waits
+    prv = [waits[n] | before[n] for n in range(len(ops))]
+
+    def sweep(ahead, behind, lag, at, rank):
+        miss = [len(a) for a in ahead]
+        ready, free, order, end = dict((n, at[n]) for n in range(len(ops)) if not miss[n]), {}, [], [0.0] * len(ops)
+        while ready:
+            t, e = min((max(r, free.get(ops[n][0], 0.0)), ops[n][0]) for n, r in ready.items())
+            mine = [n for n in ready if ops[n][0] == e]
+            n = max((n for n in mine if ready[n] <= t), key=lambda n: (rank[n], -n))
+            soon = [m for m in mine if rank[m] > rank[n] and ready[m] < t + ops[n][5] - 0.03]
+            if soon: n = min(soon, key=lambda m: (ready[m], -rank[m]))
+            free[e] = end[n] = max(ready.pop(n), t) + ops[n][5]
+            order.append(n)
+            for k in behind[n]:
+                at[k] = max(at[k], end[n] + lag(n, k))
+                miss[k] -= 1
+                if not miss[k]: ready[k] = at[k]
+        return order, end
+    best = None
+    for _ in range(SWEEPS):
+        order, end = sweep(prv, nxt, gap, [0.0] * len(ops), chain)
+        span = max(end[n] + ops[n][6] for n in order)
+        if best is None or span < best[0]: best = (span, order)
+        chain = sweep(nxt, prv, lambda n, k: gap(k, n), [o[6] for o in ops], end)[1]
+    return best[1], waits
 
 
 def emit(g, T, ops, tail):
     q = {"V": g.vector, "S": g.scalar, "P": g.tensor, "G": g, "Y": g.sync}
-    order, deps = arrange(ops)
+    if not PLAN: PLAN.extend(arrange(ops))
+    order, deps = PLAN
     place = dict((n, k) for k, n in enumerate(order))
     done, upto, after, waits = dict.fromkeys(q, 0), dict.fromkeys(q, 0), {}, {}
     for n in order:
@@ -137,7 +152,7 @@ def rank_program(g, core, T, topo):
         return x[0] if isinstance(x, tuple) else x
 
     def op(e, fn, rd, wr, cost, sem=None, lat=0.0):
-        ops.append((e, fn, rd, wr, sem, cost, lat))
+        ops.append((e, fn, rd, wr, sem, cost if sem else SLOW * cost, lat))
 
     def vec(fn, o, ins, more=(), two=False):
         rate = 0.5 if all(x[3] == 2 for x in [o] + ins) else 1.0
@@ -190,7 +205,7 @@ def rank_program(g, core, T, topo):
         tr = RemoteDMATransfer(dst_ids=[DstId(rid=topo.addr(T.cores[r])[0], pnc=topo.addr(T.cores[r])[1]) for r in peers],
                                dma_engine_mask=emask, remote_sem=T.sem["a%d_%d" % (t, rank)], srcs=[T["x%d" % t][:]],
                                dsts=[T["l%d" % t][:, rank, :] for r in peers])
-        op("G", lambda q: q.remote_dma_fused([tr], local_sem=T.sem.sent), nm(X("x%d" % t)), [("trip%d" % t, 1)], 0.3, "-", TRIP)
+        op("G", lambda q: q.remote_dma_fused([tr], local_sem=T.sem.sent), nm(X("x%d" % t)), [("trip%d" % t, 1)], 0.3, "-", TRIP if t else 1.6 * TRIP)
 
     def arrived(t, r):
         op("P", lambda q: q.wait_ge(T.sem["a%d_%d" % (t, r)], neng), [("trip%d" % t, 1)], nm(X("l%d" % t, s_[:, r])), 0.0, "-")
@@ -217,91 +232,100 @@ def rank_program(g, core, T, topo):
     iota(C("c8r", 96, 180), [[0, 12], [1, 7]])
     iota(PROW, [[0, 8], [1, 16]], -7)
     iota(X("j16"), [[16, 128]])
-    iota(X("qb"), [[16, 132]], -16)
+    iota(X("qb"), [[16, 132]])
     iota(X("nj"), [[-32, 128]])
-    for o, v in [(X("zero"), 0), (X("cm"), -2048), (X("lw"), 0), (X("lhr"), 0), (X("low"), -10 ** 7), (C("base", 32, 48), -10 ** 7),
-                 (C("tm", 16, 48), -10 ** 7), (X("lh", s_[:, 0]), 256), (X("lh", s_[:, 1]), -256),
+    for o, v in [(X("cm"), -2048), (X("lhr"), 0), (X("low"), -10 ** 7), (C("base", 48, 64), -10 ** 7),
+                 (C("tm", 16, 48), -10 ** 7), (X("lh", s_[:, 1]), -256),
                  (X("ob", s_[:, 0, 12:14, :]), 0), (X("ob", s_[:, 1, 12:14, :]), 0)]:
         iota(o, [[0, o[2]]], v)
-    for o, v in [(C("xs", 0, 16), 0.0), (C("xs", L + 16, L + 32), 0.0), (C("nx", W - 1), END), (cd(2, 0, 1), 136.0), (X("ml"), 0.0),
-                 (C("ml", 28, 96, 33), -1.0), (C("vew", M, M + 16), 0.0), (C("y0", L, L + 16), 0.0), (X("c120"), 7.5), (X("hb"), -127.5),
-                 (C("dq", 0), D0), (C("al", 128), 1.0), (C("mm", 258, 264), PADV)] + [(X("lhr", s_[:, t, :, S0 + t]), 256.0) for t in range(R - 1)]:
+    ms(X("zero"), 0.0)
+    act(X("lh", s_[:, 0]), C("zero", 0, 128), AF.Exp, 8 * math.log(2), 1.0, more=1.3)
+    ops[-1][2].append(("order exp", 1))
+    for o, v in [(C("xs", 0, 16), END), (C("xs", L + 16, L + 32), END), (C("lw", 7, 272, 257), 0.0), (C("nx", W - 1), END), (cd(2, 0, 1), 136.0), (X("ml"), 0.0),
+                 (C("ml", 28, 96, 33), -1.0), (C("vew", M, M + 16), 0.0), (C("y0", L, L + 16), 0.0),
+                 (C("dq", 0), D0), (C("al", 128), 1.0), (C("mm", 129, 136), PADV), (C("zw", 0), -1e9)] + [(X("lhr", s_[:, t, :, S0 + t]), 256.0) for t in range(R - 1)]:
         ms(o, v)
     for k, (s, o, v) in enumerate([(0, band, 15), (0, band, 3), (0, band, 12), (1, band, 240), (0, band, 16), (0, shr, 4), (0, shr, 3), (0, band, 7)]):
         ts(C("pi", 2 + k), C("pi", s), v, o)
     cp(C("pf", 0, 7), C("pi", 0, 7))
     cp(C("pf", 7, 10), C("pi", 7, 10))
-    act(C("wcol", 0), P12, AF.Exp, 0.0, 1.25 * math.log(2), more=1.3)
+    act(C("wcol", 0), P12, AF.Exp, 0.0, 1.25 * math.log(2))
+    ops[-1][2].append(("order exp", 1))
     ts(X("idw"), X("jf"), P16, eq)
     ts(C("wcol", 1), P3, 1000.0, mul, PK, add)
-    ts(X("wb"), X("jf"), C("wcol", 1), eq, C("wcol", 0), mul)
+    ts(X("e0"), X("jf"), C("wcol", 1), eq)
+    ops[-1][2].append(("order st", 1))
+    act(X("wb"), X("e0"), AF.Copy, 0.0, C("wcol", 0))
     ts(X("i16"), J16, PI, eq)
     ts(C("cc", 2, 4), C("jf", 0, 32, 16), PO, eq)
     ts(cc(6), PI, 128.0, mul, float(-H), add)
-    ts(cc(27), PI, 0.0, eq, 1e4, mul)
     ts(X("blkt"), X("grow", s_[0:8]), X("pf", s_[0:8, 0:1]), eq)
-    ts(X("jfs"), C("jf", 0, W), cc(6), add)
-    ts(C("jfs", 0, H), C("jfs", 0, H), cc(27), add)
     ts(X("bias"), X("c8r"), PC8, ne, -BIG, mul)
     ts(X("rst"), X("c8r"), 0.0, ne)
     ts(X("x0", s_[96:128]), X("jf", s_[96:128, 0:S0]), 0.0, mul)
-    ts(cc(8), PI, -16.0, mul, 119.0, add)
-    ts(cc(9), PI, END, eq, -1e8, mul)
-    ts(X("bt"), J16, -1.0, mul, cc(8), add)
-    ts(X("bf"), X("i16"), -1e8, mul, cc(9), add)
-    ms(C("bf", 15), -1e8)
-    tt(C("base", 0, 16), X("bt"), X("bf"), add)
-    ts(X("idf"), J128, PP, eq)
+    lin = lambda o, i, scale, bias=0.0: act(o, i, AF.Identity, bias, scale)
+    lin(cc(8), PI, -16.0, 119.0)
+    lin(X("bt"), J16, -1.0, cc(8))
+    for k in (0, 32): lin(C("base", k, k + 16), X("i16"), -1e8)
+    TAB = C("base", 16, 32)
+    tt(TAB, X("bt"), C("base", 32, 48), add)
+    lin(X("idf"), IDB, 1.0)
     ts(C("cc", 28, 32), C("jf", 12, 16), PSL, eq)
     m12, m13, m14, m15 = [cc(28 + k) for k in range(4)]
-    ts(cc(4), PSL, -7.0, add)
-    ts(cc(10), m14, -2.0, mul, cc(4), add)
-    ts(cc(5), m14, 100.0, mul, cc(4), add)
-    ts(cc(11), m15, -2.0, mul, cc(5), add)
-    ts(cc(12), cc(5), m15, sub)
-    ts(cc(34), PSL, 12.0, lt, m15, add)
-    ts(cc(13), cc(34), 100.0, mul)
-    ts(cc(35), m15, 100.0, mul, cc(5), add)
-    for t in range(R - 1): ts(X("lha", s_[:, t]), PROW, cc(10 + t), eq, 256.0, mul)
+    lin(cc(4), PSL, 1.0, -7.0)
+    lin(cc(10), m14, -2.0, cc(4))
+    lin(cc(5), m14, 100.0, cc(4))
+    lin(cc(11), m15, -2.0, cc(5))
+    lin(cc(12), m15, -1.0, cc(5))
+    ts(cc(13), PSL, 12.0, lt, 100.0, mul)
+    lin(cc(35), m15, 100.0, cc(5))
+    for t in range(R - 2): ts(X("lha", s_[:, t]), PROW, cc(10 + t), eq, 256.0, mul)
     sr, sel, lh = [lambda k, n=n: X(n, s_[:, k]) for n in ("sr", "sel", "lh")]
-    ts(sr(0), J7, cc(35), eq)
-    ts(sr(3), J7, 16.0, mul)
-    ts(X("db"), IDB, -2048.0, mul)
-    for k, v in enumerate([5.0, 6.0, 7.0, 16.0]): ts(X("dc", s_[:, k]), IDB, v, mul)
+    ts(C("ml", 0, 16), J7, cc(35), eq, -1.0, mul)
+    lin(sr(3), J7, 16.0)
+    lin(X("db"), IDB, -2048.0)
+    for k, v in enumerate([5.0, 6.0, 7.0, 16.0]): lin(X("dc", s_[:, k]), IDB, v)
     C119, SL = X("dc", s_[:, 4]), X("dc", s_[:, 5])
     iota(C119, [[0, 128]], -119)
-    ts(C("cc", 36, 38), C("cc", 30, 32), -1000.0, mul, 1000.0, add)
+    lin(cc(38), m15, 1000.0)
+    lin(sr(9), J7, 1.0, cc(38))
     for k in range(2):
-        ts(sr(4 + k), J7, cc(36 + k), add)
-        ts(lh(2 + k), lh(0), cc(30 + k), mul)
-    ts(sel(0), C("zero", 0, 128), PI, add, -7.0, add)
-    ts(C("base", 16, 32), X("i16"), -1e8, mul)
+        lin(lh(2 + k), lh(0), cc(30 + k))
+    lin(cc(9), PI, 1.0, -7.0)
+    lin(sel(0), C("zero", 0, 128), 1.0, cc(9))
     iota(X("ckey", s_[:, :, 0:16]), [[-16, 3], [-1, 16]], 119 - 16 * S0)
     iota(X("ckey", s_[:, :, 16:32]), [[-1, 3], [-16, 16]], 119 - S0)
     for t in range(R - 1): ms(X("ckey", s_[:, t, S0 + t:S0 + t + 1]), -1e8)
     ts(lh(5), J128, PP, gt)
-    ts(X("blk"), C("jf", 0, 8), PG, eq)
     ts(X("one"), X("grow"), PG, eq, 256.0, mul)
-    ts(X("none"), X("grow"), PG, eq, -256.0, mul)
+    lin(X("none"), X("one"), -1.0)
     ts(X("fsb"), PROW, PI, sub, -7.0, gt)
     tt(X("tri"), X("fsb"), X("one"), mul)
-    ts(X("ntri"), X("tri"), -1.0, mul)
-    ts(cc(22), PI, -16.0, mul)
-    ts(cc(7), PI, 16.0, mul, -1.0, add)
-    for b_, k, sg in [("bp", 0, 1.0), ("bp", 1, -1.0), ("bn", 0, -1.0), ("bn", 1, 1.0)]: ts(X(b_, s_[:, :, k]), X("blk"), sg, mul)
-    ts(X("fsb"), IDB, cc(7), mul)
+    lin(X("ntri"), X("tri"), -1.0)
+    lin(cc(22), PI, -16.0, 104.0)
+    lin(X("half"), X("zero"), 1.0, 8.5 / 16)
+    lin(cc(7), PI, 16.0, -1.0)
+    ts(X("bm"), C("jf", 0, 144), PK, eq, 1.0 / 16, mul)
+    dc = lambda k: X("dc", s_[:, k])
+    ts(cc(33 + 1), PI, 0.0, eq, 1.0 / 256, mul)
+    for k, m, v in [(6, IDB, 8192.0), (7, IDB, -8192.0), (8, X("one"), cc(34)), (9, IDB, -1.0 / 256), (13, IDB, 1.0 / 256)]: lin(dc(k), m, v)
+    iota(dc(11), [[0, 128]], -10240)
+    tt(dc(10), X("tri"), X("one"), sub)
+    lin(dc(15), dc(10), -1.0)
+    lin(cc(39), PI, -256.0, 2048.0)
+    lin(dc(12), C("zero", 0, 128), 1.0, cc(39))
+    lin(X("fsb"), IDB, cc(7))
     tt(X("d16"), X("fsb"), X("tri"), add)
-    ts(X("nid"), IDB, -1.0, mul)
-    for k in range(2): ts(X("e%d" % k), X("idw"), cc(2 + k), mul)
-    ts(X("idh"), IDB, 1.0 / 16, mul)
-    ts(C("cc", 32, 34), C("cc", 2, 4), 16.0, mul)
-    ts(cc(20), PI, -256.0 * 4096, mul, -(128 + D0) * 4096, add)
-    ts(cc(21), PI, 256.0 * 4096, mul, (4096 + 128 + D0) * 4096, add)
-    ts(cc(24), PI, 4096.0, mul, 256.0 * 15 + 128 + D0, add)
-    ts(cc(26), cc(6), -32.0, mul, -32.0 * H - 1, add)
-    ts(X("th"), C("jf", 0, 8), 65536.0, mul, cc(24), add)
+    lin(X("nid"), IDB, -1.0)
+    for k in range(2): lin(X("e%d" % k), X("idw"), cc(2 + k))
+    lin(cc(20), PI, -4096.0, -16 * D0)
+    lin(cc(21), PI, -4096.0, -16 * D0 - 65536)
+    lin(cc(24), PI, 4096.0, 256.0 * 15 + 128 + D0)
+    lin(cc(26), cc(6), -32.0, -32.0 * H - 1)
+    lin(X("th"), C("jf", 0, 8), 65536.0, cc(24))
 
     cp(X("stb"), X("sti"))
+    ops[-1][2].append(("order st", 1))
     for u, bank in enumerate(["pa", "pb", "pc", "ph"]):
         mm(C(bank, 0, 256), C("idw", 16 + u, 144 + u), X("stb"), True, True)
         (cp if u % 2 else act)(C("win", 256 * u, 256 * u + 256), C(bank, 0, 256))
@@ -312,6 +336,7 @@ def rank_program(g, core, T, topo):
         ts(C("lw", 8 + 128 * k, 136 + 128 * k), X("zh"), cc(2 + k), mul)
         ops[-1][2].append(("order", 1))
     cp(X("lef", s_[:, 0:1]), X("lei", s_[:, 0:1]))
+    ops[-1][2].append(("order", 1))
 
     def unturn(bank, src, u, a, b, lo):
         for h in range(4):
@@ -322,23 +347,25 @@ def rank_program(g, core, T, topo):
     unturn("pg", "lw", 16, 0, H, H + 128)
     act(X("wc"), C("pg", 0, W), AF.Exp, 0.0, -5 * math.log(2) / 1024)
     mm(C("pe", 0), X("blkt"), X("lef", s_[:, 0:1]), True, True)
-    ts(cc(23), C("pe", 0), 1.0, mul)
-    ts(C("pc", 0, W), X("jfs"), cc(23), ge, END, mul)
+    ts(cc(23), C("pe", 0), cc(6), sub)
+    ts(C("pc", 0, W), C("jf", 0, W), cc(23), ge, END, mul)
     ts(C("pc", 256, 384), C("pc", H, H + 128), 8.0, mul, -6.0, add)
-    got, left = set([-1, 16]), list(range(16))
+    got, left = set([-1, 128]), list(range(16))
     for e, a, b in GCUT:
-        (cp if e == "V" else act)(C("xs", 16 + 128 * a, 16 + 128 * b), pick(X("win"), C("offlo", 8 * a, 8 * b)))
+        (cp if e == "V" else act)(C("xs", 16 + 16 * a, 16 + 16 * b), pick(X("win"), C("offlo", a, b)))
         if e == "V": ops[-1][2].append(("order", 1))
         got.update(range(a, b))
-        for i in [i for i in left if got >= set([i - 1, i, i + 1])]:
+        for i in [i for i in left if got >= set(range(8 * i - 1, 8 * i + 9))]:
             left.remove(i)
             mm(C("ph", 0, W), C("wb", 16 - i, 144 - i), C("xs", 16 + 128 * i - H, 16 + 128 * i + 128 + H), len(left) == 15, not left)
     tt(X("zi"), C("ph", 0, W), X("wc"), mul)
     ts(X("zu"), X("zi"), 31, band)
     tt(own(5), C("zu", H, H + 128), C("pc", 256, 384), add)
     tt(cd(0), X("zu"), C("pc", 0, W), mx)
-    ts(cc(0), cc(23), PI, sub)
-    ts(cc(25), cc(23), -D0 / 256 - L, add)
+    lin(cc(27), PI, 127.0, float(-H))
+    lin(cc(1), PI, 128.0, -D0 / 256 - L - H)
+    lin(cc(0), cc(23), 1.0, cc(27))
+    lin(cc(25), cc(23), 1.0, cc(1))
     ts(X("g0"), X("j16"), cc(0), ge, float(M), mul)
     tt(X("g1"), X("g0"), X("posi"), mx)
     cp(X("offp"), X("g1"))
@@ -346,7 +373,10 @@ def rank_program(g, core, T, topo):
     mm(X("pd", s_[0:96, 0:180]), X("idw", s_[0:96, 16:112]), X("bias", s_[0:96]), True, False)
     pl = lambda h, k: X("ob", s_[:, h, 0:S0, k:64:8])
     for h in range(2):
-        for p in range(6): ts(X("ob", s_[:, h, p:12:6, :]), X("cd", s_[:, 0:6:5, H + 64 * h:H + 64 * h + 64]), float(p), eq)
+        two = X("cd", s_[:, 0:6:5, H + 64 * h:H + 64 * h + 64])
+        for p in range(6 - 2 * h): ts(X("ob", s_[:, h, p:12:6, :]), two, float(p), eq)
+        for p in range(6 - 2 * h, 6): act(C("hd", 128 * p - 512, 128 * p - 384), two, AF.Abs, float(-p))
+        for p in range(6 - 2 * h, 6): act(X("ob", s_[:, h, p:12:6, :]), C("hd", 128 * p - 512, 128 * p - 384), AF.Relu, 1.0, -1.0)
         mm(X("pd", s_[0:96, 96:180]), pl(h, 7), pl(h, 8), False, False)
         if h == 1:
             ts(X("eb"), C("jf", 0, S0), cd(0, H + 128, H + 129), eq)
@@ -361,7 +391,7 @@ def rank_program(g, core, T, topo):
         ts(X("ns"), cd(0), -1.0, mul, -200.0, add)
         back = lambda n, *k: X(n, (slice(None),) + k + (slice(W - 1, 0, -1),))
         if last:
-            ts(cd(5), cd(0), 16.0, mul, -119.0, add)
+            lin(cd(5), cd(0), 16.0, -119.0)
             scan(X("cd", s_[:, 1, W - 2::-1]), back("ns"), back("cd", 0), END, mn, mx)
             return scan(cd(2, 1), C("ns", 0, W - 1), cd(5, 0, W - 1), 16 * END - 119, mn, mx)
         act(C("pb", 0, W), cd(0), AF.Identity, -119.0, 16.0)
@@ -394,11 +424,12 @@ def rank_program(g, core, T, topo):
         if t:
             mm(C(bank, 0, 32), IDB, X("ckey", s_[:, t - 1]), True, False)
             mm(C(bank, 96, 100), IDB, C("cm", 0, 4), False, False)
-            mm(C(bank, 32, 64), X("sel", s_[0:16, 2]), X("base", s_[0:16, 0:32]), False, False)
+            mm(C(bank, 32, 64), IDB, C("zero", 0, 32), False, False)
+            mm(C(bank, 16, 64), X("sel", s_[0:16, 2]), X("base", s_[0:16, 0:48]), False, False)
             mm(C(bank, 48, 64), X("sel", s_[0:16, 1]), X("tr", s_[0:16, 0:16]), False, False)
             scan(X("rm"), X("tm"), X("low"), -1e9, mx, mx)
             vtr(C(bank, 64, 96), C("rm", 16, 48))
-        if t < R - 1: mm(C("pe", 0, 16 if t else 48), X("idf"), C("base", 0, 16 if t else 48), True, False)
+        if t < R - 1: mm(C("pe", 0, 16 if t else 48), X("idf"), C("base", 16, 32 if t else 64), True, False)
         for k in range(N):
             if k: arrived(t, peers[-k])
             if t: changed(t, bank, parts[k], k == N - 1)
@@ -434,44 +465,43 @@ def rank_program(g, core, T, topo):
             for k in range(8):
                 mm(X("pd", s_[0:8 * d + 8, 0:16]), X("ob", s_[:, h, 0:d + 1, k:64:8]), X("ob", s_[:, h, d + 1:d + 3, k:64:8]), False, h == 1 and k == 7)
         ts(C("ml", 32 * t + 16, 32 * t + 16 + c), X("sr", s_[:, 3, 0:c]), K16, add, K256, eq)
-        ts(sr(6), sr(d - 10), K, add, K16, eq)
-        tt(C("ml", 32 * t, 32 * t + 16), sr(6), sr(t), sub)
         scan(X("so"), C("rst", 0, 16), C("pd", 0, 16), 0.0, mul, mx)
-        ts(C(x, 0, 16), sr(t), C("so", 7), mul)
+        ts(C(x, 0, 16), C("ml", 32 * t, 32 * t + 16), C("so", 7), mul, -1.0, mul)
         ts(C(x, 16, 48), C("ml", 32 * t, 32 * t + 32), C("so", 15), mul, -1.0, mul)
+        ops[-1][2].append(("order send", 1))
         send(t + 1)
         ts(X("hw"), X("cd", s_[:, 1:3]), K, add, K256, eq)
         mm(C("pa", 0, W), X("db"), X("hw", s_[:, 1]), True, False)
-        ts(cc(17), K16, K256, sub, 1.0 / 16, mul)
-        act(X("da"), IDB, AF.Copy, 0.0, cc(17))
+        lin(X("da"), X("nid"), a7)
         mm(C("pa", 0, W), X("dc", s_[:, t]), X("hw", s_[:, 0]), False, False)
         mm(C("pa", 0, W), X("da"), X("hw", s_[:, 0]), False, True)
         tt(cd(0), C("pa", 0, W), cd(0), add)
+        ops[-1][2].append(("order send", 1))
         ts(X("bf"), C("pe", 0, 16), K, ne)
-        tt(C("base", 0, 16), C("pe", 0, 16), X("bf"), mul)
-        if t: ts(C("kk", 2), K16, K, sub, -100.0, add)
-        ts(cc(14 + t), C("kk", 2) if t else b7, m15 if t else m14, mul, wv, add)
+        tt(TAB, C("pe", 0, 16), X("bf"), mul)
+        lin(cc(14 + t), b7, m15 if t else m14, wv)
         if t < R - 2:
             ts(X("lhr", s_[:, t, :, 0:c]), X("prow", s_[:, :, 0:c]), b7, eq, -256.0, mul)
             ts(X("lhb"), PROW, cc(14 + t), eq, -256.0, mul)
-        ts(C("kk", 3), cc(10 + t), b7, eq, 256.0, mul)
-        ts(C("kk", 4), cc(14 + t), b7, eq, 256.0, mul)
-        ts(lh(4), C("zero", 0, 128), C("kk", 3), add, C("kk", 4), sub)
-        ts(sel(1), sel(0), a7, eq)
-        ts(sel(2), sel(0), b7, eq)
-        vtr(C("tr", 0, 32), C("base", 0, 32))
+        ts(C("kk", 3), cc(10 + t), b7, eq)
+        ts(C("kk", 4), cc(14 + t), b7, eq, C("kk", 3), sub)
+        lin(lh(4), lh(1), C("kk", 4))
+        for k, v in ((2, b7), (1, a7)):
+            act(sel(2 + k), sel(0), AF.Abs, v, -1.0)
+            act(sel(k), sel(2 + k), AF.Relu, 1.0, -1.0)
+        vtr(C("tr", 0, 32), C("base", 16, 48))
         ts(sr(7), C("ml", 32 * t + 16, 32 * t + 32), X("sel", s_[:, 2, 0:1]), mx, 1.0, lt)
-        tt(C("tm", 0, 16), C("base", 0, 16), sr(7), mul)
+        tt(C("tm", 0, 16), TAB, sr(7), mul)
         codes(t == R - 2)
         if t == R - 2: break
         if t == 1:
             act(C("pa", 0, 128), own(0), AF.Identity, -200.0, -1.0)
             for k in (3, 4): tt(own(k), own(k), C("pa", 0, 128), mx)
-        cp(X("ob", s_[:, :, 12 + t, :]), X("hw", s_[:, 0, H:H + 128]))
-        ts(cc(18 + t), a7, (m12, m13)[t], mul, cc(14) if t == 0 else wv, add)
+        act(X("ob", s_[:, :, 12 + t, :]), X("hw", s_[:, 0, H:H + 128]))
+        lin(cc(18 + t), a7, (m12, m13)[t], cc(14) if t == 0 else wv)
         wv = cc(18 + t)
-        ts(sr(8), J7, wv, eq)
-        tt(sr(t + 1), sr(0), sr(8), sub)
+        ts(sr(8), sr(9), wv, eq)
+        tt(C("ml", 32 * t + 32, 32 * t + 48), sr(8), C("ml", 0, 16), add)
         for k in (2 * t, 2 * t + 1):
             o = C("y0", 512 * k, 512 * k + 512)
             i = pick(X("vew"), C("offp", 32 * k, 32 * k + 32))
@@ -486,71 +516,95 @@ def rank_program(g, core, T, topo):
     mm(C("ph", 0, 128), X("dc", s_[:, 3]), SL, False, False)
     mm(C("ph", 128, 256), IDB, SL, False, True)
     act(C("pa", 0, 128), C("pb", 0, 128), AF.Identity, END, -1.0)
-    act(C("pa", 128, 256), C("pb", 0, 128), AF.Identity, cc(22), -1.0)
     ts(C("al", 0, 128), X("sa"), 1.0, mn)
     mm(C("pb", 0, 129), X("one"), C("al", 0, 129), True, False)
-    mm(C("pc", 0, 128), IDB, X("cm"), True, False)
-    mm(C("pc", 0, 128), IDB, X("sa"), False, False)
-    mm(C("pc", 0, 128), X("d16"), C("al", 0, 128), False, False)
+    mm(C("pc", 0, 129), X("tri"), C("al", 0, 129), True, False)
+    mm(C("pc", 1, 129), dc(15), C("al", 0, 128), False, False)
     mm(C("pe", 0, 128), C("al", 0, 128), X("one"), True, False)
-    ROT = X("p3", s_[:, 0:8, :])
-    mm(ROT, IDB, X("hb"), True, False)
-    mm(C("pg", 0, 258), IDB, C("c120", 0, 258), True, False)
-    mm(C("pg", 0, 258, 2), IDB, C("qb", 0, 129), False, False)
-    mm(C("pg", 1, 258, 2), IDB, C("qb", 1, 130), False, False)
+    ROT, LAST = C("pg", 0, 128), C("p3", 256, 384)
+    mm(C("pg", 0, 129), IDB, C("qb", 0, 129), True, False)
+    mm(C("pg", 0, 129), IDB, C("half", 0, 129), False, False)
+    mm(ROT, IDB, dc(12), False, False)
+    mm(LAST, X("one"), C("al", 0, 128), True, False)
 
     K, K16, K256, a7, b7 = winner(R - 1)
     for h in (1, 0): ts(C("fi", 128 * h, 128 * h + 128), C("ph", 128 * h, 128 * h + 128), K, add, K256, eq)
     DR = C("fi", 128, 256)
+    CODE = C("pd", 0, 128)
     mm(C("pe", 0, 128), DR, X("none"), False, True)
     mm(C("pb", 0, 128), X("none"), DR, False, True)
     mm(C("pc", 0, 128), X("ntri"), DR, False, False)
+    mm(C("pc", 1, 129), dc(10), DR, False, True)
+    mm(LAST, X("none"), DR, False, False)
     act(X("da"), C("pe", 0, 128))
-    tt(X("hd"), C("pa", 0, 256), X("fi"), mul)
-    mm(C("pc", 0, 128), IDB, C("hd", 0, 128), False, False)
-    mm(C("pc", 0, 128), IDB, C("hd", 128, 256), False, False)
-    mm(C("pc", 0, 128), X("da"), lh(5), False, True)
+    scan(C("gp", 0, 129), C("pc", 0, 129), C("zero", 0, 129), D0, add, add)
+    tt(C("hd", 0, 128), C("pa", 0, 128), C("fi", 0, 128), mul)
+    AL = C("al", 0, 128)
+    for n, (l, r) in enumerate([(IDB, dc(11)), (IDB, X("sa")), (X("d16"), AL), (dc(6), AL), (X("ntri"), DR), (dc(7), DR),
+                                (IDB, C("hd", 0, 128)), (X("da"), lh(5))]):
+        mm(CODE, l, r, n == 0, n == 7)
     scan(C("dq", 1, 130), C("pb", 0, 129), C("zero", 0, 129), D0, add, add)
     for c in range(8):
         act(X("sg", s_[:, c, 0:129]), C("dq", 1, 130), AF.Sign, C("th", c), -1.0, acc=C("acc", c), more=0.02)
-    ts(X("offs"), X("acc"), 130.0, add)
-    ts(X("dk"), C("pc", 0, 128), M4096, add, M4096, sub)
-    tt(X("xc"), C("pc", 0, 128), X("dk"), sub)
-    ts(C("ph", 0, 129), C("dq", 0, 129), M4096, add, M4096, sub)
-    tt(C("q1", 0, 129), C("ph", 0, 129), C("dq", 0, 129), sub)
-    tt(X("q2"), C("ph", 0, 128), C("dq", 1, 129), sub)
-    act(C("gl", 0, 129), C("q1", 0, 129), AF.Relu, cc(20), -4096.0)
-    act(X("gw"), X("q2"), AF.Relu, cc(21), 4096.0)
-    mm(C("pg", 1, 258, 2), X("nid"), C("gl", 0, 129), False, False)
-    mm(C("pg", 2, 258, 2), X("nid"), X("gw"), False, False)
-    for n, k in enumerate([1, 16, 2, 17, 3, 18, 4, 19, 5, 20, 6, 21, 7, 22, 8, 23]):
-        sg = k if k <= 8 else k - 8
-        o = X("rp", s_[:, n])
-        ts(o, X("xc"), 256.0 * sg - 2048, sub, 0.0, mn if k <= 8 else mx)
-        if k in (8, 16): mm(X("p3", s_[:, 0:8, 7 if k == 8 else 8]), o, X("bp", s_[:, :, 0]), False, False)
-        else: mm(X("p3", s_[:, 0:8, sg - 1:sg + 1]), o, X("bp" if k < 8 else "bn"), False, n == 15)
-    ts(X("hi"), ROT, M256, add, M256, sub)
-    tt(X("zt"), ROT, X("hi"), sub)
-    mm(C("pg", 1, 256, 2), X("zt"), X("idh"), False, False)
-    mm(C("pg", 2, 258, 2), X("zt"), X("idh"), False, True)
-    scan(C("mm", 0, 258), C("pg", 0, 258), C("zero", 0, 258), -1e9, mx, add)
+    ts(X("offs"), X("acc"), 129.0, add, 0.5, mul)
+    ts(C("dk", 0, 129), C("gp", 0, 129), M4096, add, M4096, sub)
+    tt(C("q1", 0, 129), C("gp", 0, 129), C("dk", 0, 129), sub)
+    ops[-1][2].append(("order rows", 1))
+    tt(X("xc"), CODE, C("dk", 0, 128), sub)
+    ops[-1][2].append(("order rows", 1))
+    mm(LAST, dc(8), C("q1", 0, 128), False, False)
+    mm(C("p3", 0, 129), dc(8), C("q1", 0, 129), False, True)
+    cnt = lambda k, n=128: X("cnt", s_[:, k, 0:n])
+    for o, i, bias, v in [(cnt(0), LAST, cc(22), 1.0 / 16), (cnt(1), LAST, -136.0, 1.0 / 16), (cnt(2), LAST, cc(21), 16.0),
+                          (cnt(3, 129), C("p3", 0, 129), cc(20), 16.0)]:
+        act(o, i, AF.Relu, bias, v)
+    for k in range(16):
+        o = X("rp", s_[:, k])
+        ts(o, X("xc"), 256.0 * k - 2048, mx, 256.0 * k - 1792, mn)
+        mm(ROT, C("bm", 16 - k, 144 - k), o, False, k == 15)
+        if 10 <= k < 14: mm(ROT, [X("nid"), IDB, dc(9), dc(13)][k - 10], cnt(k - 10), False, False)
+    tt(C("zo", 0, 129), C("pg", 0, 129), cnt(3, 129), sub)
+    tt(C("zw", 1, 129), ROT, cnt(2), mn)
+    scan(C("mm", 0, 129), C("zo", 0, 129), C("zw", 0, 129), -1e9, mx, mx)
     PICK = pick(X("mm"), X("offs"))
-    ts(X("offy"), PICK, M16 / 16, add, M16 / 16, sub)
-    for k, (e, a, b) in enumerate(YCUT):
-        (cp if e == "V" else act)(C("yo", 16 * a, 16 * b), pick(X("y0"), C("offy", a, b)))
-        store("S" if k == len(YCUT) - 1 else "Y", T.y[:, 16 * a:16 * b], C("yo", 16 * a, 16 * b), "y%d" % k,
-              sum(4096 * (n - m) for _, m, n in YCUT[k + 1:]) + 65536)
+    ts(X("offy"), PICK, M16 / 16, add, M16 / 16 + 1, sub)
+    pieces = [(a, b) for e, a, b in YCUT if e == "V"]
+
+    def inturn(fn, *a):
+        for f, b in [(fn, a)] + [(cp, (C("yo", 16 * m, 16 * n), pick(X("y0"), C("offy", m, n)))) for m, n in pieces[:1]]:
+            f(*b)
+            ops[-1][2].append(("order tail", 1))
+        del pieces[:1]
+    for e, a, b in YCUT:
+        if e == "S": act(C("yo", 16 * a, 16 * b), pick(X("y0"), C("offy", a, b)))
+    inturn(cp, X("g0"), X("offy"))
+    inturn(tt, X("fsb"), PICK, X("g0"), sub)
+    for u in range(3):
+        vtr(X("lf", s_[:, u]), C("fsb", u, 128, 4))
+        ops[-1][2].append(("order tail", 1))
+    inturn(vtr, X("lf", s_[:, 3]), C("fsb", 3, 128, 4))
+    for k, (e, a, b) in enumerate(YOUT):
+        store(e, T.y[:, 16 * a:16 * b], C("yo", 16 * a, 16 * b), "y%d" % k, sum(4096 * (n - m) for _, m, n in YOUT[k + 1:]) + 65536)
     ts(C("flb", 0), C("dq", 128), 1.0 / 256, mul, cc(25), add)
     store("Y", T.fl[:], X("flb", s_[0:128:16, 0:1]), "fl")
     ts(X("mgb", s_[:, :, 0:2]), X("ab7"), 7.0, add)
     ts(X("mgb", s_[:, :, 2]), X("ks", s_[:, :, 99]), 1.0 / 256, mul)
     store("Y", T.mg[:], X("mgb", s_[0:1]), "mg")
-    cp(X("g0"), X("offy"))
-    tt(X("fsb"), PICK, X("g0"), sub)
+    ts(C("pi", 10), C("pi", 0), 31, band, 1, ALU.logical_shift_right)
+    ts(C("pi", 11), C("pi", 0), 96, band)
+    ts(C("pi", 12), C("pi", 0), 1, band)
+    cp(C("pf", 10, 13), C("pi", 10, 13))
+    for u in range(2):
+        ts(cc(32 + u), C("pf", 12), float(u), ne, 1000.0, mul)
+        ts(cc(36 + u), cc(32 + u), C("pf", 10), add, C("pf", 11), add)
+        ts(X("srt", s_[:, u, 16:144]), J128, cc(36 + u), eq, 16.0, mul)
+    ms(X("srt", s_[:, :, 0:16]), 0.0)
+    lin(dc(14), IDB, -16.0)
     ts(C("flb", 1), C("flb", 0), 32.0, mul, cc(26), add)
     ts(X("emx"), X("nj"), C("flb", 1), add, -1.0, mx)
-    for k in range(2): ts(C("lf", 128 * k, 128 * k + 128), X("fsb"), 7.5 / 16, add, cc(32 + k), mul)
-    for u in range(8): unturn("pa", "lf", u, 0, 16, 16 * u)
+    mm(C("pa", 0, 128), dc(14), C("half", 0, 128), True, False)
+    for u in range(2):
+        for k in range(2): mm(C("pa", 64 * u, 64 * u + 64), X("srt", s_[:, u, 16 - 16 * k:144 - 16 * k]), X("lf", s_[:, :, 16 * k:16 * k + 16]), False, u + k == 2)
     tt(X("fso"), C("pa", 0, 128), X("emx"), mn)
     store("Y", T.fs[:], X("fso"), "fs")
     emit(g, T, ops, [("sent", R * neng)])

import math
import numpy as np
from concourse.bass import DstId, RemoteDMATransfer
from concourse.mybir import AluOpType as ALU, AxisListType as AX, ActivationFunctionType as AF

N, L, M, S0, R = 4, 2048, 4096, 12, 4
H = 12
W = 128 + 2 * H
END = 15.0
M16, M256, M4096 = 1.5 * 2.0 ** 27, 1.5 * 2.0 ** 31, 1.5 * 2.0 ** 35
PADV = L + 2.0
D0 = -1920.0
BIG = 30000.0
F, B, I, U, HF = "float32", "bfloat16", "int32", "uint16", "float16"
GCUT = [("S", 64, 90), ("V", 38, 64), ("S", 90, 114), ("V", 14, 38), ("S", 114, 128), ("V", 0, 14)]
YOUT = [("Y", 0, 12), ("Y", 48, 72), ("Y", 12, 24), ("Y", 72, 104), ("Y", 24, 48), ("S", 104, 128)]
YCUT = [("V", 0, 12), ("V", 12, 24), ("V", 24, 48), ("S", 48, 72), ("S", 72, 104), ("S", 104, 128)]
DROP = [14, 15, 15]
BANKS = ("pa", "pb", "pc", "pd", "pe", "pg", "ph", "p3")
SCRATCH = {"lei": ("sbuf", [8, 4], I), "lef": ("sbuf", [8, 4], F), "blkt": ("sbuf", [8, 128], F)}
for _dt, _shape, _names in [
        (I, [256], "sti"), (B, [256], "stb fi hd"), (B, [1024], "win"), (I, [128], "posi zh zl"), (I, [W], "zi zu"),
        (B, [M + 16], "vew"), (B, [L + 16], "y0"), (B, [L], "yo"), (B, [L + 32], "xs"), (U, [128], "offlo offp offy"),
        (U, [8], "offs"), (I, [16], "pi"), (B, [160], "idw e0 e1 wb"), (B, [272], "lw"), (B, [4, 32], "lf"), (B, [2, 144], "srt"),
        (B, [128], "grow da db d16 sa tri ntri one none cm fsb lhb nid"), (B, [8, 16], "prow"), (B, [3, 128], "lha tr3"),
        (B, [3, 8, 16], "lhr"), (F, [128], "idf g0 g1 nj j16 emx fso"), (F, [160], "jf"),
        (F, [16], "pf so bt bf"), (F, [10, 16], "sr"), (F, [8], "kk th acc"), (F, [40], "cc"), (F, [36], "tr"), (F, [R, 100], "ks"),
        (F, [100], "mk"),
        (F, [2], "wcol"), (B, [16], "i16"), (B, [W], "ns nx wc"), (HF, [128], "xc"), (B, [S0], "eb"), (B, [6, W], "cd"),
        (B, [2, 18, 64], "ob"), (B, [2, W], "hw"), (B, [180], "c8r bias"), (F, [180], "rst so0"), (HF, [S0], "x0"),
        (HF, [48], "x1 x2 x3"), (HF, [N, S0], "l0"), (HF, [N, 48], "l1 l2 l3"), (F, [48], "low rm tm"), (F, [64], "base"), (F, [R, 3], "mgb"),
        (F, [96], "ml"), (F, [5, 128], "sel"), (B, [6, 128], "lh"), (B, [3, 32], "ckey"), (B, [16, 128], "dc"),
        (F, [R, 2], "ab7"), (F, [R], "flb"), (B, [136], "al"), (F, [132], "dq zw zo gp dk"), (HF, [16, 128], "rp"), (HF, [144], "bm"),
        (B, [4, 132], "cnt"), (B, [132], "qb q1 zero half"), (F, [136], "mm"), (B, [8, 132], "sg")]:
    for _n in _names.split(): SCRATCH[_n] = ("sbuf", [128] + _shape, _dt)
for _b in BANKS: SCRATCH[_b] = ("psum", [128, 512], F)
DMAS = ["pos", "st", "le", "ve", "mg", "fl", "fs"] + ["y%d" % k for k in range(len(YOUT))]
SEMAPHORES = ["V", "S", "P", "G", "sent"] + ["d" + d for d in DMAS] + ["a%d_%d" % (t, r) for t in range(R) for r in range(N)]
CYC, PECYC, SLOW, WAKE, TRIP, LOCAL, RATE = 0.83e-3, 0.42e-3, 1.2, 0.2, 1.0, 1.0, 300e3


PLAN, SWEEPS = [], 1


def arrange(ops):
    seen, waits, before = {}, [], []
    for n, (e, fn, rd, wr, sem, cost, lat) in enumerate(ops):
        w, o = set(), set()
        for acc, write in [(a, False) for a in rd] + [(a, True) for a in wr]:
            for m, mask, wrote in seen.get(acc[0], []):
                other = ops[m][0] != e
                if (acc[0] in BANKS and e == "P" and not other) or acc[0][:5] == "order": o.add(m)
                elif (acc[0] in BANKS and other) or (mask & acc[1] and (write or wrote)): (o if ops[m][4] == "-" and not other else w).add(m)
        for acc, write in [(a, False) for a in rd] + [(a, True) for a in wr]: seen.setdefault(acc[0], []).append((n, acc[1], write))
        waits.append(w)
        before.append(o)
    gap = lambda m, n: ops[m][6] + WAKE if m in waits[n] else 0.0
    nxt = [[] for _ in ops]
    for n in range(len(ops)):
        for m in waits[n] | before[n]: nxt[m].append(n)
    chain = [0.0] * len(ops)
    for m in reversed(range(len(ops))): chain[m] = ops[m][5] + max([gap(m, n) + chain[n] for n in nxt[m]] + [ops[m][6]])
    prv = [waits[n] | before[n] for n in range(len(ops))]

    def sweep(ahead, behind, lag, at, rank):
        miss = [len(a) for a in ahead]
        ready, free, order, end = dict((n, at[n]) for n in range(len(ops)) if not miss[n]), {}, [], [0.0] * len(ops)
        while ready:
            t, e = min((max(r, free.get(ops[n][0], 0.0)), ops[n][0]) for n, r in ready.items())
            mine = [n for n in ready if ops[n][0] == e]
            n = max((n for n in mine if ready[n] <= t), key=lambda n: (rank[n], -n))
            soon = [m for m in mine if rank[m] > rank[n] and ready[m] < t + ops[n][5] - 0.03]
            if soon: n = min(soon, key=lambda m: (ready[m], -rank[m]))
            free[e] = end[n] = max(ready.pop(n), t) + ops[n][5]
            order.append(n)
            for k in behind[n]:
                at[k] = max(at[k], end[n] + lag(n, k))
                miss[k] -= 1
                if not miss[k]: ready[k] = at[k]
        return order, end
    best = None
    for _ in range(SWEEPS):
        order, end = sweep(prv, nxt, gap, [0.0] * len(ops), chain)
        span = max(end[n] + ops[n][6] for n in order)
        if best is None or span < best[0]: best = (span, order)
        chain = sweep(nxt, prv, lambda n, k: gap(k, n), [o[6] for o in ops], end)[1]
    return best[1], waits


def emit(g, T, ops, tail):
    q = {"V": g.vector, "S": g.scalar, "P": g.tensor, "G": g, "Y": g.sync}
    if not PLAN: PLAN.extend(arrange(ops))
    order, deps = PLAN
    place = dict((n, k) for k, n in enumerate(order))
    done, upto, after, waits = dict.fromkeys(q, 0), dict.fromkeys(q, 0), {}, {}
    for n in order:
        e, sem = ops[n][0], ops[n][4]
        waits[n] = []
        for m in sorted(deps[n], key=place.get, reverse=True):
            if m in after and not done[e] >> m & 1:
                waits[n].append(m)
                done[e] |= after[m]
        if sem == "-": continue
        if not sem: upto[e] |= 1 << n
        after[n] = done[e] | (1 << n if sem else upto[e])
    needed = set(m for w in waits.values() for m in w)
    count, token, top = {}, {}, {}
    for n in order:
        e, fn, sem = ops[n][0], ops[n][1], ops[n][4]
        for m in waits[n]:
            q[e].wait_ge(T.sem[token[m][0]], token[m][1])
            top[token[m][0]] = max(top.get(token[m][0], 0), token[m][1])
        ins = fn(q[e])
        if sem == "-": continue
        if sem:
            ins.then_inc(T.sem[sem], 16)
            token[n] = (sem, 16)
            count[sem] = 16
        elif n in needed:
            count[e] = count.get(e, 0) + 1
            ins.then_inc(T.sem[e], 1)
            token[n] = (e, count[e])
    for name, v in list(count.items()) + tail:
        if top.get(name, 0) < v: g.wait_ge(T.sem[name], v)


def rank_program(g, core, T, topo):
    rank = T.rank_of(core)
    if rank is None:
        return
    ops = []
    s_ = np.s_

    def X(name, ix=s_[:]):
        where, shape, dt = SCRATCH[name]
        cols = np.arange(int(np.prod(shape[1:]))).reshape([1] + shape[1:])[(slice(None),) + (ix[1:] if isinstance(ix, tuple) else ())].reshape(-1)
        bits = np.zeros(int(np.prod(shape[1:])), np.uint8)
        bits[cols] = 1
        mask = int.from_bytes(np.packbits(bits, bitorder="little").tobytes(), "little")
        return (T[name][ix], [(name, mask)], len(cols), 4 if dt in (F, I) else 2, False)

    def C(name, a, b=None, st=1):
        return X(name, s_[:, a:(a + 1 if b is None else b):st])

    def pick(win, off):
        return (win[0].indirect(off[0]), win[1] + off[1], 16 * off[2], win[3], True)

    def nm(*xs):
        return [a for x in xs if isinstance(x, tuple) for a in x[1]]

    def ap(x):
        return x[0] if isinstance(x, tuple) else x

    def op(e, fn, rd, wr, cost, sem=None, lat=0.0):
        ops.append((e, fn, rd, wr, sem, cost if sem else SLOW * cost, lat))

    def vec(fn, o, ins, more=(), two=False):
        rate = 0.5 if all(x[3] == 2 for x in [o] + ins) else 1.0
        if two: rate = 1.0 if any(x[1][0][0] in BANKS for x in ins) else 2.0
        op("V", fn, nm(*ins) + nm(*more), nm(o), 0.05 + 1.56 * o[2] * CYC if ins and ins[0][4] else max(64, rate * (ins or [o])[0][2]) * CYC)

    def ts(o, i, s1, o0, s2=None, o1=None):
        if o1 is None: vec(lambda q: q.tensor_scalar(o[0], i[0], ap(s1), None, o0), o, [i], [s1])
        else: vec(lambda q: q.tensor_scalar(o[0], i[0], ap(s1), ap(s2), o0, o1), o, [i], [s1, s2])

    def tt(o, a, b, o0):
        vec(lambda q: q.tensor_tensor(o[0], a[0], b[0], o0), o, [a, b], two=True)

    def cp(o, i):
        vec(lambda q: q.tensor_copy(o[0], i[0]), o, [i])

    def ms(o, v):
        vec(lambda q: q.memset(o[0], v), o, [])

    def scan(o, a, b, init, o0, o1):
        vec(lambda q: q.tensor_tensor_scan(o[0], a[0], b[0], init, o0, o1), o, [a, b])

    def vtr(o, i):
        vec(lambda q: q.transpose(o[0], i[0]), o, [i])

    def act(o, i, func=AF.Copy, bias=0.0, scale=1.0, acc=None, more=0.0):
        kw = {} if acc is None else {"accum_out": acc[0]}
        op("S", lambda q: q.activation(o[0], i[0], func, bias=ap(bias), scale=ap(scale), **kw), nm(i, bias, scale), nm(o, acc),
           more + (0.065 + 1.56 * o[2] * CYC if i[4] else max(64, i[2]) * CYC))

    def mm(o, l, r, start, stop):
        op("P", lambda q: q.matmul(o[0], l[0], r[0], start, stop), nm(l, r), nm(o), max(min(64, l[2]), r[2]) * PECYC * (l[3] // 2) ** 2)

    def iota(o, pat, base=0, step=0):
        kw = {} if o[1][0][0] == "pi" else {"allow_small_or_imprecise_dtypes": True}
        op("G", lambda q: q.iota(o[0], pat, base, step, **kw), [], nm(o), 0.13 + 2 * o[2] * CYC)

    def load(e, o, i, sem):
        op(e, lambda q: q.dma_start(o[0], i), [], nm(o) + [("queue" + e, 1)], 0.05, "d" + sem, LOCAL + 128 * o[2] * o[3] / RATE)

    def store(e, o, i, sem, behind=0):
        op(e, lambda q: q.dma_start(o, i[0]), nm(i), [], 0.05, "d" + sem, LOCAL + (128 * i[2] * i[3] + behind) / RATE)

    peers = [(rank + k) % N for k in range(1, N)]
    emask = topo.mask(core, T.cores[peers[0]])
    for r in peers: emask &= topo.mask(core, T.cores[r])
    neng = bin(emask).count("1")

    def send(t):
        tr = RemoteDMATransfer(dst_ids=[DstId(rid=topo.addr(T.cores[r])[0], pnc=topo.addr(T.cores[r])[1]) for r in peers],
                               dma_engine_mask=emask, remote_sem=T.sem["a%d_%d" % (t, rank)], srcs=[T["x%d" % t][:]],
                               dsts=[T["l%d" % t][:, rank, :] for r in peers])
        op("G", lambda q: q.remote_dma_fused([tr], local_sem=T.sem.sent), nm(X("x%d" % t)), [("trip%d" % t, 1)], 0.3, "-", TRIP if t else 1.6 * TRIP)

    def arrived(t, r):
        op("P", lambda q: q.wait_ge(T.sem["a%d_%d" % (t, r)], neng), [("trip%d" % t, 1)], nm(X("l%d" % t, s_[:, r])), 0.0, "-")

    add, sub, mul, mx, mn = ALU.add, ALU.subtract, ALU.mult, ALU.max, ALU.min
    eq, ge, gt, lt, ne = ALU.is_equal, ALU.is_ge, ALU.is_gt, ALU.is_lt, ALU.not_equal
    band, shr = ALU.bitwise_and, ALU.arith_shift_right
    cc = lambda k: C("cc", k)
    PP, P16, PI, P3, P12, PK, PO, PG, PSL, PC8 = [C("pf", k) for k in range(10)]
    J128, J16 = C("jf", 0, 128), C("jf", 0, 16)
    IDB, PROW, J7 = C("idw", 16, 144), X("prow"), X("prow", s_[:, 0, :])
    cd = lambda k, a=0, b=W: X("cd", s_[:, k, a:b])
    own = lambda k: cd(k, H, H + 128)

    op("S", lambda q: q.dma_start(T.sti[:], T.st[:]), [], nm(X("sti")), 0.05, "dst", LOCAL + 0.6)
    op("Y", lambda q: q.dma_start(T.posi[:], T.pos[:]), [], nm(X("posi")) + [("pos", 1)], 0.05, "dpos", LOCAL + 0.7)
    op("Y", lambda q: q.dma_start(T.lei[:, 0:1], T.le[:]), [], nm(X("lei")), 0.05, "dle", LOCAL + 1.0)
    op("Y", lambda q: q.dma_start(T.vew[:, 0:M], T.ve[:]), [("pos", 1)], nm(C("vew", 0, M)), 0.05, "dve", LOCAL + 6.0)

    iota(C("pi", 0, 2), [[16, 2]], 0, 1)
    iota(X("jf"), [[1, 160]])
    iota(X("grow"), [[1, 8], [0, 16]])
    iota(C("c8r", 0, 96), [[0, 12], [1, 8]])
    iota(C("c8r", 96, 180), [[0, 12], [1, 7]])
    iota(PROW, [[0, 8], [1, 16]], -7)
    iota(X("j16"), [[16, 128]])
    iota(X("qb"), [[16, 132]])
    iota(X("nj"), [[-32, 128]])
    for o, v in [(X("cm"), -2048), (X("lhr"), 0), (X("low"), -10 ** 7), (C("base", 48, 64), -10 ** 7),
                 (C("tm", 16, 48), -10 ** 7), (X("lh", s_[:, 1]), -256),
                 (X("ob", s_[:, 0, 12:14, :]), 0), (X("ob", s_[:, 1, 12:14, :]), 0)]:
        iota(o, [[0, o[2]]], v)
    ms(X("zero"), 0.0)
    act(X("lh", s_[:, 0]), C("zero", 0, 128), AF.Exp, 8 * math.log(2), 1.0, more=1.3)
    ops[-1][2].append(("order exp", 1))
    for o, v in [(C("xs", 0, 16), END), (C("xs", L + 16, L + 32), END), (C("lw", 7, 272, 257), 0.0), (C("nx", W - 1), END), (cd(2, 0, 1), 136.0), (X("ml"), 0.0),
                 (C("ml", 28, 96, 33), -1.0), (C("vew", M, M + 16), 0.0), (C("y0", L, L + 16), 0.0),
                 (C("dq", 0), D0), (C("al", 128), 1.0), (C("mm", 129, 136), PADV), (C("zw", 0), -1e9)] + [(X("lhr", s_[:, t, :, S0 + t]), 256.0) for t in range(R - 1)]:
        ms(o, v)
    for k, (s, o, v) in enumerate([(0, band, 15), (0, band, 3), (0, band, 12), (1, band, 240), (0, band, 16), (0, shr, 4), (0, shr, 3), (0, band, 7)]):
        ts(C("pi", 2 + k), C("pi", s), v, o)
    cp(C("pf", 0, 7), C("pi", 0, 7))
    cp(C("pf", 7, 10), C("pi", 7, 10))
    act(C("wcol", 0), P12, AF.Exp, 0.0, 1.25 * math.log(2))
    ops[-1][2].append(("order exp", 1))
    ts(X("idw"), X("jf"), P16, eq)
    ts(C("wcol", 1), P3, 1000.0, mul, PK, add)
    ts(X("e0"), X("jf"), C("wcol", 1), eq)
    ops[-1][2].append(("order st", 1))
    act(X("wb"), X("e0"), AF.Copy, 0.0, C("wcol", 0))
    ts(X("i16"), J16, PI, eq)
    ts(C("cc", 2, 4), C("jf", 0, 32, 16), PO, eq)
    ts(cc(6), PI, 128.0, mul, float(-H), add)
    ts(X("blkt"), X("grow", s_[0:8]), X("pf", s_[0:8, 0:1]), eq)
    ts(X("bias"), X("c8r"), PC8, ne, -BIG, mul)
    ts(X("rst"), X("c8r"), 0.0, ne)
    ts(X("x0", s_[96:128]), X("jf", s_[96:128, 0:S0]), 0.0, mul)
    lin = lambda o, i, scale, bias=0.0: act(o, i, AF.Identity, bias, scale)
    lin(cc(8), PI, -16.0, 119.0)
    lin(X("bt"), J16, -1.0, cc(8))
    for k in (0, 32): lin(C("base", k, k + 16), X("i16"), -1e8)
    TAB = C("base", 16, 32)
    tt(TAB, X("bt"), C("base", 32, 48), add)
    lin(X("idf"), IDB, 1.0)
    ts(C("cc", 28, 32), C("jf", 12, 16), PSL, eq)
    m12, m13, m14, m15 = [cc(28 + k) for k in range(4)]
    lin(cc(4), PSL, 1.0, -7.0)
    lin(cc(10), m14, -2.0, cc(4))
    lin(cc(5), m14, 100.0, cc(4))
    lin(cc(11), m15, -2.0, cc(5))
    lin(cc(12), m15, -1.0, cc(5))
    ts(cc(13), PSL, 12.0, lt, 100.0, mul)
    lin(cc(35), m15, 100.0, cc(5))
    for t in range(R - 2): ts(X("lha", s_[:, t]), PROW, cc(10 + t), eq, 256.0, mul)
    sr, sel, lh = [lambda k, n=n: X(n, s_[:, k]) for n in ("sr", "sel", "lh")]
    ts(C("ml", 0, 16), J7, cc(35), eq, -1.0, mul)
    lin(sr(3), J7, 16.0)
    lin(X("db"), IDB, -2048.0)
    for k, v in enumerate([5.0, 6.0, 7.0, 16.0]): lin(X("dc", s_[:, k]), IDB, v)
    C119, SL = X("dc", s_[:, 4]), X("dc", s_[:, 5])
    iota(C119, [[0, 128]], -119)
    lin(cc(38), m15, 1000.0)
    lin(sr(9), J7, 1.0, cc(38))
    for k in range(2):
        lin(lh(2 + k), lh(0), cc(30 + k))
    lin(cc(9), PI, 1.0, -7.0)
    lin(sel(0), C("zero", 0, 128), 1.0, cc(9))
    iota(X("ckey", s_[:, :, 0:16]), [[-16, 3], [-1, 16]], 119 - 16 * S0)
    iota(X("ckey", s_[:, :, 16:32]), [[-1, 3], [-16, 16]], 119 - S0)
    for t in range(R - 1): ms(X("ckey", s_[:, t, S0 + t:S0 + t + 1]), -1e8)
    ts(lh(5), J128, PP, gt)
    ts(X("one"), X("grow"), PG, eq, 256.0, mul)
    lin(X("none"), X("one"), -1.0)
    ts(X("fsb"), PROW, PI, sub, -7.0, gt)
    tt(X("tri"), X("fsb"), X("one"), mul)
    lin(X("ntri"), X("tri"), -1.0)
    lin(cc(22), PI, -16.0, 104.0)
    lin(X("half"), X("zero"), 1.0, 8.5 / 16)
    lin(cc(7), PI, 16.0, -1.0)
    ts(X("bm"), C("jf", 0, 144), PK, eq, 1.0 / 16, mul)
    dc = lambda k: X("dc", s_[:, k])
    ts(cc(33 + 1), PI, 0.0, eq, 1.0 / 256, mul)
    for k, m, v in [(6, IDB, 8192.0), (7, IDB, -8192.0), (8, X("one"), cc(34)), (9, IDB, -1.0 / 256), (13, IDB, 1.0 / 256)]: lin(dc(k), m, v)
    iota(dc(11), [[0, 128]], -10240)
    tt(dc(10), X("tri"), X("one"), sub)
    lin(dc(15), dc(10), -1.0)
    lin(cc(39), PI, -256.0, 2048.0)
    lin(dc(12), C("zero", 0, 128), 1.0, cc(39))
    lin(X("fsb"), IDB, cc(7))
    tt(X("d16"), X("fsb"), X("tri"), add)
    lin(X("nid"), IDB, -1.0)
    for k in range(2): lin(X("e%d" % k), X("idw"), cc(2 + k))
    lin(cc(20), PI, -4096.0, -16 * D0)
    lin(cc(21), PI, -4096.0, -16 * D0 - 65536)
    lin(cc(24), PI, 4096.0, 256.0 * 15 + 128 + D0)
    lin(cc(26), cc(6), -32.0, -32.0 * H - 1)
    lin(X("th"), C("jf", 0, 8), 65536.0, cc(24))

    cp(X("stb"), X("sti"))
    ops[-1][2].append(("order st", 1))
    for u, bank in enumerate(["pa", "pb", "pc", "ph"]):
        mm(C(bank, 0, 256), C("idw", 16 + u, 144 + u), X("stb"), True, True)
        (cp if u % 2 else act)(C("win", 256 * u, 256 * u + 256), C(bank, 0, 256))
    ts(X("zl"), X("posi"), 1023, band)
    ts(X("zh"), X("posi"), 3072, band)
    cp(X("offlo"), X("zl"))
    for k in range(2):
        ts(C("lw", 8 + 128 * k, 136 + 128 * k), X("zh"), cc(2 + k), mul)
        ops[-1][2].append(("order", 1))
    cp(X("lef", s_[:, 0:1]), X("lei", s_[:, 0:1]))
    ops[-1][2].append(("order", 1))

    def unturn(bank, src, u, a, b, lo):
        for h in range(4):
            p = slice(32 * h, 32 * h + 32)
            mm(X(bank, s_[p, lo:lo + b - a]), X(src, s_[p, u:u + 249:8]), X("i16", s_[p, a:b]), True, True)
    for u in range(8): unturn("pg", "lw", 8 + u, 0, 16, H + 16 * u)
    unturn("pg", "lw", 7, 16 - H, 16, 0)
    unturn("pg", "lw", 16, 0, H, H + 128)
    act(X("wc"), C("pg", 0, W), AF.Exp, 0.0, -5 * math.log(2) / 1024)
    mm(C("pe", 0), X("blkt"), X("lef", s_[:, 0:1]), True, True)
    ts(cc(23), C("pe", 0), cc(6), sub)
    ts(C("pc", 0, W), C("jf", 0, W), cc(23), ge, END, mul)
    ts(C("pc", 256, 384), C("pc", H, H + 128), 8.0, mul, -6.0, add)
    got, left = set([-1, 128]), list(range(16))
    for e, a, b in GCUT:
        (cp if e == "V" else act)(C("xs", 16 + 16 * a, 16 + 16 * b), pick(X("win"), C("offlo", a, b)))
        if e == "V": ops[-1][2].append(("order", 1))
        got.update(range(a, b))
        for i in [i for i in left if got >= set(range(8 * i - 1, 8 * i + 9))]:
            left.remove(i)
            mm(C("ph", 0, W), C("wb", 16 - i, 144 - i), C("xs", 16 + 128 * i - H, 16 + 128 * i + 128 + H), len(left) == 15, not left)
    tt(X("zi"), C("ph", 0, W), X("wc"), mul)
    ts(X("zu"), X("zi"), 31, band)
    tt(own(5), C("zu", H, H + 128), C("pc", 256, 384), add)
    tt(cd(0), X("zu"), C("pc", 0, W), mx)
    lin(cc(27), PI, 127.0, float(-H))
    lin(cc(1), PI, 128.0, -D0 / 256 - L - H)
    lin(cc(0), cc(23), 1.0, cc(27))
    lin(cc(25), cc(23), 1.0, cc(1))
    ts(X("g0"), X("j16"), cc(0), ge, float(M), mul)
    tt(X("g1"), X("g0"), X("posi"), mx)
    cp(X("offp"), X("g1"))

    mm(X("pd", s_[0:96, 0:180]), X("idw", s_[0:96, 16:112]), X("bias", s_[0:96]), True, False)
    pl = lambda h, k: X("ob", s_[:, h, 0:S0, k:64:8])
    for h in range(2):
        two = X("cd", s_[:, 0:6:5, H + 64 * h:H + 64 * h + 64])
        for p in range(6 - 2 * h): ts(X("ob", s_[:, h, p:12:6, :]), two, float(p), eq)
        for p in range(6 - 2 * h, 6): act(C("hd", 128 * p - 512, 128 * p - 384), two, AF.Abs, float(-p))
        for p in range(6 - 2 * h, 6): act(X("ob", s_[:, h, p:12:6, :]), C("hd", 128 * p - 512, 128 * p - 384), AF.Relu, 1.0, -1.0)
        mm(X("pd", s_[0:96, 96:180]), pl(h, 7), pl(h, 8), False, False)
        if h == 1:
            ts(X("eb"), C("jf", 0, S0), cd(0, H + 128, H + 129), eq)
            mm(X("pd", s_[0:96, 7:96:8]), pl(0, 7), X("ob", s_[:, 1, 0:S0, 0]), False, False)
            mm(X("pd", s_[0:96, 7:96:8]), pl(1, 7), X("eb"), False, False)
        for k in range(7): mm(X("pd", s_[0:96, 0:96]), pl(h, k), pl(h, k + 1), False, h == 1 and k == 6)
    scan(X("so0", s_[0:96]), X("rst", s_[0:96]), X("pd", s_[0:96, 0:180]), 0.0, mul, mx)
    tt(X("x0", s_[0:96]), X("so0", s_[0:96, 7:96:8]), X("so0", s_[0:96, 102:180:7]), add)
    send(0)

    def codes(last):
        ts(X("ns"), cd(0), -1.0, mul, -200.0, add)
        back = lambda n, *k: X(n, (slice(None),) + k + (slice(W - 1, 0, -1),))
        if last:
            lin(cd(5), cd(0), 16.0, -119.0)
            scan(X("cd", s_[:, 1, W - 2::-1]), back("ns"), back("cd", 0), END, mn, mx)
            return scan(cd(2, 1), C("ns", 0, W - 1), cd(5, 0, W - 1), 16 * END - 119, mn, mx)
        act(C("pb", 0, W), cd(0), AF.Identity, -119.0, 16.0)
        scan(X("nx", s_[:, W - 2::-1]), back("ns"), back("cd", 0), END, mn, mx)
        scan(C("pc", 1, W), C("ns", 0, W - 1), C("pb", 0, W - 1), 16 * END - 119, mn, mx)
        tt(cd(1), C("pb", 0, W), X("nx"), add)
        tt(cd(2, 1), C("pc", 1, W), cd(0, 1), add)
        scan(X("cd", s_[:, 4, W - 2::-1]), back("ns"), back("cd", 1), 136.0, mn, mx)
        scan(cd(3, 1), C("ns", 0, W - 1), cd(2, 0, W - 1), 136.0, mn, mx)

    iota(C("mk", 0, 96), [[0, 96]])
    iota(C("tr", 32, 36), [[0, 4]])
    for k, v in enumerate([M16, -M16, M256, -M256]): ms(C("mk", 96 + k), v)

    def table(t, src, fin):
        if t == 0: return mm(C("pe", 0, S0), X("lha", s_[0:96, 0]), src(0, S0, 96), False, fin)
        mm(C("pe", 0, 16), X("lhr", s_[:, t - 1]), src(0, 16, 128), False, False)
        mm(C("pe", 0, 16), X("lha", s_[:, t - 1]), src(32, 48, 128), False, False)
        mm(C("pe", 0, 16), X("lhb"), src(32, 48, 128), False, fin)

    def changed(t, bank, src, fin):
        mm(C(bank, 0, 32), lh(0), src(0, 32, 128), False, False)
        mm(C(bank, 32, 64), lh(1), src(0, 32, 128), False, False)
        mm(C(bank, 0, 16), lh(DROP[t - 1] - 12), src(32, 48, 128), False, False)
        mm(C(bank, 32, 48), lh(4), src(32, 48, 128), False, fin)

    def winner(t):
        parts = [lambda a, b, p: X("x%d" % t, s_[0:p, a:b])] + [lambda a, b, p, r=r: X("l%d" % t, s_[0:p, r, a:b]) for r in reversed(peers)]
        bank = "pg" if t < R - 1 else "pd"
        if t:
            mm(C(bank, 0, 32), IDB, X("ckey", s_[:, t - 1]), True, False)
            mm(C(bank, 96, 100), IDB, C("cm", 0, 4), False, False)
            mm(C(bank, 32, 64), IDB, C("zero", 0, 32), False, False)
            mm(C(bank, 16, 64), X("sel", s_[0:16, 2]), X("base", s_[0:16, 0:48]), False, False)
            mm(C(bank, 48, 64), X("sel", s_[0:16, 1]), X("tr", s_[0:16, 0:16]), False, False)
            scan(X("rm"), X("tm"), X("low"), -1e9, mx, mx)
            vtr(C(bank, 64, 96), C("rm", 16, 48))
        if t < R - 1: mm(C("pe", 0, 16 if t else 48), X("idf"), C("base", 16, 32 if t else 64), True, False)
        for k in range(N):
            if k: arrived(t, peers[-k])
            if t: changed(t, bank, parts[k], k == N - 1)
            if t < R - 1: table(t, parts[k], k == N - 1)
        if t == 0:
            scan(X("rm"), C("pe", 0, 48), X("low"), -1e9, mx, mx)
            vtr(C("tr", 0, 32), C("rm", 16, 48))
        lo = 0 if t else 64
        scan(X("ks", s_[:, t, lo:100]), C(bank, 0, 100) if t else X("tr"), C("mk", lo, 100), -1e9, mx, add)
        K, K16, K256 = [X("ks", s_[:, t, k:k + 1]) for k in (95, 97, 99)]
        a7, b7 = X("ab7", s_[:, t, 0:1]), X("ab7", s_[:, t, 1:2])
        ts(a7, K256, K16, sub, 1.0 / 16, mul)
        ts(b7, K16, K, sub)
        return K, K16, K256, a7, b7

    def turn(bank, a, b, first, last):
        for k in range(a, b): vtr(X("tr3", s_[:, k]), own(k))
        for w in range(4):
            for u in range(2):
                for k in range(2):
                    lo = 16 - 16 * (k - u)
                    mm(C(bank, 2 * w + u, 128 * (b - a), 8), C("e%d" % u, lo, lo + 128),
                       X("tr3", s_[:, a:b, 32 * w + 16 * k:32 * w + 16 * k + 16]), first and w + u + k == 0, last and w + u + k == 5)

    codes(False)
    wv = cc(13)
    for t in range(R - 1):
        c, d, x = S0 + t, DROP[t], "x%d" % (t + 1)
        mm(C("pd", 0, 16), IDB, C("bias", 0, 16), True, False)
        K, K16, K256, a7, b7 = winner(t)
        for h in range(2):
            ts(X("ob", s_[:, h, d:d + 3, :]), X("cd", s_[:, 2:5, H + 64 * h:H + 64 * h + 64]), K, add, K256, eq)
            for k in range(8):
                mm(X("pd", s_[0:8 * d + 8, 0:16]), X("ob", s_[:, h, 0:d + 1, k:64:8]), X("ob", s_[:, h, d + 1:d + 3, k:64:8]), False, h == 1 and k == 7)
        ts(C("ml", 32 * t + 16, 32 * t + 16 + c), X("sr", s_[:, 3, 0:c]), K16, add, K256, eq)
        scan(X("so"), C("rst", 0, 16), C("pd", 0, 16), 0.0, mul, mx)
        ts(C(x, 0, 16), C("ml", 32 * t, 32 * t + 16), C("so", 7), mul, -1.0, mul)
        ts(C(x, 16, 48), C("ml", 32 * t, 32 * t + 32), C("so", 15), mul, -1.0, mul)
        ops[-1][2].append(("order send", 1))
        send(t + 1)
        ts(X("hw"), X("cd", s_[:, 1:3]), K, add, K256, eq)
        mm(C("pa", 0, W), X("db"), X("hw", s_[:, 1]), True, False)
        lin(X("da"), X("nid"), a7)
        mm(C("pa", 0, W), X("dc", s_[:, t]), X("hw", s_[:, 0]), False, False)
        mm(C("pa", 0, W), X("da"), X("hw", s_[:, 0]), False, True)
        tt(cd(0), C("pa", 0, W), cd(0), add)
        ops[-1][2].append(("order send", 1))
        ts(X("bf"), C("pe", 0, 16), K, ne)
        tt(TAB, C("pe", 0, 16), X("bf"), mul)
        lin(cc(14 + t), b7, m15 if t else m14, wv)
        if t < R - 2:
            ts(X("lhr", s_[:, t, :, 0:c]), X("prow", s_[:, :, 0:c]), b7, eq, -256.0, mul)
            ts(X("lhb"), PROW, cc(14 + t), eq, -256.0, mul)
        ts(C("kk", 3), cc(10 + t), b7, eq)
        ts(C("kk", 4), cc(14 + t), b7, eq, C("kk", 3), sub)
        lin(lh(4), lh(1), C("kk", 4))
        for k, v in ((2, b7), (1, a7)):
            act(sel(2 + k), sel(0), AF.Abs, v, -1.0)
            act(sel(k), sel(2 + k), AF.Relu, 1.0, -1.0)
        vtr(C("tr", 0, 32), C("base", 16, 48))
        ts(sr(7), C("ml", 32 * t + 16, 32 * t + 32), X("sel", s_[:, 2, 0:1]), mx, 1.0, lt)
        tt(C("tm", 0, 16), TAB, sr(7), mul)
        codes(t == R - 2)
        if t == R - 2: break
        if t == 1:
            act(C("pa", 0, 128), own(0), AF.Identity, -200.0, -1.0)
            for k in (3, 4): tt(own(k), own(k), C("pa", 0, 128), mx)
        act(X("ob", s_[:, :, 12 + t, :]), X("hw", s_[:, 0, H:H + 128]))
        lin(cc(18 + t), a7, (m12, m13)[t], cc(14) if t == 0 else wv)
        wv = cc(18 + t)
        ts(sr(8), sr(9), wv, eq)
        tt(C("ml", 32 * t + 32, 32 * t + 48), sr(8), C("ml", 0, 16), add)
        for k in (2 * t, 2 * t + 1):
            o = C("y0", 512 * k, 512 * k + 512)
            i = pick(X("vew"), C("offp", 32 * k, 32 * k + 32))
            act(o, (i[0], i[1] + nm(C("pb", 0, 1)), i[2], i[3], True))

    turn("pb", 0, 1, True, True)
    act(X("sa"), C("pb", 0, 128), AF.Relu, 1.0)
    act(SL, C("pb", 0, 128))
    mm(C("ph", 0, 128), IDB, C119, True, False)
    mm(C("ph", 128, 256), IDB, C("zero", 0, 128), False, False)
    turn("ph", 1, 3, False, False)
    mm(C("ph", 0, 128), X("dc", s_[:, 3]), SL, False, False)
    mm(C("ph", 128, 256), IDB, SL, False, True)
    act(C("pa", 0, 128), C("pb", 0, 128), AF.Identity, END, -1.0)
    ts(C("al", 0, 128), X("sa"), 1.0, mn)
    mm(C("pb", 0, 129), X("one"), C("al", 0, 129), True, False)
    mm(C("pc", 0, 129), X("tri"), C("al", 0, 129), True, False)
    mm(C("pc", 1, 129), dc(15), C("al", 0, 128), False, False)
    mm(C("pe", 0, 128), C("al", 0, 128), X("one"), True, False)
    ROT, LAST = C("pg", 0, 128), C("p3", 256, 384)
    mm(C("pg", 0, 129), IDB, C("qb", 0, 129), True, False)
    mm(C("pg", 0, 129), IDB, C("half", 0, 129), False, False)
    mm(ROT, IDB, dc(12), False, False)
    mm(LAST, X("one"), C("al", 0, 128), True, False)

    K, K16, K256, a7, b7 = winner(R - 1)
    for h in (1, 0): ts(C("fi", 128 * h, 128 * h + 128), C("ph", 128 * h, 128 * h + 128), K, add, K256, eq)
    DR = C("fi", 128, 256)
    CODE = C("pd", 0, 128)
    mm(C("pe", 0, 128), DR, X("none"), False, True)
    mm(C("pb", 0, 128), X("none"), DR, False, True)
    mm(C("pc", 0, 128), X("ntri"), DR, False, False)
    mm(C("pc", 1, 129), dc(10), DR, False, True)
    mm(LAST, X("none"), DR, False, False)
    act(X("da"), C("pe", 0, 128))
    scan(C("gp", 0, 129), C("pc", 0, 129), C("zero", 0, 129), D0, add, add)
    tt(C("hd", 0, 128), C("pa", 0, 128), C("fi", 0, 128), mul)
    AL = C("al", 0, 128)
    for n, (l, r) in enumerate([(IDB, dc(11)), (IDB, X("sa")), (X("d16"), AL), (dc(6), AL), (X("ntri"), DR), (dc(7), DR),
                                (IDB, C("hd", 0, 128)), (X("da"), lh(5))]):
        mm(CODE, l, r, n == 0, n == 7)
    scan(C("dq", 1, 130), C("pb", 0, 129), C("zero", 0, 129), D0, add, add)
    for c in range(8):
        act(X("sg", s_[:, c, 0:129]), C("dq", 1, 130), AF.Sign, C("th", c), -1.0, acc=C("acc", c), more=0.02)
    ts(X("offs"), X("acc"), 129.0, add, 0.5, mul)
    ts(C("dk", 0, 129), C("gp", 0, 129), M4096, add, M4096, sub)
    tt(C("q1", 0, 129), C("gp", 0, 129), C("dk", 0, 129), sub)
    ops[-1][2].append(("order rows", 1))
    tt(X("xc"), CODE, C("dk", 0, 128), sub)
    ops[-1][2].append(("order rows", 1))
    mm(LAST, dc(8), C("q1", 0, 128), False, False)
    mm(C("p3", 0, 129), dc(8), C("q1", 0, 129), False, True)
    cnt = lambda k, n=128: X("cnt", s_[:, k, 0:n])
    for o, i, bias, v in [(cnt(0), LAST, cc(22), 1.0 / 16), (cnt(1), LAST, -136.0, 1.0 / 16), (cnt(2), LAST, cc(21), 16.0),
                          (cnt(3, 129), C("p3", 0, 129), cc(20), 16.0)]:
        act(o, i, AF.Relu, bias, v)
    for k in range(16):
        o = X("rp", s_[:, k])
        ts(o, X("xc"), 256.0 * k - 2048, mx, 256.0 * k - 1792, mn)
        mm(ROT, C("bm", 16 - k, 144 - k), o, False, k == 15)
        if 10 <= k < 14: mm(ROT, [X("nid"), IDB, dc(9), dc(13)][k - 10], cnt(k - 10), False, False)
    tt(C("zo", 0, 129), C("pg", 0, 129), cnt(3, 129), sub)
    tt(C("zw", 1, 129), ROT, cnt(2), mn)
    scan(C("mm", 0, 129), C("zo", 0, 129), C("zw", 0, 129), -1e9, mx, mx)
    PICK = pick(X("mm"), X("offs"))
    ts(X("offy"), PICK, M16 / 16, add, M16 / 16 + 1, sub)
    pieces = [(a, b) for e, a, b in YCUT if e == "V"]

    def inturn(fn, *a):
        for f, b in [(fn, a)] + [(cp, (C("yo", 16 * m, 16 * n), pick(X("y0"), C("offy", m, n)))) for m, n in pieces[:1]]:
            f(*b)
            ops[-1][2].append(("order tail", 1))
        del pieces[:1]
    for e, a, b in YCUT:
        if e == "S": act(C("yo", 16 * a, 16 * b), pick(X("y0"), C("offy", a, b)))
    inturn(cp, X("g0"), X("offy"))
    inturn(tt, X("fsb"), PICK, X("g0"), sub)
    for u in range(3):
        vtr(X("lf", s_[:, u]), C("fsb", u, 128, 4))
        ops[-1][2].append(("order tail", 1))
    inturn(vtr, X("lf", s_[:, 3]), C("fsb", 3, 128, 4))
    for k, (e, a, b) in enumerate(YOUT):
        store(e, T.y[:, 16 * a:16 * b], C("yo", 16 * a, 16 * b), "y%d" % k, sum(4096 * (n - m) for _, m, n in YOUT[k + 1:]) + 65536)
    ts(C("flb", 0), C("dq", 128), 1.0 / 256, mul, cc(25), add)
    store("Y", T.fl[:], X("flb", s_[0:128:16, 0:1]), "fl")
    ts(X("mgb", s_[:, :, 0:2]), X("ab7"), 7.0, add)
    ts(X("mgb", s_[:, :, 2]), X("ks", s_[:, :, 99]), 1.0 / 256, mul)
    store("Y", T.mg[:], X("mgb", s_[0:1]), "mg")
    ts(C("pi", 10), C("pi", 0), 31, band, 1, ALU.logical_shift_right)
    ts(C("pi", 11), C("pi", 0), 96, band)
    ts(C("pi", 12), C("pi", 0), 1, band)
    cp(C("pf", 10, 13), C("pi", 10, 13))
    for u in range(2):
        ts(cc(32 + u), C("pf", 12), float(u), ne, 1000.0, mul)
        ts(cc(36 + u), cc(32 + u), C("pf", 10), add, C("pf", 11), add)
        ts(X("srt", s_[:, u, 16:144]), J128, cc(36 + u), eq, 16.0, mul)
    ms(X("srt", s_[:, :, 0:16]), 0.0)
    lin(dc(14), IDB, -16.0)
    ts(C("flb", 1), C("flb", 0), 32.0, mul, cc(26), add)
    ts(X("emx"), X("nj"), C("flb", 1), add, -1.0, mx)
    mm(C("pa", 0, 128), dc(14), C("half", 0, 128), True, False)
    for u in range(2):
        for k in range(2): mm(C("pa", 64 * u, 64 * u + 64), X("srt", s_[:, u, 16 - 16 * k:144 - 16 * k]), X("lf", s_[:, :, 16 * k:16 * k + 16]), False, u + k == 2)
    tt(X("fso"), C("pa", 0, 128), X("emx"), mn)
    store("Y", T.fs[:], X("fso"), "fs")
    emit(g, T, ops, [("sent", R * neng)])
